import numpy as np, ml_dtypes
CORES = [35,38,43,46]
N = 4
import mx_ref
BF = ml_dtypes.bfloat16
def gcols(t, e):
    v = np.concatenate([t.reshape(8, 16, -1, 4), np.zeros((8, 16, 1, 4), BF)], axis=2)
    return np.ascontiguousarray(np.stack([v[g][:, e[g]] for g in range(8)])).reshape(128, -1)
def tile(rs):
    return np.stack(rs, axis=2).reshape(128, -1).astype(BF)
def cut(t, i, w=512):
    return t[:, w * i:w * i + w]
def pick(q, e):
    c = np.concatenate([q[0].reshape(128, -1, 4), np.zeros((128, 1, 4), np.uint8)], axis=1); s = np.concatenate([q[1], np.ones((16, 1), np.uint8)], axis=1)
    return (np.ascontiguousarray(c[:, e].reshape(128, -1)), np.ascontiguousarray(s[:, e]))
def join(*qs):
    return (np.concatenate([q[0] for q in qs], axis=1), np.concatenate([q[1] for q in qs], axis=1))
def put(q, e, v):
    c, s = q[0].reshape(128, -1, 4).copy(), q[1].copy(); c[:, e] = v[0].reshape(128, -1, 4); s[:, e] = v[1]
    return (c.reshape(128, -1), s)
def pk(c, s):
    return (np.ascontiguousarray(c), mx_ref.live(s))
def emit(q):
    return q[0], q[1]
def packed(v, rng):
    q = [mx_ref.quantize(np.ascontiguousarray(v[r])) for r in range(N)]
    return np.stack([a for a, b in q]), np.stack([mx_ref.plane(b, rng) for a, b in q])
def values_of_codes():
    e, c = np.zeros((128, 128, 4), np.float32), np.zeros((128, 2, 4), np.uint8)
    e[np.arange(128), np.arange(128), 0] = 1
    c[:127, :, 0] = np.arange(256).reshape(2, 128).T[:127]
    return mx_ref.matmul(mx_ref.quantize(e.reshape(128, 512).astype(BF)), (c.reshape(128, 8), np.full((16, 2), 127, np.uint8))).T.reshape(-1).astype(np.float64)
CODE_VALUE, SCALE_VALUE = values_of_codes(), 2.0 ** (np.arange(256) - 127.0)
def decode(q):
    return (CODE_VALUE[q[0]].reshape(16, 8, -1, 4) * SCALE_VALUE[q[1]][:, None, :, None] + 0.0).reshape(128, -1).astype(np.float32)
def f(rng, *shape):
    return mx_ref.flush((rng.standard_normal(shape, dtype=np.float32) * np.exp2(rng.integers(-2, 3, shape[:-1] + (1,)))).astype(BF))
def wide(rng, *shape, cols=0):
    v = rng.standard_normal(shape, dtype=np.float32) * np.exp2(rng.integers(-12, 13, shape)).astype(np.float32)
    if cols: v *= np.repeat(np.exp2(rng.integers(-cols, cols + 1, shape[:-2] + (1, shape[-1] // 4))) * (rng.random(shape[:-2] + (1, shape[-1] // 4)) > 0.0625), 4, axis=-1).astype(np.float32)
    return mx_ref.flush(v.astype(BF))
C, R, S = 160, 3, 40
def order(p):
    return np.argsort(p[::16] + np.float32(0.0), axis=1, kind="stable")
def trim(v):
    v = v.astype(np.float32)
    v[np.abs(v) < np.float32(2.0 ** -16)] = 0
    return v.astype(BF)
def numbers_of(rng):
    return {"x": trim(f(rng, N, 128, 4 * C)), "u": np.array(f(rng, N, 128, 512)), "v": np.array(f(rng, N, 128, 512))}
def weights(rng, w):
    c, p = packed(w, rng)
    return {"wc": c, "ws": p}
def turned(rng, s):
    w = np.zeros((N, 128, 4, 128, 4), np.float32)
    i = np.arange(128)
    for b in range(4): w[:, i, b, i, b] = 64 * s[:, None]
    return weights(rng, w.reshape(N, 128, 2048).astype(BF))
def signs(rng):
    return np.stack([rng.permutation(8) % 2 * 2.0 - 1.0 for r in range(N)])
def planted(rng, key, mark, low):
    d = numbers_of(rng)
    q, h = [int(i) for i in rng.permutation(8)[:2]]
    k = np.where(low, 2.0 ** -30, 1.0).astype(np.float32)
    x = d["x"].astype(np.float32).reshape(N, 8, 16, C, 4)
    g = ((key[..., None] >> np.arange(12)) & 1) * np.exp2(np.arange(12) - 23.0)
    x[:, :, 8:11] = g.reshape(N, 8, C, 3, 4).transpose(0, 1, 3, 2, 4)
    x[:, :, 11:] = rng.integers(4, 8, (N, 8, 5, C, 4)) * rng.choice([-1.0, 1.0], (N, 8, 5, C, 4)) * 2.0 ** -20
    x[:, q, :8] = 0
    x[:, q, 0, :, 0] = mark * 1.125 * k[:, None]
    x[:, q, 1, :, 0] = mark * k[:, None]
    x[:, h, 0] = 0
    x[:, h, 0, :, 0] = 1
    u = d["u"].reshape(N, 128, 128, 4)
    u[:, :, ::16] = 0
    u[:, :, 8] = 0
    s = signs(rng).astype(np.float32)
    for i in range(8):
        u[:, 16 * h, 16 * i, 0] = (k * s[:, i]).astype(BF)
        u[:, 16 * i + 8:16 * i + 11, 16 * i] = k.astype(BF)[:, None, None]
    u[:, 16 * q, 8, 0] = k.astype(BF)
    u[:, 16 * q + 1, 8, 0] = (-k).astype(BF)
    o = rng.permutation(N)
    if o[0] == 0: o = np.roll(o, 1)
    return {"x": x.reshape(N, 128, 4 * C).astype(BF), "u": u.reshape(N, 128, 512), "v": d["v"], **turned(rng, np.where(o == 0, -1.0, np.where(o <= N // 2, -2.0, 1.0)))}
def narrow():
    t = []
    for n in range(1, C // 2 - 1):
        g = np.array([n * (C - n), C - 2 - n, n * (C - n - 1), C - 1], np.float32)
        c = [g.astype(k).astype(np.float32) for k in (np.float16, BF)]
        if all(i[0] + i[1] > i[2] + i[3] for i in c): t.append(n)
    return t
def setup_inputs(rng):
    return {**numbers_of(rng), **weights(rng, f(rng, N, 128, 2048))}
def setup_inputs_ties(rng):
    d = numbers_of(rng)
    e = rng.permutation(N)
    x = d["x"].reshape(N, 8, 16, C, 4)
    for r in range(N):
        k = np.zeros(C, int) if r == e[0] else rng.permutation(C) % 3
        a = x[r][:, :8, :3].copy()
        a[:, :, 2] = 0
        x[r][:, :8] = a[:, :, k]
    x[e[1], :, :8] = 0
    u = d["u"].reshape(N, 8, 16, 128, 4)
    u[:, :, 8:, ::16] = 0
    u[:, :, 8:, 8] = 0
    return {"x": x.reshape(N, 128, 4 * C), "u": u.reshape(N, 128, 512), "v": d["v"], **weights(rng, f(rng, N, 128, 2048))}
def setup_inputs_near(rng):
    key = np.argsort(rng.random((N, 8, C)), axis=2) // 2
    mark = rng.integers(-1, 2, (N, C))
    e = rng.permutation(N)
    mark[e[0]] = -rng.integers(0, 2, C)
    mark[e[1]] = 1
    for i in range(2):
        c = rng.permutation(C)
        for g in range(8):
            k = rng.permutation(c[:16])
            key[e[i], g, np.concatenate([k[:8], rng.permutation(c[16:24]), k[8:], rng.permutation(c[24:])])] = np.arange(C) // 2
        mark[e[i], c[:16]] = 1 - 2 * i
        mark[e[i], c[16:24]] = 2 * i - 1
    return planted(rng, key, mark, rng.permutation(N) < N // 2)
def setup_inputs_cuts(rng):
    o = rng.permutation(N)
    a, e, b, z = [int(i) for i in np.sort(rng.permutation(8)[:4])]
    key = np.argsort(rng.random((N, 8, C)), axis=2)
    key[:, a] = key[:, b]
    if N > 4: key[:, e] = key[:, b]
    key[:, z] = C - 1 - key[:, b]
    few = int(rng.choice(narrow()))
    mark = np.zeros((N, C))
    i = np.arange(C)
    for r in range(N):
        p = np.argsort(key[r, b])
        n = int(rng.integers(C // 2 - C // 12, C // 2 + C // 12 + 1)) if o[r] == 5 else int(rng.integers(C // 4, 3 * C // 4))
        yes = i < n
        if o[r] == 0: yes[:] = True
        elif o[r] == 1: yes = (i // 2 + int(rng.integers(2))) % 2 == 0
        elif o[r] == 2:
            yes = i == C - 1
            key[r, a, p[[C - 2 - few, C - 1]]] = key[r, a, p[[C - 1, C - 2 - few]]]
        elif o[r] == 3:
            yes = (i >= 1) & (i <= few)
            key[r, a, p[[0, few]]] = key[r, a, p[[few, 0]]]
        elif o[r] == 4: yes[:] = False
        elif o[r] % 2: yes = ~yes
        if o[r] == 5: key[r, e, p[[n - 1, n]]] = key[r, e, p[[n, n - 1]]]
        mark[r, p] = np.where(yes, 1, -rng.integers(0, 2, C))
    return planted(rng, key, mark, np.zeros(N, bool))
def setup_inputs_huge(rng):
    d = numbers_of(rng)
    o = rng.permutation(N)
    c = np.stack([rng.permutation(C) % 2 * 2.0 - 1.0 for r in range(N)])
    c[o < N // 2] = 1
    x = 2.0 ** 30 * (0.4 + 0.2 * rng.random((N, 128, C, 4))) * c[:, None, :, None]
    g = signs(rng)
    for r in range(N):
        k = int(np.argmax(g[r] != g[r, 0]))
        g[r, [k, 7]] = g[r, [7, k]]
    s = np.concatenate([g, (o % 2 * 2.0 - 1.0)[:, None]], axis=1)
    a = 2.0 ** 30 * (1 - 0.25 * rng.random((N, 128, 9, 4))) * s[:, None, :, None]
    u = d["u"].reshape(N, 128, 128, 4)
    u[:, :, np.append(16 * np.arange(8), 8)] = a.astype(np.float32).astype(BF)
    return {"x": x.astype(np.float32).reshape(N, 128, 4 * C).astype(BF), "u": u.reshape(N, 128, 512), "v": d["v"], **turned(rng, np.where(np.arange(N) // (N // 2) == int(rng.integers(2)), -1.5, -0.5))}
def setup_inputs_spread(rng):
    d = setup_inputs(rng)
    d["x"] = trim(wide(rng, N, 128, 4 * C, cols=6))
    return d
def check_inputs(d):
    b = []
    for k in ("x", "u", "v"):
        a = np.abs(d[k].astype(np.float32))
        if not (np.isfinite(a).all() and ((a == 0) | (a >= 2.0 ** -30) & (a <= 2.0 ** 30)).all()): b.append("a value of " + k)
    return b
def reference(x, u, v, wc, ws):
    qu = [mx_ref.quantize(u[r]) for r in range(N)]
    lay = [pk(wc[r], ws[r]) for r in range(N)]
    now = [x[r] for r in range(N)]
    node = np.zeros((N, C), np.int64)
    for t in range(R):
        score = [mx_ref.matmul(qu[r], mx_ref.quantize(now[r])) for r in range(N)]
        if t == 0:
            o = np.stack([order(p) for p in score])
            at = np.argsort(o, axis=2)
        yes = np.stack([p[8] for p in score]) + np.float32(0.0) > 0
        new = 2 * node
        for m in range(2 ** t):
            gain, cuts = np.zeros((N, 8), np.int64), np.full((N, 8), C)
            seq = []
            for r in range(N):
                n = np.count_nonzero(node[r] == m)
                seq.append(o[r][node[r][o[r]] == m].reshape(8, n))
                if n < 2: continue
                pos = np.cumsum(yes[r][seq[r]], axis=1)
                e = np.abs(pos[:, :-1] * n - pos[:, -1:] * np.arange(1, n))
                gain[r], cuts[r] = np.max(e, axis=1), 1 + np.argmax(e, axis=1)
            g = np.argmax(np.sum(gain, axis=0))
            for r in range(N): new[r, seq[r][g, cuts[r, g]:]] += 1
        node = new
        lists = np.argsort(node[:, None] * C + at, axis=2)
        place = np.argsort(lists, axis=2)
        sent = [mx_ref.quantize(gcols(now[r], lists[r])) for r in range(N)]
        back = []
        for d in range(N):
            q = join(*[pick(sent[r], np.arange(S * d, S * d + S)) for r in range(N)])
            h = tile([mx_ref.matmul(pick(lay[d], np.arange(128 * b, 128 * b + 128)), q) * np.float32(0.015625) for b in range(4)])
            back.append(decode(mx_ref.quantize(h)).astype(BF))
        for r in range(N):
            came = np.concatenate([cut(back[d], r, 4 * S) for d in range(N)], axis=1)
            now[r] = (now[r].astype(np.float32) + gcols(came, place[r]).astype(np.float32)).astype(BF)
    y, ol = np.zeros((N, 128, C), np.float32), np.zeros((N, 8, C), np.float32)
    oc, osc = np.zeros((N, 128, 4 * C), np.uint8), np.zeros((N, 16, C), np.uint8)
    for r in range(N):
        q = mx_ref.quantize(now[r])
        y[r] = mx_ref.matmul(mx_ref.quantize(v[r]), q)
        ol[r] = lists[r]
        oc[r], osc[r] = emit(q)
    return {"y": y, "ol": ol, "oc": oc, "osc": osc}

@@ -1,0 +1,594 @@
+from concourse.bass import DstId, RemoteDMATransfer
+from concourse.mybir import dt, AluOpType, AxisListType, ActivationFunctionType
+
+C, R, S, N = 160, 3, 40, 4
+XW = 288
+TW = 224
+BIG = 1e29
+F32, BF, I32, U16, MX, U8 = "float32", "bfloat16", "int32", "uint16", "float8_e4m3fn_x4", "uint8"
+
+
+def _sb(n, d):
+    return ("sbuf", [128, n], d)
+
+
+SCRATCH = {
+    "ps": ("psum", [128, 4096], F32),
+    "xt": _sb(640, BF), "ut": _sb(512, BF), "vt": _sb(512, BF),
+    "uq": _sb(128, MX), "us": _sb(128, U8), "vq": _sb(128, MX), "vs": _sb(128, U8),
+    "upq": _sb(256, MX), "ups": _sb(256, U8), "wq": _sb(512, MX), "wsc": _sb(512, U8),
+    "tq": _sb(4 * C, MX), "tsc": _sb(4 * C, U8),
+    "fq": _sb(R * XW, MX), "fs": _sb(R * XW, U8), "hq": _sb(R * XW, MX), "hs": _sb(R * XW, U8),
+    "ft": _sb(640, BF), "ht": _sb(640, BF), "gt": _sb(640, BF), "tt": _sb(640, BF), "tp": _sb(640, BF),
+    "et": _sb(2048, BF), "eq": _sb(512, MX), "es": _sb(512, U8), "ea": _sb(516, F32), "xw": _sb(516, F32),
+    "kt": _sb(1024, BF), "kq": _sb(256, MX), "ks": _sb(256, U8), "ha": _sb(128, BF),
+    "ct": _sb(1920, BF), "cq": _sb(480, MX), "cs": _sb(480, U8), "sg": _sb(480, BF),
+    "ki": _sb(20, I32), "kf": _sb(32, F32), "uoi": _sb(16, I32), "uof": _sb(16, U16), "xf": _sb(224, F32), "xb": _sb(C, BF),
+    "jm": _sb(C, BF), "gi": _sb(128, BF), "pk": _sb(C, BF), "up": _sb(C, BF), "xlo": _sb(C, F32),
+    "one": _sb(C, BF), "cf": _sb(C, F32), "tph": _sb(C, F32), "xh": _sb(C, F32), "mtau": _sb(32, F32), "xi": _sb(64, F32),
+    "oh": _sb(8, F32), "awx": _sb(16, F32), "kc": _sb(4, F32), "wof": _sb(4, U16),
+    "pm": _sb(C, F32), "pw": _sb(C, F32), "rm": _sb(C, BF), "rw": _sb(C, BF), "ato": _sb(10, U16),
+    "agf": _sb(C, F32), "atn": _sb(C, BF), "l0": _sb(C, BF), "l1": _sb(C, BF), "l2": _sb(C, BF),
+    "lab": _sb(C, BF), "pp": _sb(4, F32), "w": _sb(C, F32), "wn": _sb(C, F32), "e": _sb(C, F32), "se": _sb(C, F32), "cmp": _sb(C, F32),
+    "gx": _sb(8 * R, F32), "sm": _sb(8, F32), "za": _sb(128, F32), "zat": _sb(128, F32), "zb": _sb(128, F32), "zbt": _sb(128, F32),
+    "tab": _sb(16, F32), "junk": _sb(80, F32), "ri": _sb(2, I32), "of1": _sb(2, U16),
+    "atp": _sb(208, BF), "atl": _sb(208, BF), "cx": _sb(208, BF), "z": _sb(208, BF), "fl": _sb(208, BF),
+    "b": _sb(208, BF), "rr": _sb(208, BF), "xx": _sb(208, BF), "y1": _sb(208, BF), "yy": _sb(208, BF),
+    "cb": _sb(240, BF), "tb1": _sb(448, BF), "tb2": _sb(416, BF), "tb3": _sb(416, BF),
+    "sel": _sb(16, U16), "lfl": _sb(224, BF), "lro": _sb(16, U16), "ltr": _sb(16, U16), "ib": _sb(208, BF), "iof": _sb(16, U16),
+    "st": _sb(16, F32), "sx": _sb(16, F32), "sc": _sb(8, F32), "a1": _sb(C, F32), "a3": _sb(C, F32), "a4": _sb(32, F32),
+    "mk": _sb(C, F32), "fr0": _sb(C, F32), "fr": _sb(C, F32), "mt": _sb(C, F32), "thr": _sb(C, F32), "zm": _sb(32, F32),
+    "mw": _sb(192, F32), "mof": _sb(16, U16), "nof": _sb(16, U16),
+    "olf": _sb(C, F32), "yo": _sb(C, F32),
+}
+SEMAPHORES = (["sv", "sa", "sp", "sg", "sent"] + ["ar%d" % k for k in range(3 * R)] + ["d%d" % k for k in range(12)])
+
+A = AluOpType
+AF = ActivationFunctionType
+
+
+def v(name, c0, c1, step=1, p0=0, p1=128, ind=None, cast=None):
+    return (name, c0, c1, step, p0, p1, ind, cast)
+
+
+def col(name, c, p0=0, p1=128):
+    return v(name, c, c + 1, 1, p0, p1)
+
+
+def bank(k, n=C):
+    return v("ps", 512 * k, 512 * k + n)
+
+
+def _meet(a, b):
+    if a[0] != b[0]:
+        return False
+    if a[0] == "ps":
+        return a[1] // 512 == b[1] // 512
+    if a[5] <= b[4] or b[5] <= a[4] or a[2] <= b[1] or b[2] <= a[1]:
+        return False
+    return not (a[3] == b[3] and a[3] > 1 and a[1] % a[3] != b[1] % a[3])
+
+
+def plan(d):
+    rot = 2 * S if (S * d) % (2 * S) != (S if 2 * d >= N else 0) else 0
+    return rot, (S * d - rot) % C == 0
+
+
+def deal(topo, cores, r):
+    free = {o: topo.engines(cores[r], cores[o]) for o in range(N) if o != r}
+    out, taken = {}, []
+    for width in sorted(set(len(f) for f in free.values())):
+        same = [o for o in free if len(free[o]) == width]
+        left = [e for e in free[same[0]] if e not in taken]
+        k = 1
+        while 2 * k * len(same) <= len(left):
+            k *= 2
+        for n_, o in enumerate(same):
+            out[o] = left[n_ * k:(n_ + 1) * k]
+            taken += out[o]
+    return out
+
+
+def rank_program(g, core, T, topo):
+    d = T.rank_of(core)
+    if d is None:
+        return
+    ops = []
+
+    def ap(x):
+        if not isinstance(x, tuple):
+            return x
+        a = T[x[0]][x[4]:x[5], x[1]:x[2]] if x[3] == 1 else T[x[0]][x[4]:x[5], x[1]:x[2]:x[3]]
+        if x[7] is not None:
+            a = a.bitcast(x[7])
+        if x[6] is not None:
+            a = a.indirect(ap(x[6]))
+        return a
+
+    def op(eng, fn, outs, ins, **kw):
+        rd = [x for x in ins if isinstance(x, tuple)]
+        rd += [x[6] for x in rd + list(outs) if x[6] is not None]
+        ops.append(dict(eng=eng, fn=fn, wr=list(outs), rd=rd, **kw))
+
+    def ts(o, i, s1, op0, s2=None, op1=None):
+        if op1 is None:
+            op("v", lambda e: e.tensor_scalar(ap(o), ap(i), ap(s1), None, op0), [o], [i, s1])
+        else:
+            op("v", lambda e: e.tensor_scalar(ap(o), ap(i), ap(s1), ap(s2), op0, op1), [o], [i, s1, s2])
+
+    def tt(o, a, b, k):
+        op("v", lambda e: e.tensor_tensor(ap(o), ap(a), ap(b), k), [o], [a, b])
+
+    def cp(o, i):
+        op("v", lambda e: e.tensor_copy(ap(o), ap(i)), [o], [i])
+
+    def ms(o, c):
+        op("v", lambda e: e.memset(ap(o), c), [o], [])
+
+    def red(o, i, k, absolute=False):
+        if absolute:
+            op("v", lambda e: e.tensor_reduce(ap(o), ap(i), AxisListType.X, k, apply_absolute_value=True), [o], [i])
+        else:
+            op("v", lambda e: e.tensor_reduce(ap(o), ap(i), AxisListType.X, k), [o], [i])
+
+    def scan(o, a, b, init, op0, op1):
+        op("v", lambda e: e.tensor_tensor_scan(ap(o), ap(a), ap(b), ap(init), op0, op1), [o], [a, b, init])
+
+    def tr(o, i):
+        op("v", lambda e: e.transpose(ap(o), ap(i)), [o], [i])
+
+    def qz(q, s, c, n, i):
+        op("v", lambda e: e.quantize_mx(ap(v(q, c, c + n)), ap(v(s, c, c + n)), ap(i)), [v(q, c, c + n), v(s, c, c + n)], [i])
+
+    def act(o, i, f=None, bias=None, scale=None, acc=None):
+        kw = {}
+        if bias is not None:
+            kw["bias"] = bias
+        if scale is not None:
+            kw["scale"] = scale
+        if acc is not None:
+            kw["accum_out"] = acc
+        f = f if f is not None else (AF.Copy if bias is None else AF.Identity)
+        op("a", lambda e: e.activation(ap(o), ap(i), f, **{k: ap(x) for k, x in kw.items()}),
+           [o] + ([acc] if acc is not None else []), [i, bias, scale])
+
+    def mm(o, wq, ws, wc, xq, xs, xc, n=C, start=True, stop=True):
+        a = [v(wq, wc, wc + 128), v(ws, wc, wc + 128), v(xq, xc, xc + n), v(xs, xc, xc + n)]
+        op("p", lambda e: e.matmul_mx(ap(o), ap(a[0]), ap(a[1]), ap(a[2]), ap(a[3]), start, stop), [o], a, chain=not start)
+
+    def iota(o, pat, base=0, cm=0):
+        if SCRATCH[o[0]][2] == I32:
+            op("g", lambda e: e.iota(ap(o), pat, base, cm), [o], [])
+        else:
+            op("g", lambda e: e.iota(ap(o), pat, base, cm, allow_small_or_imprecise_dtypes=True), [o], [])
+
+    nd = [0]
+
+    def dma(eng, o, i, outs, ins):
+        op(eng, lambda e: e.dma_start(o, i), outs, ins, dma="d%d" % nd[0])
+        nd[0] += 1
+
+    peers = [r for r in range(N) if r != d]
+    eng_of = deal(topo, T.cores, d)
+    coming = sum(len(deal(topo, T.cores, r)[d]) for r in peers)
+    sent = [0]
+
+    def send(sem, pairs):
+        def fn(e):
+            tr_ = []
+            for r in peers:
+                rid, pid, _se = topo.addr(T.cores[r])
+                tr_.append(RemoteDMATransfer(dst_ids=[DstId(rid=rid, pnc=pid)], dma_engine_mask=sum(1 << k for k in eng_of[r]),
+                                             remote_sem=T.sem[sem], src=ap(pairs[r][0]), dst=ap(pairs[r][1])))
+            return e.remote_dma_fused(tr_, local_sem=T.sem.sent)
+        op("g", fn, [], [pairs[r][0] for r in peers], remote=True)
+        sent[0] += sum(len(eng_of[r]) for r in peers)
+
+    def arrive(sem, calls, outs):
+        ops.append(dict(eng=None, wr=outs, rd=[], arr=(sem, calls * coming)))
+
+    def bytes_(x):
+        return x[:7] + (dt.uint8,)
+
+    def words(x, ind=None):
+        return x[:6] + (ind, dt.uint32)
+
+    rot, first = plan(d)
+
+    def lay(r):
+        return (128, 8, 0, 120) if plan(r)[1] else (0, 120, 128, 8)
+
+    def slot(r, o):
+        k = [x for x in range(N) if x != r].index(o)
+        return S * k if plan(r)[1] else S + S * k
+
+    def place(r, o):
+        return (S * o - plan(r)[0]) % C
+
+    dma("s", T.ut[:], T.u[:], [v("ut", 0, 512)], [])
+    dma("a", T.xt[:], T.x[:], [v("xt", 0, 640)], [])
+    dma("s", T.wq[:].bitcast(dt.uint8), T.wc[:], [v("wq", 0, 512)], [v("xt", 0, 640)])
+    dma("s", T.wsc[:], T.ws[:], [v("wsc", 0, 512)], [])
+    dma("s", T.vt[:], T.v[:], [v("vt", 0, 512)], [])
+    iota(col("ki", 0), [[0, 1]], 0, 1)
+    iota(v("uoi", 0, 8), [[16, 8]])
+    iota(v("jm", 0, C), [[0, 10], [1, 16]])
+    iota(v("gi", 0, 128), [[1, 8], [0, 16]])
+    iota(v("xf", 0, 224), [[1, 224]])
+    iota(v("xw", 0, 516), [[1, 516]])
+    iota(v("xi", 0, 64), [[0, 4], [16, 16]], 15)
+    iota(v("awx", 0, 16), [[16, 16]], -48)
+    iota(v("kc", 0, 4), [[16, 4]], C + 16)
+    P_, R_, G_, M_, M1_, U_, X_, KD_ = range(8)
+    NG, TIE, NB4, KTA, KTB, KDA, KDB, HI, MTS, R12, RTR, RRO, XA, XB_ = range(8, 22)
+    NB = 24
+    kf = lambda k: col("kf", k)
+    p_ = col("ki", 0)
+    ms(v("uoi", 8, 16), 8)
+    ms(v("ct", 1280 + 3, 1920, 4), 0.0)
+    ts(col("ki", R_), p_, 15, A.bitwise_and)
+    ts(col("ki", G_), p_, 4, A.arith_shift_right)
+    ts(col("ki", M_), p_, 3, A.bitwise_and)
+    ts(col("ki", M1_), p_, 1, A.bitwise_and)
+    ts(col("ki", U_), p_, 4, A.arith_shift_right, 1, A.bitwise_and)
+    ts(col("ki", X_), p_, 3, A.arith_shift_right, 1, A.bitwise_and)
+    ts(col("ki", KD_), p_, 2, A.arith_shift_right, 1, A.bitwise_and)
+    cp(v("uof", 0, 16), v("uoi", 0, 16))
+    cp(v("kf", 0, 8), v("ki", 0, 8))
+    ms(v("cb", 0, 240), 0.0)
+    ts(v("pk", 0, C), v("jm", 0, C), kf(R_), A.not_equal, 2 * BIG, A.mult)
+    ts(v("up", 0, C), v("jm", 0, C), 0.0, A.is_equal, 2 * BIG, A.mult)
+    ts(kf(R12), kf(R_), 12.0, A.min, kf(U_), A.subtract)
+    ts(kf(RTR), kf(R_), 10.0, A.is_ge, -10.0, A.mult)
+    ts(kf(RRO), kf(R_), float(C - rot) / 16, A.is_ge, -10.0, A.mult)
+    ts(v("pk", 0, C), v("pk", 0, C), -BIG, A.add)
+    for t in range(4):
+        ts(v("kt", t, 512, 4), v("gi", 0, 128), kf(G_), A.is_equal)
+    act(kf(NG), kf(G_), scale=-1.0)
+    act(kf(MTS), kf(X_), bias=-256.0, scale=256.0)
+    act(v("ha", 0, 128), v("jm", 0, 128), AF.Abs, bias=kf(NG))
+    act(v("one", 0, C), v("jm", 0, C), bias=1.0, scale=0.0)
+    for t in range(4):
+        act(v("kt", 512 + t, 1024, 4), v("ha", 0, 128), AF.Relu, bias=1.0, scale=-1.0)
+    act(v("mtau", 0, 32), v("kt", 512, 640, 4), scale=kf(MTS))
+    act(kf(HI), kf(X_), bias=-256.0, scale=256.0)
+    ts(col("ki", 8), kf(R12), 1.0, A.add)
+    ts(col("ki", 9), kf(RTR), kf(R12), A.add, 1.0, A.add)
+    ts(col("ki", 10), kf(RRO), kf(R12), A.add, 1.0 + rot // 16, A.add)
+    qz("kq", "ks", 0, 128, v("kt", 0, 512))
+    ts(v("ki", 12, 15), v("ki", 8, 11), 1, A.bitwise_and)
+    ts(v("ki", 16, 19), v("ki", 8, 11), 1, A.arith_shift_right)
+    ts(v("ki", 12, 15), v("ki", 12, 15), float(TW // 16), A.mult, kf(U_), A.add)
+    ts(v("ki", 16, 19), v("ki", 16, 19), 2.0, A.mult)
+    tt(v("kf", NB, NB + 3), v("ki", 12, 15), v("ki", 16, 19), A.add)
+    ts(v("wof", 0, 4, 2), v("kf", NB + 1, NB + 3), 16.0, A.mult, 8.0, A.add)
+    wtrue, wrot = col("wof", 0), col("wof", 2)
+
+    qz("uq", "us", 0, 128, v("ut", 0, 512))
+    for k in range(2):
+        o = v("uof", 8 * k, 8 * k + 8)
+        cp(words(v("upq", 128 * k, 128 * k + 128)), words(v("uq", 0, 128), o))
+        act(v("ups", 128 * k, 128 * k + 128), v("us", 0, 128, ind=o))
+        if k == 0:
+            qz("tq", "tsc", 0, C, v("xt", 0, 640))
+            mm(bank(0), "upq", "ups", 0, "tq", "tsc", 0)
+            mm(bank(3), "upq", "ups", 0, "tq", "tsc", 0)
+    mm(bank(4), "upq", "ups", 128, "tq", "tsc", 0)
+    tt(v("pm", 0, C), bank(0), v("pk", 0, C), A.max)
+    act(v("l0", 0, C), bank(4), AF.Sign)
+    scan(v("pw", 0, C), v("up", 0, C), v("pm", 0, C), 0.0, A.add, A.min)
+    qz("kq", "ks", 128, 128, v("kt", 512, 1024))
+    for c in range(7, 10):
+        act(v("sg", C * (c - 7), C * (c - 6)), bank(3), AF.Sign, bias=col("pw", 16 * c + 15), scale=-1.0)
+    for c in range(7, 10):
+        base, k, so = 1280 + c - 7, 16 * c + 16, C * (c - 7)
+        act(v("ct", base, base + 4 * k - 3, 4), v("sg", so, so + k), AF.Relu, scale=-1.0)
+        if k < C:
+            act(v("ct", base + 4 * k, base + 637, 4), v("sg", so + k, so + C), AF.Sign, bias=1.0, scale=-1.0)
+    act(v("l1", 0, C), v("l0", 0, C), AF.Relu)
+    act(v("xlo", 0, C), v("xf", 0, C), bias=kf(HI), scale=kf(X_))
+    act(v("l2", 0, C), v("l1", 0, C), scale=-1.0, acc=col("pp", 1))
+    act(v("fr", 0, C), v("xf", 0, C), bias=255.0 / 256, scale=-1.0 / 256)
+    act(v("wn", 0, C), v("l1", 0, C), bias=col("pp", 1), scale=float(C))
+    act(kf(NB4), kf(P_), bias=-3.0, scale=-4.0)
+    act(kf(KTA), kf(KD_), bias=-1.0 / 256, scale=1.0 / 256)
+    act(v("ea", 0, 516), v("xw", 0, 516), AF.Abs, bias=kf(NB4))
+    act(kf(KTB), kf(KD_), bias=1.0, scale=-1.0)
+
+    def unit(b):
+        act(v("et", 512 * b, 512 * b + 512), v("ea", 3 - b, 515 - b), AF.Relu, bias=1.0, scale=-1.0)
+
+    unit(0)
+    for c in range(7):
+        base, k = 640 * (c // 4) + c % 4, 16 * c + 16
+        ts(v("ct", base, base + 4 * k - 3, 4), bank(0, k), col("pw", k - 1), A.is_gt)
+        ts(v("ct", base + 4 * k, base + 637, 4), v("ps", k, C), col("pw", k - 1), A.is_ge)
+        if c == 4:
+            qz("cq", "cs", 0, C, v("ct", 0, 640))
+            mm(bank(1), "kq", "ks", 0, "cq", "cs", 0, stop=False)
+        if c == 5:
+            tt(v("ct", 643, 1280, 4), bank(0), v("pw", 0, C), A.is_equal)
+    for s in (2, 1):
+        qz("cq", "cs", C * s, C, v("ct", 640 * s, 640 * s + 640))
+        mm(bank(1), "kq", "ks", 0, "cq", "cs", C * s, start=False, stop=s == 1)
+    for s in range(3):
+        mm(bank(2), "kq", "ks", 128, "cq", "cs", C * s, start=s == 0, stop=s == 2)
+    tt(v("rm", 0, C), bank(1), v("pk", 0, C), A.max)
+    scan(v("rw", 0, C), v("up", 0, C), v("rm", 0, C), 0.0, A.add, A.min)
+    ts(v("ato", 0, 10), v("rw", 15, C, 16), -1.0, A.add)
+    ato = v("ato", 0, 10)
+    cp(v("w", 0, C, ind=ato), v("wn", 0, C))
+
+    def spread(z, mask, val, on_vector):
+        jobs = [(0, 0, 0, 128), (1, 0, 64, 64), (1, 64, 0, 64)]
+        jobs += [(2, 32 * q, 32 * (q ^ 1), 32) for q in range(4)] + [(3, 32 * q, 32 * (q ^ 3), 32) for q in range(4)]
+        for n_, (blk, to, fro, k) in enumerate(jobs):
+            o, m, s = v(z, 32 * blk, 32 * blk + 32, 1, to, to + k), v(mask, 0, 32, 1, fro, fro + k), col(val[0], val[1], fro, fro + k)
+            if n_ < on_vector:
+                ts(o, m, s, A.mult)
+            else:
+                act(o, m, scale=s)
+
+    def turn(tb, src, blocks):
+        tr(v(tb, 0, 32 * blocks), v(src, 0, 32 * blocks))
+        tr(v(tb, TW, TW + 32 * blocks), v(src, 16, 16 + 32 * blocks))
+
+    qf, mv, qh, dm = lay(d)
+    ltr, lro, iof = v("ltr" if rot else "lro", 0, 10), v("lro", 0, 10), v("iof", 0, 10)
+
+    for t in range(R):
+        nn = 2 ** t
+        n = 10 + nn - 1
+        NP = 16 * n
+        if t > 0:
+            mm(bank(4), "upq", "ups", 128, "tq", "tsc", C * t)
+            for b in range(4):
+                act(v("tp", C * b, C * b + C), v("tt", b, 640, 4))
+            tt(v("lab", 0, C), bank(4), v("thr", 0, C), A.is_gt)
+            red(col("pp", 0), v("lab", 0, C), A.add)
+            ts(v("w", 0, C), v("lab", 0, C, ind=ltr), col("sc", 2), A.mult, col("pp", 0), A.subtract)
+        scan(v("e", 0, C), v("w", 0, C), v("mk" if t else "one", 0, C), 0.0, A.add, A.mult)
+        gain = col("gx", 8 * t + 2)
+        red(gain, v("e", 0, C), A.max, True)
+        send("ar%d" % (3 * t), {r: (gain, col("gx", 8 * t + 4 + [x for x in range(N) if x != r].index(d))) for r in peers})
+        act(v("se", 0, C), v("e", 0, C), AF.Abs)
+        if t == 0:
+            tt(v("atn", 0, C), bank(2), v("xlo", 0, C), A.add)
+            for b in range(3):
+                act(v("tp", C * b, C * b + C), v("xt", b, 640, 4))
+        tt(v("cmp", 0, C), v("se", 0, C), v("fr", 0, C), A.add)
+        red(col("sm", 0), v("cmp", 0, C), A.max)
+        if t == 0:
+            ts(col("sm", 1), col("sm", 0), gain, A.subtract)
+            cp(v("atp", 0, C, ind=ato), v("atn", 0, C))
+            spread("za", "mtau", ("sm", 1), 3)
+        else:
+            ts(col("sm", 1), col("sm", 0), gain, A.subtract, col("sc", 5), A.max)
+            spread("za", "mtau", ("sm", 1), 7)
+        tr(v("zat", 0, 128), v("za", 0, 128))
+        for m in range(nn):
+            red(col("tab", m), v("zat", m, 128, 8), A.add)
+        if t == 0:
+            red(col("tab", 8), v("zat", 4, 128, 8), A.add)
+            act(kf(TIE), kf(G_), scale=-0.0625)
+            act(v("zm", 0, 32), v("one", 0, 32))
+            act(v("gx", 3, 8 * R, 8), v("one", 0, R), scale=kf(TIE))
+            ts(v("b", 0, C), v("atp", 0, C), col("tab", 0), A.is_gt)
+            ts(col("tab", 9), col("tab", 8), 271.0, A.add)
+            ts(v("z", 0, C), v("atp", 0, C), col("tab", 0), A.is_le)
+            scan(v("y1", 0, C), v("one", 0, C), v("b", 0, C), col("tab", 9), A.mult, A.add)
+            scan(v("xx", 0, C), v("one", 0, C), v("z", 0, C), 15.0, A.mult, A.add)
+        else:
+            for m in range(nn):
+                act(v("junk", 16 * m, 16 * m + 16), v("zat", 4 + m, 128, 8), acc=col("tab", 8 + m))
+            nof = v("nof", 0, n)
+            act(v("fl", 0, NP), v("tab", 8, 8 + nn, ind=nof), bias=271.0)
+            tt(v("b", 0, NP), v("tab", 0, nn, ind=nof), v("atp", 0, NP), A.is_lt)
+            scan(v("rr", 0, NP), v("z", 0, NP), v("b", 0, NP), 0.0, A.mult, A.add)
+            scan(v("y1", 0, NP), v("b", 0, NP), v("fl", 0, NP), col("fl", 0), A.add, A.max)
+            tt(v("xx", 0, NP), v("cx", 0, NP), v("rr", 0, NP), A.subtract)
+        tt(v("yy", 0, NP), v("y1", 0, NP), v("b", 0, NP), A.mult)
+        if t < R - 1:
+            for m in range(nn):
+                act(v("cb", 16 + NP + 16 * m, 32 + NP + 16 * m), v("one", 0, 16), bias=271.0, scale=col("tab", 8 + m))
+        if t == 0:
+            act(v("lfl", 0, 224), v("xf", 0, 224), scale=0.0)
+            act(v("tb2", 192, TW), v("one", 0, 32))
+            act(v("tp", 3 * C, 4 * C), v("xt", 3, 640, 4))
+            act(v("xb", 0, C), v("xf", 0, C))
+            act(v("ib", 0, 208), v("xf", 0, 208), scale=0.0)
+        tt(v("cb", 16, 16 + NP), v("xx", 0, NP), v("yy", 0, NP), A.max)
+        turn("tb1", "cb", 7)
+        arrive("ar%d" % (3 * t), 1, [v("gx", 8 * t + 4, 8 * t + 7)])
+        if t == 0:
+            red(col("sm", 2), v("gx", 2, 7), A.add)
+            spread("zb", "zm", ("sm", 2), 7)
+        else:
+            act(v("junk", 64, 69), v("gx", 8 * t + 2, 8 * t + 7), acc=col("sm", 2))
+            spread("zb", "zm", ("sm", 2), 3)
+        tr(v("zbt", 0, 128), v("zb", 0, 128))
+        red(col("sm", 3), v("zbt", 0, 128), A.max)
+        ts(col("ri", 0), col("sm", 3), kf(NB), A.add)
+        ts(col("of1", 0), col("ri", 0), col("sm", 3), A.subtract, 16.0, A.mult)
+        cp(v("sel", 0, 16), v("tb1", 0, 448, ind=col("of1", 0)))
+        cp(v("lfl", 0, 224, ind=v("sel", 0, n)), v("atp", 0, NP))
+        turn("tb2", "lfl", 6)
+        cp(v("lro", 0, 16), v("tb2", 0, 416, ind=wrot))
+        for b in range(4):
+            (act if b % 2 else cp)(v("ft", b, 640, 4), v("tp", C * b, C * b + C, ind=lro))
+        x0 = XW * t
+        qz("fq", "fs", x0 + qf, C, v("ft", 0, 640))
+        for nm, f in (("fq", bytes_), ("fs", lambda x: x)):
+            send("ar%d" % (3 * t + 1), {r: (f(v(nm, x0 + qf + place(d, r), x0 + qf + place(d, r) + S)),
+                                            f(v(nm, x0 + lay(r)[1] + slot(r, d), x0 + lay(r)[1] + slot(r, d) + S))) for r in peers})
+        more = t < R - 1
+        n2 = 2 * nn
+        so = 8 * t
+        if t == 0:
+            act(v("xh", 0, C), v("xf", 0, C), bias=0.5)
+            for b in range(1, 4):
+                unit(b)
+            ms(v("tb3", 192, TW), 0.0)
+            ms(v("st", 0, 16), float(C))
+            ms(v("atl", C, 208), -300.0)
+        cp(v("ib", 16, 16 + C, ind=lro), v("xb", 0, C))
+        if rot:
+            cp(v("ltr", 0, 16), v("tb2", 0, 416, ind=wtrue))
+        if t == 0:
+            ts(kf(KDA), kf(KD_), -1.0 / 256, A.mult)
+            ts(kf(KDB), kf(KD_), 255.0 / 256, A.mult)
+            ts(v("oh", 0, 4), v("xf", 0, 4), kf(M1_), A.is_equal)
+            ts(v("oh", 4, 8), v("xf", 0, 4), kf(M_), A.is_equal)
+            ms(v("st", 0, 16, 8), 0.0)
+        turn("tb3", "ib", 6)
+        if not more:
+            cp(v("olf", 0, C), v("lfl", 16, 16 + C))
+            dma("s", T.ol[:], T.olf[8:128:16, :], [], [v("olf", 0, C)])
+            qz("vq", "vs", 0, 128, v("vt", 0, 512))
+        if t == 0:
+            ts(col("st", 1), col("sel", n), -15.0, A.add)
+        if t == 1:
+            ts(v("st", 9, 12, 2), v("sel", n, n + 2), -15.0, A.add)
+            cp(col("st", 10), col("st", 1))
+        cp(v("iof", 0, 16), v("tb3", 0, 416, ind=wtrue))
+        if more:
+            tt(v("sx", 0, 4), v("st", so, so + 4), v("oh", 4 * t, 4 * t + 4), A.mult)
+            tt(v("sx", 4, 8), v("st", so + 1, so + 5), v("oh", 4 * t, 4 * t + 4), A.mult)
+            tt(v("sx", 8, 8 + n2 - 1), v("kc", 0, n2 - 1), v("st", so + 1, so + n2), A.subtract)
+            red(col("sc", 0), v("sx", 0, 4), A.add)
+            red(col("sc", 1), v("sx", 4, 8), A.add)
+            if t == 0:
+                ts(v("awx", 0, 16), v("awx", 0, 16), kf(R_), A.add)
+            ts(col("sc", 3), col("sc", 0), col("sc", 1), A.add, -0.5, A.mult)
+            ts(col("sc", 4), col("sc", 1), col("sc", 0), A.subtract, 0.5, A.mult)
+            tt(col("sc", 2), col("sc", 1), col("sc", 0), A.subtract)
+            ts(col("sc", 5), col("sc", 1), kf(KDA), A.mult, kf(KD_), A.add)
+        lo = x0 + (8 if first else C)
+        arrive("ar%d" % (3 * t + 1), 2, [v("fq", lo, lo + 3 * S), v("fs", lo, lo + 3 * S)])
+        for b in range(4):
+            mm(bank(4 + b), "wq", "wsc", 128 * b, "fq", "fs", x0 + mv)
+        for b in range(4):
+            if b % 2:
+                ts(v("ht", b, 640, 4), bank(4 + b), 0.015625, A.mult)
+            else:
+                act(v("ht", b, 640, 4), bank(4 + b), scale=0.015625)
+        qz("hq", "hs", x0 + qh, C, v("ht", 0, 640))
+        for nm, f in (("hq", bytes_), ("hs", lambda x: x)):
+            send("ar%d" % (3 * t + 2), {r: (f(v(nm, x0 + qh + slot(d, r), x0 + qh + slot(d, r) + S)),
+                                            f(v(nm, x0 + lay(r)[3] + place(r, d), x0 + lay(r)[3] + place(r, d) + S))) for r in peers})
+        if t == 0:
+            if rot:
+                act(v("tph", 0, C - rot), v("xh", rot, C))
+                act(v("tph", C - rot, C), v("xh", 0, rot))
+            act(v("agf", 0, C), bank(1), bias=kf(KTB), scale=kf(KTA))
+            act(v("cf", 0, C), v("xf", 0, C), bias=kf(KDB), scale=kf(KDA))
+        if more:
+            n_2 = 10 + n2 - 1
+            act(v("a3", 0, C), v("tph" if rot else "xh", 0, C), AF.Abs, bias=col("sc", 3))
+            act(v("a1", 0, C), v("xh", 0, C), AF.Abs, bias=col("sc", 3))
+            act(v("atl", 0, C), v("atn", 0, C, ind=ltr))
+            if t == 0:
+                qz("eq", "es", 0, 512, v("et", 0, 2048))
+                ms(v("xi", 11, 32, 16), 0.0)
+                ms(v("xi", 12, 32, 16), float(C + 15))
+                ts(kf(XA), kf(M1_), -16.0, A.mult, -7.5, A.add)
+                ts(kf(XB_), kf(M_), -16.0, A.mult, -7.5, A.add)
+            blk = lambda k, a=0: v("mw", 16 * k + a, 16 * k + a + n_2)
+            for m in range(1, n2):
+                ts(v("mw", 16 * (m - 1), 16 * m), v("awx", 0, 16), col("st", so + m), A.is_ge, col("sx", 7 + m), A.mult)
+                ts(blk(2 + m), v("awx", 4 - m, 4 - m + n_2), col("st", so + m), A.is_ge)
+            if t == 0:
+                ts(v("xi", 0, 32), v("xi", 0, 32), kf(XA), A.add)
+                ts(v("xi", 32, 64), v("xi", 32, 64), kf(XB_), A.add)
+            for m in range(1, n2):
+                tt(blk(5 + m), blk(m - 1, 4 - m), blk(m - 1, 3 - m), A.subtract)
+            if n2 > 2:
+                tt(blk(9), blk(3), blk(4), A.add)
+                tt(blk(10), blk(6), blk(7), A.add)
+                tt(blk(11), blk(8), v("awx", 3, 3 + n_2), A.add)
+                tt(blk(3), blk(9), blk(5), A.add)
+                tt(blk(11), blk(11), blk(10), A.add)
+            else:
+                tt(blk(11), blk(6), v("awx", 3, 3 + n_2), A.add)
+            ts(blk(9), blk(3), -16.0, A.mult)
+            ts(v("mt", 0, C), v("a3", 0, C), col("sc", 4), A.is_ge, BIG, A.mult)
+            act(v("thr", 0, C), v("mt", 0, C, ind=iof))
+            tt(blk(10), blk(11), blk(9), A.add)
+            cp(v("nof", 0, n_2), blk(3))
+            cp(v("mof", 0, n_2), blk(10))
+            mof, NQ = v("mof", 0, n_2), 16 * n_2
+            ts(v("mk", 0, C), v("a1", 0, C), col("sc", 4), A.is_lt)
+            tt(v("fr0", 0, C), v("agf", 0, C, ind=ltr), v("cf", 0, C), A.add)
+            act(v("cx", 0, NQ), v("xf", 0, 208, ind=mof), bias=16.0)
+            act(v("a4", 0, 32), v("xi", 32 * t, 32 * t + 32), AF.Abs, bias=col("sc", 3))
+            act(v("atp", 0, NQ), v("atl", 0, 208, ind=mof))
+            tt(v("fr", 0, C), v("fr0", 0, C), v("mk", 0, C), A.mult)
+            ts(v("z", 0, NQ), v("cx", 0, NQ), C + 15.5, A.is_lt)
+            ts(v("zm", 0, 32), v("a4", 0, 32), -8.0, A.add, col("sc", 4), A.is_lt)
+        lo = x0 + (C if first else 8)
+        arrive("ar%d" % (3 * t + 2), 2, [v("hq", lo, lo + 3 * S), v("hs", lo, lo + 3 * S)])
+        for b in range(4):
+            mm(bank(b), "eq", "es", 128 * b, "hq", "hs", x0 + dm)
+        for b in range(4):
+            tt(v("gt", C * b, C * b + C), v("ft", b, 640, 4), bank(b), A.add)
+        for b in range(2):
+            act(v("tt", b, 640, 4), v("gt", C * b, C * b + C, ind=iof))
+        act(v("tt", 2, 384, 4), v("gt", 2 * C, 3 * C, ind=v("iof", 0, 6)))
+        cp(v("tt", 384 + 2, 640, 4), v("gt", 2 * C, 3 * C, ind=v("iof", 6, 10)))
+        cp(v("tt", 3, 640, 4), v("gt", 3 * C, 4 * C, ind=iof))
+        qz("tq", "tsc", C * (t + 1), C, v("tt", 0, 640))
+
+    o = C * R
+    mm(bank(5), "vq", "vs", 0, "tq", "tsc", o)
+    dma("s", T.oc[:], T.tq[:, o:o + C].bitcast(dt.uint8), [], [v("tq", o, o + C)])
+    for k in range(4):
+        dma("a" if k else "s", T.osc[4 * k:4 * k + 4, :], T.tsc[32 * k:32 * k + 4, o:o + C], [], [v("tsc", o, o + C)])
+    cp(v("yo", 0, C), bank(5))
+    dma("s", T.y[:], T.yo[:], [], [v("yo", 0, C)])
+
+    queue = {"v": g.vector, "a": g.scalar, "p": g.tensor, "s": g.sync, "g": g}
+    counter = {"v": "sv", "a": "sa", "p": "sp", "g": "sg"}
+    known = {q: {} for q in queue}
+    for i, o_ in enumerate(ops):
+        o_["src"] = o_["arr"][0] if "arr" in o_ else o_.get("dma", o_["eng"])
+        if o_["eng"] is None:
+            o_["after"] = {}
+            continue
+        need = {}
+        for j in range(i):
+            e_ = ops[j]
+            if e_.get("remote") or (o_.get("chain") and e_["eng"] == "p"):
+                continue
+            if (any(_meet(a, b_) for a in o_["rd"] + o_["wr"] for b_ in e_["wr"]) or any(_meet(a, b_) for a in o_["wr"] for b_ in e_["rd"])
+                    or (e_["eng"] != o_["eng"] and any(a[0] == "ps" and _meet(a, b_) for a in o_["rd"] for b_ in e_["rd"]))):
+                need[e_["src"]] = j
+        kn = known[o_["eng"]]
+        o_["waits"] = []
+        for src, j in sorted(need.items(), key=lambda x: -x[1]):
+            if kn.get(src, -1) < j:
+                o_["waits"].append(j)
+                ops[j]["told"] = True
+                kn[src] = j
+                for s2, j2 in ops[j]["after"].items():
+                    kn[s2] = max(kn.get(s2, -1), j2)
+        o_["after"] = dict(kn)
+    count = {q: 0 for q in counter}
+    for o_ in ops:
+        if o_["eng"] is None:
+            o_["sig"] = o_["arr"]
+            continue
+        q = queue[o_["eng"]]
+        for j in o_["waits"]:
+            q.wait_ge(T.sem[ops[j]["sig"][0]], ops[j]["sig"][1])
+        ins = o_["fn"](q)
+        if "dma" in o_:
+            ins.then_inc(T.sem[o_["dma"]], 16)
+            o_["sig"] = (o_["dma"], 16)
+        elif o_.get("told"):
+            count[o_["eng"]] += 1
+            ins.then_inc(T.sem[counter[o_["eng"]]], 1)
+            o_["sig"] = (counter[o_["eng"]], count[o_["eng"]])
+    g.wait_ge(T.sem.sent, sent[0])
+    for o_ in ops:
+        if "dma" in o_ and not o_.get("told"):
+            queue[o_["eng"]].wait_ge(T.sem[o_["dma"]], 16)

@@ -3,8 +3,11 @@ from concourse.mybir import dt, AluOpType, AxisListType, ActivationFunctionType
 
 C, R, S, N = 160, 3, 40, 4
 XW = 288
-TW = 224
+TW = 192
+DW = 176
+WHOLE = 1.5 * 2 ** 23
 BIG = 1e29
+FAR = 2.0 ** 80
 F32, BF, I32, U16, MX, U8 = "float32", "bfloat16", "int32", "uint16", "float8_e4m3fn_x4", "uint8"
 
 
@@ -20,25 +23,25 @@ SCRATCH = {
     "tq": _sb(4 * C, MX), "tsc": _sb(4 * C, U8),
     "fq": _sb(R * XW, MX), "fs": _sb(R * XW, U8), "hq": _sb(R * XW, MX), "hs": _sb(R * XW, U8),
     "ft": _sb(640, BF), "ht": _sb(640, BF), "gt": _sb(640, BF), "tt": _sb(640, BF), "tp": _sb(640, BF),
-    "et": _sb(2048, BF), "eq": _sb(512, MX), "es": _sb(512, U8), "ea": _sb(516, F32), "xw": _sb(516, F32),
-    "kt": _sb(1024, BF), "kq": _sb(256, MX), "ks": _sb(256, U8), "ha": _sb(128, BF),
-    "ct": _sb(1920, BF), "cq": _sb(480, MX), "cs": _sb(480, U8), "sg": _sb(480, BF),
-    "ki": _sb(20, I32), "kf": _sb(32, F32), "uoi": _sb(16, I32), "uof": _sb(16, U16), "xf": _sb(224, F32), "xb": _sb(C, BF),
-    "jm": _sb(C, BF), "gi": _sb(128, BF), "pk": _sb(C, BF), "up": _sb(C, BF), "xlo": _sb(C, F32),
-    "one": _sb(C, BF), "cf": _sb(C, F32), "tph": _sb(C, F32), "xh": _sb(C, F32), "mtau": _sb(32, F32), "xi": _sb(64, F32),
-    "oh": _sb(8, F32), "awx": _sb(16, F32), "kc": _sb(4, F32), "wof": _sb(4, U16),
-    "pm": _sb(C, F32), "pw": _sb(C, F32), "rm": _sb(C, BF), "rw": _sb(C, BF), "ato": _sb(10, U16),
-    "agf": _sb(C, F32), "atn": _sb(C, BF), "l0": _sb(C, BF), "l1": _sb(C, BF), "l2": _sb(C, BF),
-    "lab": _sb(C, BF), "pp": _sb(4, F32), "w": _sb(C, F32), "wn": _sb(C, F32), "e": _sb(C, F32), "se": _sb(C, F32), "cmp": _sb(C, F32),
-    "gx": _sb(8 * R, F32), "sm": _sb(8, F32), "za": _sb(128, F32), "zat": _sb(128, F32), "zb": _sb(128, F32), "zbt": _sb(128, F32),
-    "tab": _sb(16, F32), "junk": _sb(80, F32), "ri": _sb(2, I32), "of1": _sb(2, U16),
-    "atp": _sb(208, BF), "atl": _sb(208, BF), "cx": _sb(208, BF), "z": _sb(208, BF), "fl": _sb(208, BF),
-    "b": _sb(208, BF), "rr": _sb(208, BF), "xx": _sb(208, BF), "y1": _sb(208, BF), "yy": _sb(208, BF),
-    "cb": _sb(240, BF), "tb1": _sb(448, BF), "tb2": _sb(416, BF), "tb3": _sb(416, BF),
-    "sel": _sb(16, U16), "lfl": _sb(224, BF), "lro": _sb(16, U16), "ltr": _sb(16, U16), "ib": _sb(208, BF), "iof": _sb(16, U16),
-    "st": _sb(16, F32), "sx": _sb(16, F32), "sc": _sb(8, F32), "a1": _sb(C, F32), "a3": _sb(C, F32), "a4": _sb(32, F32),
-    "mk": _sb(C, F32), "fr0": _sb(C, F32), "fr": _sb(C, F32), "mt": _sb(C, F32), "thr": _sb(C, F32), "zm": _sb(32, F32),
-    "mw": _sb(192, F32), "mof": _sb(16, U16), "nof": _sb(16, U16),
+    "eq": _sb(512, MX), "es": _sb(512, U8), "ea": _sb(516, BF),
+    "kt": _sb(512, BF), "kq": _sb(128, MX), "ks": _sb(128, U8), "ha": _sb(128, BF),
+    "ct": _sb(1920, BF), "cq": _sb(480, MX), "cs": _sb(480, U8), "sg": _sb(5 * C, BF),
+    "ki": _sb(20, I32), "kf": _sb(48, F32), "uoi": _sb(16, I32), "uof": _sb(16, U16), "xf": _sb(C, F32), "xb": _sb(C, BF),
+    "jm": _sb(C, BF), "hj": _sb(128, BF), "pk": _sb(C, BF), "up": _sb(C, BF), "rs": _sb(C, BF),
+    "one": _sb(C, BF), "kc": _sb(2 * C, BF), "xr": _sb(C, BF), "m8": _sb(40, F32), "zi": _sb(64, F32), "zm": _sb(96, F32),
+    "awx": _sb(12, F32), "wof": _sb(6, U16),
+    "pm": _sb(C, F32), "pw": _sb(C, F32), "tie": _sb(C, BF), "so": _sb(10 * C, BF), "ato": _sb(10, U16),
+    "atn": _sb(C, BF), "l0": _sb(C, BF), "l1": _sb(C, BF), "wn": _sb(2 * C, BF), "pl": _sb(2 * C, BF),
+    "lab": _sb(C, BF), "pp": _sb(4, F32), "w": _sb(C, F32), "e": _sb(C, F32), "se": _sb(C + 3, F32), "fin": _sb(C + 3, F32),
+    "dl": _sb(R * DW, F32), "sm": _sb(8, F32), "za": _sb(32, F32), "zat": _sb(32, F32), "zb": _sb(128, F32), "zbt": _sb(144, F32),
+    "tab": _sb(16, F32), "rx": _sb(72, F32), "rin": _sb(72, F32), "of": _sb(8, U16),
+    "ky": _sb(C, BF), "fl": _sb(C, BF), "b": _sb(C, BF), "y1": _sb(C, BF), "nb": _sb(C, BF), "x1": _sb(C, BF), "yb": _sb(C, BF),
+    "lf": _sb(6 * TW + 16, BF),
+    "tb1": _sb(2 * TW, BF), "tb2": _sb(2 * TW, BF), "tb3": _sb(2 * TW, BF), "gm": _sb(80, BF), "hm": _sb(80, BF),
+    "npo": _sb(16, U16), "lro": _sb(16, U16), "ltr": _sb(16, U16), "iof": _sb(16, U16),
+    "cu": _sb(64, F32), "cut": _sb(64, F32), "th": _sb(32, F32), "sc": _sb(24, F32), "ge": _sb(256, BF), "nd": _sb(32, BF), "nof": _sb(10, U16),
+    "a2": _sb(C, BF), "a3": _sb(C, BF), "mk": _sb(C, BF), "thr": _sb(C, F32), "t1": _sb(C, BF), "t2": _sb(C, BF), "at0": _sb(C, BF),
+    "ph": _sb(C + 2, BF),
     "olf": _sb(C, F32), "yo": _sb(C, F32),
 }
 SEMAPHORES = (["sv", "sa", "sp", "sg", "sent"] + ["ar%d" % k for k in range(3 * R)] + ["d%d" % k for k in range(12)])
@@ -127,7 +130,7 @@ def rank_program(g, core, T, topo):
 
     def red(o, i, k, absolute=False):
         if absolute:
-            op("v", lambda e: e.tensor_reduce(ap(o), ap(i), AxisListType.X, k, apply_absolute_value=True), [o], [i])
+            op("v", lambda e: e.tensor_reduce(ap(o), ap(i), AxisListType.X, k, negate=True, apply_absolute_value=True), [o], [i])
         else:
             op("v", lambda e: e.tensor_reduce(ap(o), ap(i), AxisListType.X, k), [o], [i])
 
@@ -205,215 +208,237 @@ def rank_program(g, core, T, topo):
     def place(r, o):
         return (S * o - plan(r)[0]) % C
 
+    def row(k, ind=None):
+        return v("lf", TW * k + 16, TW * k + 16 + C, ind=ind)
+
     dma("s", T.ut[:], T.u[:], [v("ut", 0, 512)], [])
     dma("a", T.xt[:], T.x[:], [v("xt", 0, 640)], [])
     dma("s", T.wq[:].bitcast(dt.uint8), T.wc[:], [v("wq", 0, 512)], [v("xt", 0, 640)])
     dma("s", T.wsc[:], T.ws[:], [v("wsc", 0, 512)], [])
     dma("s", T.vt[:], T.v[:], [v("vt", 0, 512)], [])
-    iota(col("ki", 0), [[0, 1]], 0, 1)
+    iota(col("ki", 9), [[0, 1]], 0, 1)
     iota(v("uoi", 0, 8), [[16, 8]])
     iota(v("jm", 0, C), [[0, 10], [1, 16]])
-    iota(v("gi", 0, 128), [[1, 8], [0, 16]])
-    iota(v("xf", 0, 224), [[1, 224]])
-    iota(v("xw", 0, 516), [[1, 516]])
-    iota(v("xi", 0, 64), [[0, 4], [16, 16]], 15)
-    iota(v("awx", 0, 16), [[16, 16]], -48)
-    iota(v("kc", 0, 4), [[16, 4]], C + 16)
-    P_, R_, G_, M_, M1_, U_, X_, KD_ = range(8)
-    NG, TIE, NB4, KTA, KTB, KDA, KDB, HI, MTS, R12, RTR, RRO, XA, XB_ = range(8, 22)
-    NB = 24
+    iota(v("m8", 0, 8), [[0, 4], [1, 2]])
+    iota(v("m8", 8, 16), [[0, 2], [1, 2], [0, 2]])
+    for q in range(4):
+        for x in range(2):
+            iota(v("hj", 32 * q + x, 32 * q + 32, 2), [[0, 4], [1, 2], [-4 if q & 2 else 4, 2]], 2 * (q ^ x))
+    iota(v("xf", 0, C), [[1, C]])
+    iota(v("zi", 0, 32), [[0, 8], [1, 2], [0, 2]])
+    iota(v("zi", 32, 64), [[0, 4], [1, 4], [0, 2]])
+    iota(v("awx", 0, 12), [[16, 12]])
+    R_, G_, B0, B1, B2, B3, GA, N2, K1 = range(9)
+    (NB3, NGA, SIG, KB, C0, W16, T1S, T1B, TI0, H1, V0, PA1, PA2, CA1, CA2, CB, COL1, COL2, O20, O21, KK, PB, PS0, PS1, PS2, NB2, NN2, Z0, NB0,
+     WB, NG) = range(9, 40)
     kf = lambda k: col("kf", k)
-    p_ = col("ki", 0)
+    p_ = col("ki", 9)
     ms(v("uoi", 8, 16), 8)
     ms(v("ct", 1280 + 3, 1920, 4), 0.0)
+    ms(v("dl", 0, C + 1), 1.0 / 256)
+    ms(col("dl", C + 1), 0.0)
     ts(col("ki", R_), p_, 15, A.bitwise_and)
     ts(col("ki", G_), p_, 4, A.arith_shift_right)
-    ts(col("ki", M_), p_, 3, A.bitwise_and)
-    ts(col("ki", M1_), p_, 1, A.bitwise_and)
-    ts(col("ki", U_), p_, 4, A.arith_shift_right, 1, A.bitwise_and)
-    ts(col("ki", X_), p_, 3, A.arith_shift_right, 1, A.bitwise_and)
-    ts(col("ki", KD_), p_, 2, A.arith_shift_right, 1, A.bitwise_and)
+    for k, (sh, m) in enumerate(((0, 1), (1, 1), (2, 1), (3, 1), (4, 1), (1, 3), (2, 3))):
+        ts(col("ki", B0 + k), p_, sh, A.arith_shift_right, m, A.bitwise_and)
     cp(v("uof", 0, 16), v("uoi", 0, 16))
-    cp(v("kf", 0, 8), v("ki", 0, 8))
-    ms(v("cb", 0, 240), 0.0)
+    cp(v("kf", 0, 9), v("ki", 0, 9))
     ts(v("pk", 0, C), v("jm", 0, C), kf(R_), A.not_equal, 2 * BIG, A.mult)
     ts(v("up", 0, C), v("jm", 0, C), 0.0, A.is_equal, 2 * BIG, A.mult)
-    ts(kf(R12), kf(R_), 12.0, A.min, kf(U_), A.subtract)
-    ts(kf(RTR), kf(R_), 10.0, A.is_ge, -10.0, A.mult)
-    ts(kf(RRO), kf(R_), float(C - rot) / 16, A.is_ge, -10.0, A.mult)
+    ts(v("rs", 0, C), v("jm", 0, C), 0.0, A.not_equal)
     ts(v("pk", 0, C), v("pk", 0, C), -BIG, A.add)
-    for t in range(4):
-        ts(v("kt", t, 512, 4), v("gi", 0, 128), kf(G_), A.is_equal)
-    act(kf(NG), kf(G_), scale=-1.0)
-    act(kf(MTS), kf(X_), bias=-256.0, scale=256.0)
-    act(v("ha", 0, 128), v("jm", 0, 128), AF.Abs, bias=kf(NG))
+    act(kf(NGA), kf(GA), scale=-1.0)
+    act(kf(NB3), kf(B3), bias=1.0, scale=-1.0)
     act(v("one", 0, C), v("jm", 0, C), bias=1.0, scale=0.0)
+    act(kf(NG), kf(G_), scale=-1.0)
+    act(v("kc", 0, C), v("jm", 0, C), bias=kf(B3), scale=0.0)
+    act(kf(W16), kf(B3), bias=float(C), scale=-float(C))
+    act(kf(NN2), kf(B3), bias=-1.0)
+    act(kf(SIG), kf(B3), bias=-1.0, scale=2.0)
+    act(kf(KB), kf(B3), bias=162.0, scale=-323.0)
+    act(kf(TI0), kf(GA), bias=-1.0, scale=0.0625)
+    act(kf(Z0), kf(B3), bias=-8.0, scale=8.0)
+    for k in range(7):
+        act(v("lf", max(0, TW * k - 16), TW * k + 16), v("one", 0, 32 if k else 16), scale=0.0)
+    act(col("dl", C + 3), kf(G_), bias=kf(TI0), scale=0.125)
+    act(v("zm", 0, 32), v("one", 0, 32), scale=kf(Z0))
+    act(v("ha", 0, 128), v("hj", 0, 128), AF.Abs, bias=kf(NG))
+    act(kf(O20), kf(GA), bias=11.5, scale=16.0)
     for t in range(4):
-        act(v("kt", 512 + t, 1024, 4), v("ha", 0, 128), AF.Relu, bias=1.0, scale=-1.0)
-    act(v("mtau", 0, 32), v("kt", 512, 640, 4), scale=kf(MTS))
-    act(kf(HI), kf(X_), bias=-256.0, scale=256.0)
-    ts(col("ki", 8), kf(R12), 1.0, A.add)
-    ts(col("ki", 9), kf(RTR), kf(R12), A.add, 1.0, A.add)
-    ts(col("ki", 10), kf(RRO), kf(R12), A.add, 1.0 + rot // 16, A.add)
-    qz("kq", "ks", 0, 128, v("kt", 0, 512))
-    ts(v("ki", 12, 15), v("ki", 8, 11), 1, A.bitwise_and)
-    ts(v("ki", 16, 19), v("ki", 8, 11), 1, A.arith_shift_right)
-    ts(v("ki", 12, 15), v("ki", 12, 15), float(TW // 16), A.mult, kf(U_), A.add)
-    ts(v("ki", 16, 19), v("ki", 16, 19), 2.0, A.mult)
-    tt(v("kf", NB, NB + 3), v("ki", 12, 15), v("ki", 16, 19), A.add)
-    ts(v("wof", 0, 4, 2), v("kf", NB + 1, NB + 3), 16.0, A.mult, 8.0, A.add)
-    wtrue, wrot = col("wof", 0), col("wof", 2)
+        act(v("kt", t, 512, 4), v("ha", 0, 128), AF.Relu, bias=1.0, scale=-1.0)
+    ts(kf(PA1), kf(B3), -2.0, A.add)
+    ts(v("m8", 16, 24), v("m8", 0, 8), kf(GA), A.is_equal, 256.0, A.mult)
+    ts(v("m8", 24, 32), v("m8", 8, 16), kf(PA1), A.mult, kf(NB3), A.add)
+    ts(kf(KK), kf(R_), 9.0, A.min)
+    ts(kf(PB), kf(R_), 10.0, A.is_ge, kf(B0), A.max)
+    ms(col("se", C), 0.0)
+    ms(v("se", C + 1, C + 3), -BIG)
+    tt(v("m8", 32, 40), v("m8", 16, 24), v("m8", 24, 32), A.mult)
+    tt(kf(PS0), kf(PB), kf(GA), A.is_equal)
 
     qz("uq", "us", 0, 128, v("ut", 0, 512))
-    for k in range(2):
-        o = v("uof", 8 * k, 8 * k + 8)
-        cp(words(v("upq", 128 * k, 128 * k + 128)), words(v("uq", 0, 128), o))
-        act(v("ups", 128 * k, 128 * k + 128), v("us", 0, 128, ind=o))
-        if k == 0:
-            qz("tq", "tsc", 0, C, v("xt", 0, 640))
-            mm(bank(0), "upq", "ups", 0, "tq", "tsc", 0)
-            mm(bank(3), "upq", "ups", 0, "tq", "tsc", 0)
+    ts(kf(PS1), kf(PS0), TW // 16 - 1.0, A.mult, kf(KK), A.add)
+    ts(kf(PS2), kf(R_), 10.0 - rot // 16, A.is_ge, -10.0, A.mult)
+    cp(words(v("upq", 0, 128)), words(v("uq", 0, 128), v("uof", 0, 8)))
+    act(v("ups", 0, 128), v("us", 0, 128, ind=v("uof", 0, 8)))
+    qz("tq", "tsc", 0, C, v("xt", 0, 640))
+    mm(bank(0), "upq", "ups", 0, "tq", "tsc", 0)
+    mm(bank(3), "upq", "ups", 0, "tq", "tsc", 0)
+    cp(words(v("upq", 128, 256)), words(v("uq", 0, 128), v("uof", 8, 16)))
+    act(v("ups", 128, 256), v("us", 0, 128, ind=v("uof", 8, 16)))
     mm(bank(4), "upq", "ups", 128, "tq", "tsc", 0)
+    ts(col("wof", 0), kf(PS1), 16.0, A.mult, 24.0, A.add)
+    ts(kf(PS2), kf(PS2), kf(KK), A.add, float(TW // 16 - 1 + rot // 16), A.add)
     tt(v("pm", 0, C), bank(0), v("pk", 0, C), A.max)
+    qz("kq", "ks", 0, 128, v("kt", 0, 512))
     act(v("l0", 0, C), bank(4), AF.Sign)
     scan(v("pw", 0, C), v("up", 0, C), v("pm", 0, C), 0.0, A.add, A.min)
-    qz("kq", "ks", 128, 128, v("kt", 512, 1024))
-    for c in range(7, 10):
-        act(v("sg", C * (c - 7), C * (c - 6)), bank(3), AF.Sign, bias=col("pw", 16 * c + 15), scale=-1.0)
-    for c in range(7, 10):
-        base, k, so = 1280 + c - 7, 16 * c + 16, C * (c - 7)
-        act(v("ct", base, base + 4 * k - 3, 4), v("sg", so, so + k), AF.Relu, scale=-1.0)
+    ts(kf(PB), kf(PS0), 1.0 - TW // 16, A.mult, kf(PS2), A.add)
+    ts(col("wof", 4), kf(PS1), 16.0, A.mult, 25.0, A.add)
+    NV = 6
+    cmp_ = lambda c, a=0, b=C: v("ct", 640 * (c // 4) + c % 4 + 4 * a, 640 * (c // 4) + c % 4 + 4 * b - 3, 4)
+    count_ = lambda c: scan(v("so", C * c, C * c + C), v("one", 0, C), cmp_(c), col("tie", 16 * c + 15), A.mult, A.add)
+    for c in range(NV, 10):
+        act(v("sg", C * (c - NV), C * (c - NV + 1)), bank(3), AF.Sign, bias=col("pw", 16 * c + 15), scale=-1.0)
+        if c == NV:
+            act(v("l1", 0, C), v("l0", 0, C), AF.Relu, acc=col("pp", 1))
+        if c == NV + 1:
+            act(col("pp", 3), col("pp", 1), bias=kf(B3), scale=kf(NN2))
+        if c == 9:
+            act(v("wn", 0, C), v("l1", 0, C), bias=col("pp", 3), scale=kf(W16))
+    for c in range(NV, 10):
+        k, so = 16 * c + 16, C * (c - NV)
+        act(cmp_(c, 0, k), v("sg", so, so + k), AF.Relu, scale=-1.0)
         if k < C:
-            act(v("ct", base + 4 * k, base + 637, 4), v("sg", so + k, so + C), AF.Sign, bias=1.0, scale=-1.0)
-    act(v("l1", 0, C), v("l0", 0, C), AF.Relu)
-    act(v("xlo", 0, C), v("xf", 0, C), bias=kf(HI), scale=kf(X_))
-    act(v("l2", 0, C), v("l1", 0, C), scale=-1.0, acc=col("pp", 1))
-    act(v("fr", 0, C), v("xf", 0, C), bias=255.0 / 256, scale=-1.0 / 256)
-    act(v("wn", 0, C), v("l1", 0, C), bias=col("pp", 1), scale=float(C))
-    act(kf(NB4), kf(P_), bias=-3.0, scale=-4.0)
-    act(kf(KTA), kf(KD_), bias=-1.0 / 256, scale=1.0 / 256)
-    act(v("ea", 0, 516), v("xw", 0, 516), AF.Abs, bias=kf(NB4))
-    act(kf(KTB), kf(KD_), bias=1.0, scale=-1.0)
-
-    def unit(b):
-        act(v("et", 512 * b, 512 * b + 512), v("ea", 3 - b, 515 - b), AF.Relu, bias=1.0, scale=-1.0)
-
-    unit(0)
-    for c in range(7):
-        base, k = 640 * (c // 4) + c % 4, 16 * c + 16
-        ts(v("ct", base, base + 4 * k - 3, 4), bank(0, k), col("pw", k - 1), A.is_gt)
-        ts(v("ct", base + 4 * k, base + 637, 4), v("ps", k, C), col("pw", k - 1), A.is_ge)
-        if c == 4:
-            qz("cq", "cs", 0, C, v("ct", 0, 640))
-            mm(bank(1), "kq", "ks", 0, "cq", "cs", 0, stop=False)
-        if c == 5:
-            tt(v("ct", 643, 1280, 4), bank(0), v("pw", 0, C), A.is_equal)
-    for s in (2, 1):
-        qz("cq", "cs", C * s, C, v("ct", 640 * s, 640 * s + 640))
-        mm(bank(1), "kq", "ks", 0, "cq", "cs", C * s, start=False, stop=s == 1)
-    for s in range(3):
-        mm(bank(2), "kq", "ks", 128, "cq", "cs", C * s, start=s == 0, stop=s == 2)
-    tt(v("rm", 0, C), bank(1), v("pk", 0, C), A.max)
-    scan(v("rw", 0, C), v("up", 0, C), v("rm", 0, C), 0.0, A.add, A.min)
-    ts(v("ato", 0, 10), v("rw", 15, C, 16), -1.0, A.add)
+            act(cmp_(c, k, C), v("sg", so + k, so + C), AF.Sign, bias=1.0, scale=-1.0)
+    tt(cmp_(10), bank(0), v("pw", 0, C), A.is_equal)
+    for c in range(NV):
+        k = 16 * c + 16
+        ts(cmp_(c, 0, k), bank(0, k), col("pw", k - 1), A.is_gt)
+        ts(cmp_(c, k, C), v("ps", k, C), col("pw", k - 1), A.is_ge)
+        if c == 0:
+            scan(v("tie", 0, C), v("rs", 0, C), cmp_(10), 0.0, A.mult, A.add)
+    for c in range(10):
+        count_(c)
+        if c == NV - 1:
+            scan(v("wn", C, 2 * C), v("kc", 0, C), v("wn", 0, C), -1.0, A.mult, A.add)
+    qz("cq", "cs", 0, C, v("ct", 0, 640))
+    ts(v("ato", 0, 10), v("so", C - 1, 10 * C, C), -1.0, A.mult, float(C), A.add)
     ato = v("ato", 0, 10)
-    cp(v("w", 0, C, ind=ato), v("wn", 0, C))
+    qz("cq", "cs", C, C, v("ct", 640, 1280))
+    cp(row(5, ato), v("wn", C, 2 * C))
+    qz("cq", "cs", 2 * C, C, v("ct", 1280, 1920))
+    for s in range(3):
+        mm(bank(2), "kq", "ks", 0, "cq", "cs", C * s, start=s == 0, stop=s == 2)
+    act(v("kc", C, 2 * C), v("one", 0, C), scale=kf(NB3))
+    for b in range(3):
+        act(v("tp", C * b, C * b + C), v("xt", b, 640, 4))
+    act(v("pl", 0, C), row(5), bias=kf(NB3), scale=kf(B3))
 
-    def spread(z, mask, val, on_vector):
-        jobs = [(0, 0, 0, 128), (1, 0, 64, 64), (1, 64, 0, 64)]
-        jobs += [(2, 32 * q, 32 * (q ^ 1), 32) for q in range(4)] + [(3, 32 * q, 32 * (q ^ 3), 32) for q in range(4)]
-        for n_, (blk, to, fro, k) in enumerate(jobs):
-            o, m, s = v(z, 32 * blk, 32 * blk + 32, 1, to, to + k), v(mask, 0, 32, 1, fro, fro + k), col(val[0], val[1], fro, fro + k)
-            if n_ < on_vector:
-                ts(o, m, s, A.mult)
-            else:
-                act(o, m, scale=s)
+    def spread(put, on_vector):
+        jobs = [(0, 0, 0, 128), (2, 0, 64, 64), (2, 64, 0, 64)]
+        jobs += [(x, 32 * q, 32 * (q ^ x), 32) for x in (1, 3) for q in range(4)]
+        for n_, (x, to, fro, k) in enumerate(jobs):
+            put(n_ < on_vector, x, (to, to + k), (fro, fro + k))
 
-    def turn(tb, src, blocks):
-        tr(v(tb, 0, 32 * blocks), v(src, 0, 32 * blocks))
-        tr(v(tb, TW, TW + 32 * blocks), v(src, 16, 16 + 32 * blocks))
+    def turn(tb, k):
+        tr(v(tb, 0, TW), v("lf", TW * k, TW * k + TW))
+        tr(v(tb, TW, 2 * TW), v("lf", TW * k + 16, TW * k + 16 + TW))
 
     qf, mv, qh, dm = lay(d)
-    ltr, lro, iof = v("ltr" if rot else "lro", 0, 10), v("lro", 0, 10), v("iof", 0, 10)
+    wtrue, wrot, wcol = col("wof", 0), col("wof", 2 if rot else 0), col("wof", 4)
+    ltr, lro, iof, nof = v("ltr" if rot else "lro", 0, 10), v("lro", 0, 10), v("iof", 0, 10), v("nof", 0, 10)
+    SZ, VO, S2, NS, LH, TP, VB, DD, HX = range(4, 13)
+    sc = lambda k: col("sc", k)
 
     for t in range(R):
         nn = 2 ** t
-        n = 10 + nn - 1
-        NP = 16 * n
+        E = 2 * nn if t else 1
+        nk = -(-10 * E // 16)
+        go = 48 * (t - 1)
         if t > 0:
             mm(bank(4), "upq", "ups", 128, "tq", "tsc", C * t)
             for b in range(4):
                 act(v("tp", C * b, C * b + C), v("tt", b, 640, 4))
             tt(v("lab", 0, C), bank(4), v("thr", 0, C), A.is_gt)
             red(col("pp", 0), v("lab", 0, C), A.add)
-            ts(v("w", 0, C), v("lab", 0, C, ind=ltr), col("sc", 2), A.mult, col("pp", 0), A.subtract)
-        scan(v("e", 0, C), v("w", 0, C), v("mk" if t else "one", 0, C), 0.0, A.add, A.mult)
-        gain = col("gx", 8 * t + 2)
+            ts(v("w", 0, C), v("lab", 0, C, ind=ltr), sc(SZ), A.mult, col("pp", 0), A.subtract)
+            scan(v("e", 0, C), v("w", 0, C), v("mk", 0, C), 0.0, A.add, A.mult)
+        else:
+            scan(v("e", 0, C), v("one", 0, C), row(5), 0.0, A.mult, A.add)
+            turn("tb2", 5)
+        do = DW * t
+        gain = col("dl", do + C + 2)
         red(gain, v("e", 0, C), A.max, True)
-        send("ar%d" % (3 * t), {r: (gain, col("gx", 8 * t + 4 + [x for x in range(N) if x != r].index(d))) for r in peers})
+        send("ar%d" % (3 * t), {r: (gain, col("dl", do + C + 4 + [x for x in range(N) if x != r].index(d))) for r in peers})
         act(v("se", 0, C), v("e", 0, C), AF.Abs)
         if t == 0:
-            tt(v("atn", 0, C), bank(2), v("xlo", 0, C), A.add)
-            for b in range(3):
-                act(v("tp", C * b, C * b + C), v("xt", b, 640, 4))
-        tt(v("cmp", 0, C), v("se", 0, C), v("fr", 0, C), A.add)
-        red(col("sm", 0), v("cmp", 0, C), A.max)
+            iota(v("ea", 0, 516), [[0, 516]], 1)
+            op("g", lambda e: e.affine_select(ap(v("ea", 0, 516)), ap(v("ea", 0, 516)), [[1, 516]], A.is_equal, 0.0, -3, -4),
+               [v("ea", 0, 516)], [v("ea", 0, 516)])
+            cp(v("ltr", 0, 16), v("tb2", 0, 2 * TW, ind=wtrue))
+            act(v("atn", 0, C), bank(2), bias=kf(KB), scale=kf(SIG))
+        scan(v("fin", 0, C + 3), v("dl", do, do + C + 3), v("se", 0, C + 3), 0.0 if t else -1.0 / 256, A.add, A.max)
         if t == 0:
-            ts(col("sm", 1), col("sm", 0), gain, A.subtract)
-            cp(v("atp", 0, C, ind=ato), v("atn", 0, C))
-            spread("za", "mtau", ("sm", 1), 3)
-        else:
-            ts(col("sm", 1), col("sm", 0), gain, A.subtract, col("sc", 5), A.max)
-            spread("za", "mtau", ("sm", 1), 7)
-        tr(v("zat", 0, 128), v("za", 0, 128))
-        for m in range(nn):
-            red(col("tab", m), v("zat", m, 128, 8), A.add)
+            scan(v("pl", C, 2 * C), v("kc", C, 2 * C), v("pl", 0, C), -1.0, A.mult, A.add)
+            act(v("ky", 0, C), v("atn", 0, C, ind=v("ltr", 0, 10)))
+
+        def put_cut(vec, x, to, fro, t=t):
+            o, m, s = v("za", x, 32, 4, *to), v("m8", 32, 40, 1, *fro), col("fin", C + 2, *fro)
+            if t == 0:
+                ts(o, m, s, A.mult) if vec else act(o, m, scale=s)
+            elif vec:
+                ts(o, m, s, A.mult, col("sc", S2, *fro), A.add)
+            else:
+                act(o, m, bias=col("sc", S2, *fro), scale=s)
+        spread(put_cut, 6 if t else 9)
+        tr(v("zat", 0, 32), v("za", 0, 32))
         if t == 0:
-            red(col("tab", 8), v("zat", 4, 128, 8), A.add)
-            act(kf(TIE), kf(G_), scale=-0.0625)
-            act(v("zm", 0, 32), v("one", 0, 32))
-            act(v("gx", 3, 8 * R, 8), v("one", 0, R), scale=kf(TIE))
-            ts(v("b", 0, C), v("atp", 0, C), col("tab", 0), A.is_gt)
-            ts(col("tab", 9), col("tab", 8), 271.0, A.add)
-            ts(v("z", 0, C), v("atp", 0, C), col("tab", 0), A.is_le)
-            scan(v("y1", 0, C), v("one", 0, C), v("b", 0, C), col("tab", 9), A.mult, A.add)
-            scan(v("xx", 0, C), v("one", 0, C), v("z", 0, C), 15.0, A.mult, A.add)
-        else:
-            for m in range(nn):
-                act(v("junk", 16 * m, 16 * m + 16), v("zat", 4 + m, 128, 8), acc=col("tab", 8 + m))
-            nof = v("nof", 0, n)
-            act(v("fl", 0, NP), v("tab", 8, 8 + nn, ind=nof), bias=271.0)
-            tt(v("b", 0, NP), v("tab", 0, nn, ind=nof), v("atp", 0, NP), A.is_lt)
-            scan(v("rr", 0, NP), v("z", 0, NP), v("b", 0, NP), 0.0, A.mult, A.add)
-            scan(v("y1", 0, NP), v("b", 0, NP), v("fl", 0, NP), col("fl", 0), A.add, A.max)
-            tt(v("xx", 0, NP), v("cx", 0, NP), v("rr", 0, NP), A.subtract)
-        tt(v("yy", 0, NP), v("y1", 0, NP), v("b", 0, NP), A.mult)
-        if t < R - 1:
-            for m in range(nn):
-                act(v("cb", 16 + NP + 16 * m, 32 + NP + 16 * m), v("one", 0, 16), bias=271.0, scale=col("tab", 8 + m))
-        if t == 0:
-            act(v("lfl", 0, 224), v("xf", 0, 224), scale=0.0)
-            act(v("tb2", 192, TW), v("one", 0, 32))
             act(v("tp", 3 * C, 4 * C), v("xt", 3, 640, 4))
-            act(v("xb", 0, C), v("xf", 0, C))
-            act(v("ib", 0, 208), v("xf", 0, 208), scale=0.0)
-        tt(v("cb", 16, 16 + NP), v("xx", 0, NP), v("yy", 0, NP), A.max)
-        turn("tb1", "cb", 7)
-        arrive("ar%d" % (3 * t), 1, [v("gx", 8 * t + 4, 8 * t + 7)])
-        if t == 0:
-            red(col("sm", 2), v("gx", 2, 7), A.add)
-            spread("zb", "zm", ("sm", 2), 7)
+            ts(v("b", 0, C), v("ky", 0, C), col("zat", 0), A.subtract, col("zat", 16), A.is_gt)
+            ts(col("tab", 8), col("zat", 0), col("zat", 16), A.add, float(C), A.add)
+            ts(v("nb", 0, C), v("ky", 0, C), col("zat", 0), A.subtract, col("zat", 16), A.is_le)
+            ms(v("rin", 0, 64), 0.0)
+            ms(col("rin", 64), WHOLE)
+            scan(v("y1", 0, C), v("one", 0, C), v("b", 0, C), col("tab", 8), A.mult, A.add)
+            scan(v("x1", 0, C), v("one", 0, C), v("nb", 0, C), -1.0, A.mult, A.add)
+            ms(col("rin", 65), -WHOLE)
+            ms(v("zbt", 128, 144), 0.0)
+            scan(v("yb", 0, C), v("y1", 0, C), v("b", 0, C), 0.0, A.max, A.mult)
+            ts(col("rin", 66), kf(PS1), 2.0, A.mult, 3.4375, A.add)
+            if rot:
+                ts(col("wof", 2), kf(PB), 16.0, A.mult, 24.0, A.add)
+            tt(row(3), v("x1", 0, C), v("yb", 0, C), A.max)
         else:
-            act(v("junk", 64, 69), v("gx", 8 * t + 2, 8 * t + 7), acc=col("sm", 2))
-            spread("zb", "zm", ("sm", 2), 3)
+            tt(v("tab", 0, 16), v("zat", 0, 16), v("zat", 16, 32), A.add)
+            act(v("fl", 0, C), v("tab", 8, 16, ind=nof))
+            tt(v("b", 0, C), v("tab", 0, 8, ind=nof), v("ky", 0, C), A.is_lt)
+        arrive("ar%d" % (3 * t), 1, [v("dl", do + C + 4, do + C + 7)])
+        red(col("sm", 2), v("dl", do + C + 2, do + C + 7), A.add)
+        if t:
+            scan(v("y1", 0, C), v("fl", 0, C), v("b", 0, C), -1.0, A.max, A.add)
+
+        def put_sum(vec, x, to, fro, t=t):
+            o, m, s = v("zb", 32 * x, 32 * x + 32, 1, *to), v("zm", 32 * t, 32 * t + 32, 1, *fro), col("sm", 2, *fro)
+            ts(o, m, s, A.mult, 0.4375 - x / 8.0, A.add) if vec else act(o, m, bias=0.4375 - x / 8.0, scale=s)
+        spread(put_sum, 6 if t == 0 else 5)
+        if t:
+            scan(row(3), v("y1", 0, C), v("b", 0, C), 0.0, A.max, A.mult)
         tr(v("zbt", 0, 128), v("zb", 0, 128))
-        red(col("sm", 3), v("zbt", 0, 128), A.max)
-        ts(col("ri", 0), col("sm", 3), kf(NB), A.add)
-        ts(col("of1", 0), col("ri", 0), col("sm", 3), A.subtract, 16.0, A.mult)
-        cp(v("sel", 0, 16), v("tb1", 0, 448, ind=col("of1", 0)))
-        cp(v("lfl", 0, 224, ind=v("sel", 0, n)), v("atp", 0, NP))
-        turn("tb2", "lfl", 6)
-        cp(v("lro", 0, 16), v("tb2", 0, 416, ind=wrot))
+        turn("tb1", 3)
+        red(col("sm", 3), v("zbt", 0, 128, 2), A.max)
+        scan(v("rx", 0, 66 + nk), v("zbt", 0, 132 + 2 * nk, 2), v("rin", 0, 66 + nk), 0.0, A.max, A.add)
+        ts(v("of", 0, nk), v("rx", 66, 66 + nk), col("sm", 3), A.subtract, 8.0, A.mult)
+        picks = v("tb1", 0, 2 * TW, ind=v("of", 0, nk))
+        if t == 0:
+            cp(v("npo", 0, 16), picks)
+        else:
+            tt(v("gm", 0, 16 * nk), picks, v("ge", go, go + 16 * nk), A.mult)
+            scan(v("hm", 0, 16 * nk), v("ge", 128 + go, 128 + go + 16 * nk), v("gm", 0, 16 * nk), 0.0, A.mult, A.add)
+            cp(v("npo", 0, 10), v("hm", E - 1, 10 * E, E))
+        cp(row(t, v("npo", 0, 10)), row(t - 1) if t else v("pl", C, 2 * C))
+        turn("tb2", t)
+        cp(v("lro", 0, 16), v("tb2", 0, 2 * TW, ind=wrot))
         for b in range(4):
             (act if b % 2 else cp)(v("ft", b, 640, 4), v("tp", C * b, C * b + C, ind=lro))
         x0 = XW * t
@@ -422,49 +447,61 @@ def rank_program(g, core, T, topo):
             send("ar%d" % (3 * t + 1), {r: (f(v(nm, x0 + qf + place(d, r), x0 + qf + place(d, r) + S)),
                                             f(v(nm, x0 + lay(r)[1] + slot(r, d), x0 + lay(r)[1] + slot(r, d) + S))) for r in peers})
         more = t < R - 1
-        n2 = 2 * nn
-        so = 8 * t
         if t == 0:
-            act(v("xh", 0, C), v("xf", 0, C), bias=0.5)
-            for b in range(1, 4):
-                unit(b)
-            ms(v("tb3", 192, TW), 0.0)
-            ms(v("st", 0, 16), float(C))
-            ms(v("atl", C, 208), -300.0)
-        cp(v("ib", 16, 16 + C, ind=lro), v("xb", 0, C))
-        if rot:
-            cp(v("ltr", 0, 16), v("tb2", 0, 416, ind=wtrue))
+            act(v("xb", 0, C), v("xf", 0, C))
+            act(kf(NB0), kf(B0), bias=float(rot), scale=-float(rot))
+            act(kf(O21), col("rin", 66), bias=kf(O20), scale=-8.0)
+            act(kf(WB), kf(B0), bias=-float(rot), scale=float(rot))
+            if rot:
+                act(v("xr", 0, C - rot), v("xf", 0, C - rot), bias=kf(NB0))
+                act(v("xr", C - rot, C), v("xf", C - rot, C), bias=kf(WB))
+        if more:
+            for m in range(nn):
+                act(v("cu", 32 * m, 32 * m + 32), v("one", 0, 32), bias=1.0, scale=col("tab", 8 + 4 * m))
+            if rot:
+                cp(v("ltr", 0, 16), v("tb2", 0, 2 * TW, ind=wtrue))
+            ts(col("of", 6), col("of", 0), kf(O21), A.add)
+            tr(v("cut", 0, 32 * nn), v("cu", 0, 32 * nn))
+            act(v("ky", 0, C), v("atn", 0, C, ind=ltr))
+        cp(row(4, lro), v("xr" if rot else "xb", 0, C))
         if t == 0:
-            ts(kf(KDA), kf(KD_), -1.0 / 256, A.mult)
-            ts(kf(KDB), kf(KD_), 255.0 / 256, A.mult)
-            ts(v("oh", 0, 4), v("xf", 0, 4), kf(M1_), A.is_equal)
-            ts(v("oh", 4, 8), v("xf", 0, 4), kf(M_), A.is_equal)
-            ms(v("st", 0, 16, 8), 0.0)
-        turn("tb3", "ib", 6)
+            act(kf(T1S), kf(B3), bias=-1.0 / 256, scale=1.0 / 256)
+            act(kf(T1B), kf(B3), bias=160.0 / 256, scale=-161.0 / 256)
+            act(kf(V0), kf(B3), scale=-160.0 / 256)
+            act(kf(H1), kf(B1), scale=float(C))
+        if more:
+            lo, hi = sc(2 * t), sc(2 * t + 1)
+            cp(v("th", 16 * t, 16 * t + 16), v("cut", 0, 32 * nn, ind=col("of", 6)))
+            act(v("t1", 0, C), row(t), bias=kf(T1B), scale=kf(T1S))
+        turn("tb3", 4)
         if not more:
-            cp(v("olf", 0, C), v("lfl", 16, 16 + C))
+            cp(v("olf", 0, C), row(t))
             dma("s", T.ol[:], T.olf[8:128:16, :], [], [v("olf", 0, C)])
             qz("vq", "vs", 0, 128, v("vt", 0, 512))
         if t == 0:
-            ts(col("st", 1), col("sel", n), -15.0, A.add)
+            ts(lo, kf(B2), col("th", 0), A.mult)
+            ts(hi, kf(B2), float(C), A.mult, col("th", 0), A.max)
         if t == 1:
-            ts(v("st", 9, 12, 2), v("sel", n, n + 2), -15.0, A.add)
-            cp(col("st", 10), col("st", 1))
-        cp(v("iof", 0, 16), v("tb3", 0, 416, ind=wtrue))
+            ts(sc(DD), col("th", 18), col("th", 16), A.subtract, kf(B2), A.mult)
+        cp(v("iof", 0, 16), v("tb3", 0, 2 * TW, ind=wcol))
+        if t == 1:
+            ts(sc(TP), sc(DD), col("th", 16), A.add)
+            ts(lo, kf(B1), sc(TP), A.mult, sc(0), A.max)
+            ts(hi, kf(H1), sc(TP), A.max, sc(1), A.min)
         if more:
-            tt(v("sx", 0, 4), v("st", so, so + 4), v("oh", 4 * t, 4 * t + 4), A.mult)
-            tt(v("sx", 4, 8), v("st", so + 1, so + 5), v("oh", 4 * t, 4 * t + 4), A.mult)
-            tt(v("sx", 8, 8 + n2 - 1), v("kc", 0, n2 - 1), v("st", so + 1, so + n2), A.subtract)
-            red(col("sc", 0), v("sx", 0, 4), A.add)
-            red(col("sc", 1), v("sx", 4, 8), A.add)
-            if t == 0:
-                ts(v("awx", 0, 16), v("awx", 0, 16), kf(R_), A.add)
-            ts(col("sc", 3), col("sc", 0), col("sc", 1), A.add, -0.5, A.mult)
-            ts(col("sc", 4), col("sc", 1), col("sc", 0), A.subtract, 0.5, A.mult)
-            tt(col("sc", 2), col("sc", 1), col("sc", 0), A.subtract)
-            ts(col("sc", 5), col("sc", 1), kf(KDA), A.mult, kf(KD_), A.add)
-        lo = x0 + (8 if first else C)
-        arrive("ar%d" % (3 * t + 1), 2, [v("fq", lo, lo + 3 * S), v("fs", lo, lo + 3 * S)])
+            scan(v("t2", 0, C), v("kc", 0, C), v("t1", 0, C), 161.0 / 256, A.mult, A.add)
+            ts(sc(LH), lo, hi, A.add, -1.0, A.add)
+            tt(sc(SZ), hi, lo, A.subtract)
+            ts(sc(VB), lo, -1.0, A.add, kf(B3), A.mult)
+            ts(v("at0", 0, C), v("xb", 0, C), lo, A.is_equal)
+            act(v("a2", 0, C), v("xf", 0, C), AF.Abs, bias=sc(LH), scale=-2.0)
+            act(v("a3", 0, C), row(4), AF.Abs, bias=sc(LH), scale=-2.0)
+            act(sc(NS), sc(SZ), scale=-FAR)
+        if t == 0:
+            for b in range(4):
+                qz("eq", "es", 128 * b, 128, v("ea", 3 - b, 515 - b))
+        lo_ = x0 + (8 if first else C)
+        arrive("ar%d" % (3 * t + 1), 2, [v("fq", lo_, lo_ + 3 * S), v("fs", lo_, lo_ + 3 * S)])
         for b in range(4):
             mm(bank(4 + b), "wq", "wsc", 128 * b, "fq", "fs", x0 + mv)
         for b in range(4):
@@ -477,56 +514,43 @@ def rank_program(g, core, T, topo):
             send("ar%d" % (3 * t + 2), {r: (f(v(nm, x0 + qh + slot(d, r), x0 + qh + slot(d, r) + S)),
                                             f(v(nm, x0 + lay(r)[3] + place(r, d), x0 + lay(r)[3] + place(r, d) + S))) for r in peers})
         if t == 0:
-            if rot:
-                act(v("tph", 0, C - rot), v("xh", rot, C))
-                act(v("tph", C - rot, C), v("xh", 0, rot))
-            act(v("agf", 0, C), bank(1), bias=kf(KTB), scale=kf(KTA))
-            act(v("cf", 0, C), v("xf", 0, C), bias=kf(KDB), scale=kf(KDA))
+            ms(v("ph", 0, C + 2, C + 1), 0.0)
+            ms(v("ge", 0, 256), 1.0)
+            ts(v("awx", 0, 12), v("awx", 0, 12), kf(R_), A.add)
+            act(v("dl", DW + C + 3, R * DW, DW), v("one", 0, 2), scale=col("dl", C + 3))
+            ts(v("zm", 32, 64), v("zi", 0, 32), kf(B2), A.is_equal, -8.0, A.mult)
+            ts(v("zm", 64, 96), v("zi", 32, 64), kf(N2), A.is_equal, -8.0, A.mult)
+            act(kf(CB), kf(B0), bias=2.0 * (TW // 16 - 1) + 2.4375)
+            act(kf(CA2), kf(B1), bias=kf(O20), scale=32.0)
         if more:
-            n_2 = 10 + n2 - 1
-            act(v("a3", 0, C), v("tph" if rot else "xh", 0, C), AF.Abs, bias=col("sc", 3))
-            act(v("a1", 0, C), v("xh", 0, C), AF.Abs, bias=col("sc", 3))
-            act(v("atl", 0, C), v("atn", 0, C, ind=ltr))
+            E2, g2 = 4 * nn, 48 * t
+            n2 = 12 if t == 0 else 10
+            act(kf(PA2), kf(B2 + t), AF.Abs, bias=kf(NGA))
+            act(v("thr", 0, C), v("a3", 0, C), AF.Relu, bias=sc(NS), scale=FAR)
+            act(kf(CA1), kf(B3 if t else K1), bias=kf(CB), scale=2.0)
+            act(sc(S2), sc(VB), scale=0.5)
+            act(col("dl", do + DW + C + 1), sc(VB), bias=kf(V0), scale=1.0 / 256)
+            act(col("rin", 66), kf(PA2), bias=kf(CA1), scale=-2.0 * (TW // 16 - 1))
+            ms(v("rin", 67, 72), 32.0 / E2)
+            scan(v("ph", 1, C + 1), v("at0", 0, C), v("t2", 0, C), 0.0, A.add, A.min)
+            starts = [col("th", 0)] if t == 0 else [col("th", 16), col("th", 0), col("th", 18)]
+            step = lambda m: v("ge", g2 + 2 * m, g2 + 10 * E2, E2)
+            for m, st in enumerate(starts):
+                ts(v("ge", g2 + 2 * m + 2, g2 + n2 * E2, E2), v("awx", 0, n2), st, A.is_ge)
+            tt(v("dl", do + DW, do + DW + C + 1), v("ph", 0, C + 1), v("ph", 1, C + 2), A.subtract)
+            act(v("ge", g2 + 1, g2 + n2 * E2, 2), v("ge", g2, g2 + n2 * E2, 2))
+            act(v("ge", 128 + g2, 128 + g2 + n2 * E2, 2), v("ge", g2, g2 + n2 * E2, 2), bias=1.0, scale=-1.0)
             if t == 0:
-                qz("eq", "es", 0, 512, v("et", 0, 2048))
-                ms(v("xi", 11, 32, 16), 0.0)
-                ms(v("xi", 12, 32, 16), float(C + 15))
-                ts(kf(XA), kf(M1_), -16.0, A.mult, -7.5, A.add)
-                ts(kf(XB_), kf(M_), -16.0, A.mult, -7.5, A.add)
-            blk = lambda k, a=0: v("mw", 16 * k + a, 16 * k + a + n_2)
-            for m in range(1, n2):
-                ts(v("mw", 16 * (m - 1), 16 * m), v("awx", 0, 16), col("st", so + m), A.is_ge, col("sx", 7 + m), A.mult)
-                ts(blk(2 + m), v("awx", 4 - m, 4 - m + n_2), col("st", so + m), A.is_ge)
-            if t == 0:
-                ts(v("xi", 0, 32), v("xi", 0, 32), kf(XA), A.add)
-                ts(v("xi", 32, 64), v("xi", 32, 64), kf(XB_), A.add)
-            for m in range(1, n2):
-                tt(blk(5 + m), blk(m - 1, 4 - m), blk(m - 1, 3 - m), A.subtract)
-            if n2 > 2:
-                tt(blk(9), blk(3), blk(4), A.add)
-                tt(blk(10), blk(6), blk(7), A.add)
-                tt(blk(11), blk(8), v("awx", 3, 3 + n_2), A.add)
-                tt(blk(3), blk(9), blk(5), A.add)
-                tt(blk(11), blk(11), blk(10), A.add)
+                act(kf(O21), col("rin", 66), bias=kf(CA2), scale=-8.0)
+                ts(nof, step(1), 4.0, A.mult)
             else:
-                tt(blk(11), blk(6), v("awx", 3, 3 + n_2), A.add)
-            ts(blk(9), blk(3), -16.0, A.mult)
-            ts(v("mt", 0, C), v("a3", 0, C), col("sc", 4), A.is_ge, BIG, A.mult)
-            act(v("thr", 0, C), v("mt", 0, C, ind=iof))
-            tt(blk(10), blk(11), blk(9), A.add)
-            cp(v("nof", 0, n_2), blk(3))
-            cp(v("mof", 0, n_2), blk(10))
-            mof, NQ = v("mof", 0, n_2), 16 * n_2
-            ts(v("mk", 0, C), v("a1", 0, C), col("sc", 4), A.is_lt)
-            tt(v("fr0", 0, C), v("agf", 0, C, ind=ltr), v("cf", 0, C), A.add)
-            act(v("cx", 0, NQ), v("xf", 0, 208, ind=mof), bias=16.0)
-            act(v("a4", 0, 32), v("xi", 32 * t, 32 * t + 32), AF.Abs, bias=col("sc", 3))
-            act(v("atp", 0, NQ), v("atl", 0, 208, ind=mof))
-            tt(v("fr", 0, C), v("fr0", 0, C), v("mk", 0, C), A.mult)
-            ts(v("z", 0, NQ), v("cx", 0, NQ), C + 15.5, A.is_lt)
-            ts(v("zm", 0, 32), v("a4", 0, 32), -8.0, A.add, col("sc", 4), A.is_lt)
-        lo = x0 + (C if first else 8)
-        arrive("ar%d" % (3 * t + 2), 2, [v("hq", lo, lo + 3 * S), v("hs", lo, lo + 3 * S)])
+                tt(v("nd", 0, 10), step(1), step(2), A.add)
+            ts(v("mk", 0, C), v("a2", 0, C), sc(SZ), A.is_lt)
+            if t == 1:
+                tt(v("nd", 16, 26), v("nd", 0, 10), step(3), A.add)
+                ts(nof, v("nd", 16, 26), 2.0, A.mult)
+        lo_ = x0 + (C if first else 8)
+        arrive("ar%d" % (3 * t + 2), 2, [v("hq", lo_, lo_ + 3 * S), v("hs", lo_, lo_ + 3 * S)])
         for b in range(4):
             mm(bank(b), "eq", "es", 128 * b, "hq", "hs", x0 + dm)
         for b in range(4):

@@ -22,7 +22,7 @@ SCRATCH = {
     "upq": _sb(256, MX), "ups": _sb(256, U8), "wq": _sb(512, MX), "wsc": _sb(512, U8),
     "tq": _sb(4 * C, MX), "tsc": _sb(4 * C, U8),
     "fq": _sb(R * XW, MX), "fs": _sb(R * XW, U8), "hq": _sb(R * XW, MX), "hs": _sb(R * XW, U8),
-    "ft": _sb(640, BF), "ht": _sb(640, BF), "gt": _sb(640, BF), "tt": _sb(640, BF), "tp": _sb(640, BF),
+    "oq": _sb(R * 128, MX), "osp": _sb(R * 128, U8), "ft": _sb(640, BF), "ht": _sb(640, BF), "gt": _sb(640, BF), "tt": _sb(640, BF), "tp": _sb(640, BF),
     "eq": _sb(512, MX), "es": _sb(512, U8), "ea": _sb(516, BF),
     "kt": _sb(512, BF), "kq": _sb(128, MX), "ks": _sb(128, U8), "ha": _sb(128, BF),
     "ct": _sb(1920, BF), "cq": _sb(480, MX), "cs": _sb(480, U8), "sg": _sb(5 * C, BF),
@@ -46,6 +46,7 @@ SCRATCH = {
 }
 SEMAPHORES = (["sv", "sa", "sp", "sg", "sent"] + ["ar%d" % k for k in range(3 * R)] + ["d%d" % k for k in range(12)])
 
+ORDER = ["max sum unit zb6 zbt turn best", "tab fl sum b zb5 y1 zbt cb best turn"]
 A = AluOpType
 AF = ActivationFunctionType
 
@@ -84,10 +85,11 @@ def deal(topo, cores, r):
         same = [o for o in free if len(free[o]) == width]
         left = [e for e in free[same[0]] if e not in taken]
         k = 1
-        while 2 * k * len(same) <= len(left):
+        while 2 * k * len(same) <= len(left) and (not taken or 2 * k <= len(out[min(out)])):
             k *= 2
+        part = len(left) // len(same)
         for n_, o in enumerate(same):
-            out[o] = left[n_ * k:(n_ + 1) * k]
+            out[o] = left[n_ * part:(n_ + 1) * part:part // k]
             taken += out[o]
     return out
 
@@ -199,11 +201,13 @@ def rank_program(g, core, T, topo):
     rot, first = plan(d)
 
     def lay(r):
-        return (128, 8, 0, 120) if plan(r)[1] else (0, 120, 128, 8)
+        return (128, 8, 0, 120) if plan(r)[1] else (0, 128, 128, 8)
+
+    def turn_(r, o):
+        return [x for x in range(N) if x != r].index(o)
 
     def slot(r, o):
-        k = [x for x in range(N) if x != r].index(o)
-        return S * k if plan(r)[1] else S + S * k
+        return S * turn_(r, o) + (0 if plan(r)[1] else S)
 
     def place(r, o):
         return (S * o - plan(r)[0]) % C
@@ -228,6 +232,10 @@ def rank_program(g, core, T, topo):
     iota(v("zi", 0, 32), [[0, 8], [1, 2], [0, 2]])
     iota(v("zi", 32, 64), [[0, 4], [1, 4], [0, 2]])
     iota(v("awx", 0, 12), [[16, 12]])
+    iota(v("ea", 0, 516), [[0, 516]], 1)
+    op("g", lambda e: e.affine_select(ap(v("ea", 0, 516)), ap(v("ea", 0, 516)), [[1, 516]], A.is_equal, 0.0, -3, -4),
+       [v("ea", 0, 516)], [v("ea", 0, 516)])
+    unit = lambda b: qz("eq", "es", 128 * b, 128, v("ea", 3 - b, 515 - b))
     R_, G_, B0, B1, B2, B3, GA, N2, K1 = range(9)
     (NB3, NGA, SIG, KB, C0, W16, T1S, T1B, TI0, H1, V0, PA1, PA2, CA1, CA2, CB, COL1, COL2, O20, O21, KK, PB, PS0, PS1, PS2, NB2, NN2, Z0, NB0,
      WB, NG) = range(9, 40)
@@ -235,8 +243,6 @@ def rank_program(g, core, T, topo):
     p_ = col("ki", 9)
     ms(v("uoi", 8, 16), 8)
     ms(v("ct", 1280 + 3, 1920, 4), 0.0)
-    ms(v("dl", 0, C + 1), 1.0 / 256)
-    ms(col("dl", C + 1), 0.0)
     ts(col("ki", R_), p_, 15, A.bitwise_and)
     ts(col("ki", G_), p_, 4, A.arith_shift_right)
     for k, (sh, m) in enumerate(((0, 1), (1, 1), (2, 1), (3, 1), (4, 1), (1, 3), (2, 3))):
@@ -254,47 +260,35 @@ def rank_program(g, core, T, topo):
     act(v("kc", 0, C), v("jm", 0, C), bias=kf(B3), scale=0.0)
     act(kf(W16), kf(B3), bias=float(C), scale=-float(C))
     act(kf(NN2), kf(B3), bias=-1.0)
-    act(kf(SIG), kf(B3), bias=-1.0, scale=2.0)
-    act(kf(KB), kf(B3), bias=162.0, scale=-323.0)
-    act(kf(TI0), kf(GA), bias=-1.0, scale=0.0625)
-    act(kf(Z0), kf(B3), bias=-8.0, scale=8.0)
     for k in range(7):
         act(v("lf", max(0, TW * k - 16), TW * k + 16), v("one", 0, 32 if k else 16), scale=0.0)
-    act(col("dl", C + 3), kf(G_), bias=kf(TI0), scale=0.125)
-    act(v("zm", 0, 32), v("one", 0, 32), scale=kf(Z0))
     act(v("ha", 0, 128), v("hj", 0, 128), AF.Abs, bias=kf(NG))
-    act(kf(O20), kf(GA), bias=11.5, scale=16.0)
-    for t in range(4):
-        act(v("kt", t, 512, 4), v("ha", 0, 128), AF.Relu, bias=1.0, scale=-1.0)
     ts(kf(PA1), kf(B3), -2.0, A.add)
     ts(v("m8", 16, 24), v("m8", 0, 8), kf(GA), A.is_equal, 256.0, A.mult)
     ts(v("m8", 24, 32), v("m8", 8, 16), kf(PA1), A.mult, kf(NB3), A.add)
     ts(kf(KK), kf(R_), 9.0, A.min)
     ts(kf(PB), kf(R_), 10.0, A.is_ge, kf(B0), A.max)
-    ms(col("se", C), 0.0)
-    ms(v("se", C + 1, C + 3), -BIG)
-    tt(v("m8", 32, 40), v("m8", 16, 24), v("m8", 24, 32), A.mult)
-    tt(kf(PS0), kf(PB), kf(GA), A.is_equal)
 
     qz("uq", "us", 0, 128, v("ut", 0, 512))
-    ts(kf(PS1), kf(PS0), TW // 16 - 1.0, A.mult, kf(KK), A.add)
-    ts(kf(PS2), kf(R_), 10.0 - rot // 16, A.is_ge, -10.0, A.mult)
+    qz("tq", "tsc", 0, C, v("xt", 0, 640))
     cp(words(v("upq", 0, 128)), words(v("uq", 0, 128), v("uof", 0, 8)))
     act(v("ups", 0, 128), v("us", 0, 128, ind=v("uof", 0, 8)))
-    qz("tq", "tsc", 0, C, v("xt", 0, 640))
     mm(bank(0), "upq", "ups", 0, "tq", "tsc", 0)
     mm(bank(3), "upq", "ups", 0, "tq", "tsc", 0)
     cp(words(v("upq", 128, 256)), words(v("uq", 0, 128), v("uof", 8, 16)))
     act(v("ups", 128, 256), v("us", 0, 128, ind=v("uof", 8, 16)))
     mm(bank(4), "upq", "ups", 128, "tq", "tsc", 0)
-    ts(col("wof", 0), kf(PS1), 16.0, A.mult, 24.0, A.add)
-    ts(kf(PS2), kf(PS2), kf(KK), A.add, float(TW // 16 - 1 + rot // 16), A.add)
+    tt(kf(PS0), kf(PB), kf(GA), A.is_equal)
+    tt(v("m8", 32, 40), v("m8", 16, 24), v("m8", 24, 32), A.mult)
+    ts(kf(PS2), kf(R_), 10.0 - rot // 16, A.is_ge, -10.0, A.mult)
+    for t in range(4):
+        act(v("kt", t, 512, 4), v("ha", 0, 128), AF.Relu, bias=1.0, scale=-1.0)
     tt(v("pm", 0, C), bank(0), v("pk", 0, C), A.max)
-    qz("kq", "ks", 0, 128, v("kt", 0, 512))
+    ts(kf(PS1), kf(PS0), TW // 16 - 1.0, A.mult, kf(KK), A.add)
+    ts(kf(PS2), kf(PS2), kf(KK), A.add, float(TW // 16 - 1 + rot // 16), A.add)
     act(v("l0", 0, C), bank(4), AF.Sign)
     scan(v("pw", 0, C), v("up", 0, C), v("pm", 0, C), 0.0, A.add, A.min)
-    ts(kf(PB), kf(PS0), 1.0 - TW // 16, A.mult, kf(PS2), A.add)
-    ts(col("wof", 4), kf(PS1), 16.0, A.mult, 25.0, A.add)
+    qz("kq", "ks", 0, 128, v("kt", 0, 512))
     NV = 6
     cmp_ = lambda c, a=0, b=C: v("ct", 640 * (c // 4) + c % 4 + 4 * a, 640 * (c // 4) + c % 4 + 4 * b - 3, 4)
     count_ = lambda c: scan(v("so", C * c, C * c + C), v("one", 0, C), cmp_(c), col("tie", 16 * c + 15), A.mult, A.add)
@@ -323,6 +317,7 @@ def rank_program(g, core, T, topo):
         if c == NV - 1:
             scan(v("wn", C, 2 * C), v("kc", 0, C), v("wn", 0, C), -1.0, A.mult, A.add)
     qz("cq", "cs", 0, C, v("ct", 0, 640))
+    ts(col("wof", 0), kf(PS1), 16.0, A.mult, 24.0, A.add)
     ts(v("ato", 0, 10), v("so", C - 1, 10 * C, C), -1.0, A.mult, float(C), A.add)
     ato = v("ato", 0, 10)
     qz("cq", "cs", C, C, v("ct", 640, 1280))
@@ -331,8 +326,19 @@ def rank_program(g, core, T, topo):
     for s in range(3):
         mm(bank(2), "kq", "ks", 0, "cq", "cs", C * s, start=s == 0, stop=s == 2)
     act(v("kc", C, 2 * C), v("one", 0, C), scale=kf(NB3))
-    for b in range(3):
-        act(v("tp", C * b, C * b + C), v("xt", b, 640, 4))
+    act(kf(SIG), kf(B3), bias=-1.0, scale=2.0)
+    act(kf(KB), kf(B3), bias=162.0, scale=-323.0)
+    act(kf(TI0), kf(GA), bias=-1.0, scale=0.0625)
+    act(kf(Z0), kf(B3), bias=-8.0, scale=8.0)
+    act(kf(O20), kf(GA), bias=11.5, scale=16.0)
+    act(v("dl", 0, C), v("one", 0, C), scale=1.0 / 256)
+    act(col("dl", C), col("one", 0), scale=1.0 / 256)
+    act(col("dl", C + 1), col("one", 0), scale=0.0)
+    act(col("se", C), col("one", 0), scale=0.0)
+    act(v("se", C + 1, C + 3), v("one", 0, 2), scale=-BIG)
+    act(col("dl", C + 3), kf(G_), bias=kf(TI0), scale=0.125)
+    act(v("zm", 0, 32), v("one", 0, 32), scale=kf(Z0))
+    act(v("tp", 0, C), v("xt", 0, 640, 4))
     act(v("pl", 0, C), row(5), bias=kf(NB3), scale=kf(B3))
 
     def spread(put, on_vector):
@@ -345,7 +351,7 @@ def rank_program(g, core, T, topo):
         tr(v(tb, 0, TW), v("lf", TW * k, TW * k + TW))
         tr(v(tb, TW, 2 * TW), v("lf", TW * k + 16, TW * k + 16 + TW))
 
-    qf, mv, qh, dm = lay(d)
+    qf, qh, f0 = lay(d)[0], lay(d)[2], 32 if first else 0
     wtrue, wrot, wcol = col("wof", 0), col("wof", 2 if rot else 0), col("wof", 4)
     ltr, lro, iof, nof = v("ltr" if rot else "lro", 0, 10), v("lro", 0, 10), v("iof", 0, 10), v("nof", 0, 10)
     SZ, VO, S2, NS, LH, TP, VB, DD, HX = range(4, 13)
@@ -360,9 +366,19 @@ def rank_program(g, core, T, topo):
             mm(bank(4), "upq", "ups", 128, "tq", "tsc", C * t)
             for b in range(4):
                 act(v("tp", C * b, C * b + C), v("tt", b, 640, 4))
+            step = lambda m: v("ge", go + 2 * m, go + 10 * E, E)
+            tt(v("dl", DW * t, DW * t + C + 1), v("ph", 0, C + 1), v("ph", 1, C + 2), A.subtract)
+            ts(v("mk", 0, C), v("a2", 0, C), sc(SZ), A.is_lt)
+            ms(v("rin", 67, 72), 32.0 / E)
             tt(v("lab", 0, C), bank(4), v("thr", 0, C), A.is_gt)
-            red(col("pp", 0), v("lab", 0, C), A.add)
-            ts(v("w", 0, C), v("lab", 0, C, ind=ltr), sc(SZ), A.mult, col("pp", 0), A.subtract)
+            ts(nof, step(1), 4.0, A.mult) if t == 1 else tt(v("nd", 0, 10), step(1), step(2), A.add)
+            red(col("pp", 0), v("lab", 0, C), A.add, True)
+            if t == 2:
+                tt(v("nd", 16, 26), v("nd", 0, 10), step(3), A.add)
+            ts(v("w", 0, 96), v("lab", 0, C, ind=v(ltr[0], 0, 6)), sc(SZ), A.mult, col("pp", 0), A.add)
+            act(v("w", 96, C), v("lab", 0, C, ind=v(ltr[0], 6, 10)), bias=col("pp", 0), scale=sc(SZ))
+            if t == 2:
+                ts(nof, v("nd", 16, 26), 2.0, A.mult)
             scan(v("e", 0, C), v("w", 0, C), v("mk", 0, C), 0.0, A.add, A.mult)
         else:
             scan(v("e", 0, C), v("one", 0, C), row(5), 0.0, A.mult, A.add)
@@ -373,10 +389,8 @@ def rank_program(g, core, T, topo):
         send("ar%d" % (3 * t), {r: (gain, col("dl", do + C + 4 + [x for x in range(N) if x != r].index(d))) for r in peers})
         act(v("se", 0, C), v("e", 0, C), AF.Abs)
         if t == 0:
-            iota(v("ea", 0, 516), [[0, 516]], 1)
-            op("g", lambda e: e.affine_select(ap(v("ea", 0, 516)), ap(v("ea", 0, 516)), [[1, 516]], A.is_equal, 0.0, -3, -4),
-               [v("ea", 0, 516)], [v("ea", 0, 516)])
             cp(v("ltr", 0, 16), v("tb2", 0, 2 * TW, ind=wtrue))
+            unit(0)
             act(v("atn", 0, C), bank(2), bias=kf(KB), scale=kf(SIG))
         scan(v("fin", 0, C + 3), v("dl", do, do + C + 3), v("se", 0, C + 3), 0.0 if t else -1.0 / 256, A.add, A.max)
         if t == 0:
@@ -392,9 +406,23 @@ def rank_program(g, core, T, topo):
             else:
                 act(o, m, bias=col("sc", S2, *fro), scale=s)
         spread(put_cut, 6 if t else 9)
+        if t == 0:
+            unit(1)
         tr(v("zat", 0, 32), v("za", 0, 32))
         if t == 0:
-            act(v("tp", 3 * C, 4 * C), v("xt", 3, 640, 4))
+            unit(2)
+            for b in range(1, 4):
+                act(v("tp", C * b, C * b + C), v("xt", b, 640, 4))
+            act(v("xb", 0, C), v("xf", 0, C))
+            act(kf(NB0), kf(B0), bias=float(rot), scale=-float(rot))
+            act(kf(WB), kf(B0), bias=-float(rot), scale=float(rot))
+            act(kf(T1S), kf(B3), bias=-1.0 / 256, scale=1.0 / 256)
+            act(kf(T1B), kf(B3), bias=160.0 / 256, scale=-161.0 / 256)
+            act(kf(V0), kf(B3), scale=-160.0 / 256)
+            act(kf(H1), kf(B1), scale=float(C))
+            if rot:
+                act(v("xr", 0, C - rot), v("xf", 0, C - rot), bias=kf(NB0))
+                act(v("xr", C - rot, C), v("xf", C - rot, C), bias=kf(WB))
             ts(v("b", 0, C), v("ky", 0, C), col("zat", 0), A.subtract, col("zat", 16), A.is_gt)
             ts(col("tab", 8), col("zat", 0), col("zat", 16), A.add, float(C), A.add)
             ts(v("nb", 0, C), v("ky", 0, C), col("zat", 0), A.subtract, col("zat", 16), A.is_le)
@@ -403,117 +431,127 @@ def rank_program(g, core, T, topo):
             scan(v("y1", 0, C), v("one", 0, C), v("b", 0, C), col("tab", 8), A.mult, A.add)
             scan(v("x1", 0, C), v("one", 0, C), v("nb", 0, C), -1.0, A.mult, A.add)
             ms(col("rin", 65), -WHOLE)
+            ts(kf(PB), kf(PS0), 1.0 - TW // 16, A.mult, kf(PS2), A.add)
             ms(v("zbt", 128, 144), 0.0)
             scan(v("yb", 0, C), v("y1", 0, C), v("b", 0, C), 0.0, A.max, A.mult)
             ts(col("rin", 66), kf(PS1), 2.0, A.mult, 3.4375, A.add)
             if rot:
                 ts(col("wof", 2), kf(PB), 16.0, A.mult, 24.0, A.add)
-            tt(row(3), v("x1", 0, C), v("yb", 0, C), A.max)
-        else:
-            tt(v("tab", 0, 16), v("zat", 0, 16), v("zat", 16, 32), A.add)
-            act(v("fl", 0, C), v("tab", 8, 16, ind=nof))
-            tt(v("b", 0, C), v("tab", 0, 8, ind=nof), v("ky", 0, C), A.is_lt)
+            act(kf(O21), col("rin", 66), bias=kf(O20), scale=-8.0)
+        more = t < R - 1
+        lo, hi = sc(2 * t), sc(2 * t + 1)
         arrive("ar%d" % (3 * t), 1, [v("dl", do + C + 4, do + C + 7)])
-        red(col("sm", 2), v("dl", do + C + 2, do + C + 7), A.add)
-        if t:
-            scan(v("y1", 0, C), v("fl", 0, C), v("b", 0, C), -1.0, A.max, A.add)
 
         def put_sum(vec, x, to, fro, t=t):
             o, m, s = v("zb", 32 * x, 32 * x + 32, 1, *to), v("zm", 32 * t, 32 * t + 32, 1, *fro), col("sm", 2, *fro)
             ts(o, m, s, A.mult, 0.4375 - x / 8.0, A.add) if vec else act(o, m, bias=0.4375 - x / 8.0, scale=s)
-        spread(put_sum, 6 if t == 0 else 5)
-        if t:
-            scan(row(3), v("y1", 0, C), v("b", 0, C), 0.0, A.max, A.mult)
-        tr(v("zbt", 0, 128), v("zb", 0, 128))
-        turn("tb1", 3)
-        red(col("sm", 3), v("zbt", 0, 128, 2), A.max)
-        scan(v("rx", 0, 66 + nk), v("zbt", 0, 132 + 2 * nk, 2), v("rin", 0, 66 + nk), 0.0, A.max, A.add)
-        ts(v("of", 0, nk), v("rx", 66, 66 + nk), col("sm", 3), A.subtract, 8.0, A.mult)
-        picks = v("tb1", 0, 2 * TW, ind=v("of", 0, nk))
-        if t == 0:
-            cp(v("npo", 0, 16), picks)
-        else:
-            tt(v("gm", 0, 16 * nk), picks, v("ge", go, go + 16 * nk), A.mult)
-            scan(v("hm", 0, 16 * nk), v("ge", 128 + go, 128 + go + 16 * nk), v("gm", 0, 16 * nk), 0.0, A.mult, A.add)
-            cp(v("npo", 0, 10), v("hm", E - 1, 10 * E, E))
-        cp(row(t, v("npo", 0, 10)), row(t - 1) if t else v("pl", C, 2 * C))
-        turn("tb2", t)
-        cp(v("lro", 0, 16), v("tb2", 0, 2 * TW, ind=wrot))
-        for b in range(4):
-            (act if b % 2 else cp)(v("ft", b, 640, 4), v("tp", C * b, C * b + C, ind=lro))
-        x0 = XW * t
-        qz("fq", "fs", x0 + qf, C, v("ft", 0, 640))
-        for nm, f in (("fq", bytes_), ("fs", lambda x: x)):
-            send("ar%d" % (3 * t + 1), {r: (f(v(nm, x0 + qf + place(d, r), x0 + qf + place(d, r) + S)),
-                                            f(v(nm, x0 + lay(r)[1] + slot(r, d), x0 + lay(r)[1] + slot(r, d) + S))) for r in peers})
-        more = t < R - 1
-        if t == 0:
-            act(v("xb", 0, C), v("xf", 0, C))
-            act(kf(NB0), kf(B0), bias=float(rot), scale=-float(rot))
-            act(kf(O21), col("rin", 66), bias=kf(O20), scale=-8.0)
-            act(kf(WB), kf(B0), bias=-float(rot), scale=float(rot))
-            if rot:
-                act(v("xr", 0, C - rot), v("xf", 0, C - rot), bias=kf(NB0))
-                act(v("xr", C - rot, C), v("xf", C - rot, C), bias=kf(WB))
+        steps = {
+            "tab": lambda: tt(v("tab", 0, 16), v("zat", 0, 16), v("zat", 16, 32), A.add),
+            "fl": lambda: act(v("fl", 0, C), v("tab", 8, 16, ind=nof)),
+            "b": lambda: tt(v("b", 0, C), v("tab", 0, 8, ind=nof), v("ky", 0, C), A.is_lt),
+            "y1": lambda: scan(v("y1", 0, C), v("fl", 0, C), v("b", 0, C), -1.0, A.max, A.add),
+            "cb": lambda: scan(row(3), v("y1", 0, C), v("b", 0, C), 0.0, A.max, A.mult),
+            "max": lambda: tt(row(3), v("x1", 0, C), v("yb", 0, C), A.max),
+            "turn": lambda: turn("tb1", 3),
+            "unit": lambda: unit(3),
+            "sum": lambda: red(col("sm", 2), v("dl", do + C + 2, do + C + 7), A.add),
+            "zb5": lambda: spread(put_sum, 5), "zb6": lambda: spread(put_sum, 6), "zb4": lambda: spread(put_sum, 4), "zb7": lambda: spread(put_sum, 7),
+            "zbt": lambda: tr(v("zbt", 0, 128), v("zb", 0, 128)),
+            "best": lambda: (red(col("sm", 3), v("zbt", 0, 128, 2), A.max),
+                             scan(v("rx", 0, 66 + nk), v("zbt", 0, 132 + 2 * nk, 2), v("rin", 0, 66 + nk), 0.0, A.max, A.add)),
+        }
+        for name in ORDER[min(t, 1)].split():
+            steps[name]()
         if more:
             for m in range(nn):
                 act(v("cu", 32 * m, 32 * m + 32), v("one", 0, 32), bias=1.0, scale=col("tab", 8 + 4 * m))
-            if rot:
-                cp(v("ltr", 0, 16), v("tb2", 0, 2 * TW, ind=wtrue))
-            ts(col("of", 6), col("of", 0), kf(O21), A.add)
+        ts(v("of", 0, nk), v("rx", 66, 66 + nk), col("sm", 3), A.subtract, 8.0, A.mult)
+        if more:
             tr(v("cut", 0, 32 * nn), v("cu", 0, 32 * nn))
-            act(v("ky", 0, C), v("atn", 0, C, ind=ltr))
-        cp(row(4, lro), v("xr" if rot else "xb", 0, C))
-        if t == 0:
-            act(kf(T1S), kf(B3), bias=-1.0 / 256, scale=1.0 / 256)
-            act(kf(T1B), kf(B3), bias=160.0 / 256, scale=-161.0 / 256)
-            act(kf(V0), kf(B3), scale=-160.0 / 256)
-            act(kf(H1), kf(B1), scale=float(C))
+        picks = v("tb1", 0, 2 * TW, ind=v("of", 0, nk))
+        bounds = []
         if more:
-            lo, hi = sc(2 * t), sc(2 * t + 1)
-            cp(v("th", 16 * t, 16 * t + 16), v("cut", 0, 32 * nn, ind=col("of", 6)))
-            act(v("t1", 0, C), row(t), bias=kf(T1B), scale=kf(T1S))
-        turn("tb3", 4)
-        if not more:
-            cp(v("olf", 0, C), row(t))
-            dma("s", T.ol[:], T.olf[8:128:16, :], [], [v("olf", 0, C)])
-            qz("vq", "vs", 0, 128, v("vt", 0, 512))
+            bounds += [lambda: ts(col("of", 6), col("of", 0), kf(O21), A.add),
+                       lambda: cp(v("th", 16 * t, 16 * t + 16), v("cut", 0, 32 * nn, ind=col("of", 6)))]
         if t == 0:
-            ts(lo, kf(B2), col("th", 0), A.mult)
-            ts(hi, kf(B2), float(C), A.mult, col("th", 0), A.max)
+            bounds += [lambda: (ts(lo, kf(B2), col("th", 0), A.mult), ts(hi, kf(B2), float(C), A.mult, col("th", 0), A.max))]
         if t == 1:
-            ts(sc(DD), col("th", 18), col("th", 16), A.subtract, kf(B2), A.mult)
-        cp(v("iof", 0, 16), v("tb3", 0, 2 * TW, ind=wcol))
-        if t == 1:
-            ts(sc(TP), sc(DD), col("th", 16), A.add)
-            ts(lo, kf(B1), sc(TP), A.mult, sc(0), A.max)
-            ts(hi, kf(H1), sc(TP), A.max, sc(1), A.min)
+            bounds += [lambda: ts(sc(DD), col("th", 18), col("th", 16), A.subtract, kf(B2), A.mult),
+                       lambda: ts(sc(TP), sc(DD), col("th", 16), A.add),
+                       lambda: (ts(lo, kf(B1), sc(TP), A.mult, sc(0), A.max), ts(hi, kf(H1), sc(TP), A.max, sc(1), A.min))]
         if more:
-            scan(v("t2", 0, C), v("kc", 0, C), v("t1", 0, C), 161.0 / 256, A.mult, A.add)
-            ts(sc(LH), lo, hi, A.add, -1.0, A.add)
-            tt(sc(SZ), hi, lo, A.subtract)
-            ts(sc(VB), lo, -1.0, A.add, kf(B3), A.mult)
-            ts(v("at0", 0, C), v("xb", 0, C), lo, A.is_equal)
-            act(v("a2", 0, C), v("xf", 0, C), AF.Abs, bias=sc(LH), scale=-2.0)
-            act(v("a3", 0, C), row(4), AF.Abs, bias=sc(LH), scale=-2.0)
-            act(sc(NS), sc(SZ), scale=-FAR)
-        if t == 0:
+            bounds += [lambda: (ts(sc(LH), lo, hi, A.add, -1.0, A.add), tt(sc(SZ), hi, lo, A.subtract))]
+        chain = [lambda: cp(v("npo", 0, 16), picks)]
+        if t:
+            chain = [lambda: tt(v("gm", 0, 16 * nk), picks, v("ge", go, go + 16 * nk), A.mult),
+                     lambda: scan(v("hm", 0, 16 * nk), v("ge", 128 + go, 128 + go + 16 * nk), v("gm", 0, 16 * nk), 0.0, A.mult, A.add),
+                     lambda: cp(v("npo", 0, 10), v("hm", E - 1, 10 * E, E))]
+        chain += [lambda: cp(row(t, v("npo", 0, 10)), row(t - 1) if t else v("pl", C, 2 * C)),
+                  lambda: turn("tb2", t),
+                  lambda: cp(v("lro", 0, 16), v("tb2", 0, 2 * TW, ind=wrot))]
+        for k, step_ in enumerate(chain):
+            step_()
+            if k < len(bounds):
+                bounds[k]()
+        x0 = XW * t
+
+        def gather_f(c0, c1, every):
             for b in range(4):
-                qz("eq", "es", 128 * b, 128, v("ea", 3 - b, 515 - b))
-        lo_ = x0 + (8 if first else C)
+                (cp if (b + 1) % every else act)(v("ft", 64 * c0 + b, 64 * c1, 4), v("tp", C * b, C * b + C, ind=v("lro", c0, c1)))
+
+        def scaled(at, k, a, n, every):
+            for b in range(4):
+                o, i = v("ht", 4 * at + b, 4 * (at + n), 4), v("ps", 512 * (k + b) + a, 512 * (k + b) + a + n)
+                ts(o, i, 0.015625, A.mult) if b % every else act(o, i, scale=0.015625)
+
+        def added(at, k, a, n):
+            for b in range(4):
+                tt(v("gt", C * b + at, C * b + at + n), v("ft", 4 * at + b, 4 * (at + n), 4), v("ps", 512 * (k + b) + a, 512 * (k + b) + a + n), A.add)
+
+        gather_f(f0 // 16, f0 // 16 + 8, 2)
+        qz("fq", "fs", x0 + qf, 128, v("ft", 4 * f0, 4 * f0 + 512))
+        for nm, f in (("fq", bytes_), ("fs", lambda x: x)):
+            send("ar%d" % (3 * t + 1), {r: (f(v(nm, x0 + qf + place(d, r) - f0, x0 + qf + place(d, r) - f0 + S)),
+                                            f(v(nm, x0 + lay(r)[1] + S * turn_(r, d), x0 + lay(r)[1] + S * turn_(r, d) + S))) for r in peers})
+        gather_f(*((0, 2) if first else (8, 10)), 1)
+        if more and rot:
+            cp(v("ltr", 0, 16), v("tb2", 0, 2 * TW, ind=wtrue))
+        if more:
+            ts(sc(VB), lo, -1.0, A.add, kf(B3), A.mult)
+            act(v("t1", 0, C), row(t), bias=kf(T1B), scale=kf(T1S))
+            act(v("a2", 0, C), v("xf", 0, C), AF.Abs, bias=sc(LH), scale=-2.0)
+        qz("oq", "osp", 128 * t, 128, v("ft", 128 - 4 * f0, 640 - 4 * f0))
+        for b in range(4):
+            mm(bank(b, 128), "wq", "wsc", 128 * b, "oq", "osp", 128 * t, 128)
+        cp(row(4, lro), v("xr" if rot else "xb", 0, C))
+        if more:
+            act(v("ky", 0, C), v("atn", 0, C, ind=ltr))
+        scaled(3 * S if first else 0, 0, 0 if first else 128 - S, S, 1)
+        if more:
+            act(sc(NS), sc(SZ), scale=-FAR)
+        else:
+            act(v("olf", 0, C), row(t))
+            dma("s", T.ol[:], T.olf[8:128:16, :], [], [v("olf", 0, C)])
+        lo_ = x0 + lay(d)[1]
         arrive("ar%d" % (3 * t + 1), 2, [v("fq", lo_, lo_ + 3 * S), v("fs", lo_, lo_ + 3 * S)])
         for b in range(4):
-            mm(bank(4 + b), "wq", "wsc", 128 * b, "fq", "fs", x0 + mv)
-        for b in range(4):
-            if b % 2:
-                ts(v("ht", b, 640, 4), bank(4 + b), 0.015625, A.mult)
-            else:
-                act(v("ht", b, 640, 4), bank(4 + b), scale=0.015625)
+            mm(bank(4 + b, 128), "wq", "wsc", 128 * b, "fq", "fs", x0 + (8 if first else 120), 128)
+        scaled(0 if first else S, 4, 0 if first else 8, 3 * S, 2)
         qz("hq", "hs", x0 + qh, C, v("ht", 0, 640))
         for nm, f in (("hq", bytes_), ("hs", lambda x: x)):
             send("ar%d" % (3 * t + 2), {r: (f(v(nm, x0 + qh + slot(d, r), x0 + qh + slot(d, r) + S)),
                                             f(v(nm, x0 + lay(r)[3] + place(r, d), x0 + lay(r)[3] + place(r, d) + S))) for r in peers})
+        for b in range(4):
+            mm(bank(4 + b, 128), "eq", "es", 128 * b, "hq", "hs", x0 + (32 if first else 128), 128)
+        turn("tb3", 4)
+        if not more:
+            qz("vq", "vs", 0, 128, v("vt", 0, 512))
+        else:
+            act(v("a3", 0, C), row(4), AF.Abs, bias=sc(LH), scale=-2.0)
+            ts(v("at0", 0, C), v("xb", 0, C), lo, A.is_equal)
+            scan(v("t2", 0, C), v("kc", 0, C), v("t1", 0, C), 161.0 / 256, A.mult, A.add)
         if t == 0:
+            ts(col("wof", 4), kf(PS1), 16.0, A.mult, 25.0, A.add)
             ms(v("ph", 0, C + 2, C + 1), 0.0)
             ms(v("ge", 0, 256), 1.0)
             ts(v("awx", 0, 12), v("awx", 0, 12), kf(R_), A.add)
@@ -522,6 +560,7 @@ def rank_program(g, core, T, topo):
             ts(v("zm", 64, 96), v("zi", 32, 64), kf(N2), A.is_equal, -8.0, A.mult)
             act(kf(CB), kf(B0), bias=2.0 * (TW // 16 - 1) + 2.4375)
             act(kf(CA2), kf(B1), bias=kf(O20), scale=32.0)
+        cp(v("iof", 0, 16), v("tb3", 0, 2 * TW, ind=wcol))
         if more:
             E2, g2 = 4 * nn, 48 * t
             n2 = 12 if t == 0 else 10
@@ -531,35 +570,22 @@ def rank_program(g, core, T, topo):
             act(sc(S2), sc(VB), scale=0.5)
             act(col("dl", do + DW + C + 1), sc(VB), bias=kf(V0), scale=1.0 / 256)
             act(col("rin", 66), kf(PA2), bias=kf(CA1), scale=-2.0 * (TW // 16 - 1))
-            ms(v("rin", 67, 72), 32.0 / E2)
             scan(v("ph", 1, C + 1), v("at0", 0, C), v("t2", 0, C), 0.0, A.add, A.min)
             starts = [col("th", 0)] if t == 0 else [col("th", 16), col("th", 0), col("th", 18)]
-            step = lambda m: v("ge", g2 + 2 * m, g2 + 10 * E2, E2)
             for m, st in enumerate(starts):
                 ts(v("ge", g2 + 2 * m + 2, g2 + n2 * E2, E2), v("awx", 0, n2), st, A.is_ge)
-            tt(v("dl", do + DW, do + DW + C + 1), v("ph", 0, C + 1), v("ph", 1, C + 2), A.subtract)
             act(v("ge", g2 + 1, g2 + n2 * E2, 2), v("ge", g2, g2 + n2 * E2, 2))
             act(v("ge", 128 + g2, 128 + g2 + n2 * E2, 2), v("ge", g2, g2 + n2 * E2, 2), bias=1.0, scale=-1.0)
             if t == 0:
                 act(kf(O21), col("rin", 66), bias=kf(CA2), scale=-8.0)
-                ts(nof, step(1), 4.0, A.mult)
-            else:
-                tt(v("nd", 0, 10), step(1), step(2), A.add)
-            ts(v("mk", 0, C), v("a2", 0, C), sc(SZ), A.is_lt)
-            if t == 1:
-                tt(v("nd", 16, 26), v("nd", 0, 10), step(3), A.add)
-                ts(nof, v("nd", 16, 26), 2.0, A.mult)
+        added(0 if first else 3 * S, 4, 128 - S if first else 0, S)
         lo_ = x0 + (C if first else 8)
         arrive("ar%d" % (3 * t + 2), 2, [v("hq", lo_, lo_ + 3 * S), v("hs", lo_, lo_ + 3 * S)])
         for b in range(4):
-            mm(bank(b), "eq", "es", 128 * b, "hq", "hs", x0 + dm)
+            mm(bank(b, 128), "eq", "es", 128 * b, "hq", "hs", x0 + (C - 8 if first else 8), 128)
+        added(S if first else 0, 0, 8 if first else 0, 3 * S)
         for b in range(4):
-            tt(v("gt", C * b, C * b + C), v("ft", b, 640, 4), bank(b), A.add)
-        for b in range(2):
-            act(v("tt", b, 640, 4), v("gt", C * b, C * b + C, ind=iof))
-        act(v("tt", 2, 384, 4), v("gt", 2 * C, 3 * C, ind=v("iof", 0, 6)))
-        cp(v("tt", 384 + 2, 640, 4), v("gt", 2 * C, 3 * C, ind=v("iof", 6, 10)))
-        cp(v("tt", 3, 640, 4), v("gt", 3 * C, 4 * C, ind=iof))
+            (cp if b % 2 else act)(v("tt", b, 640, 4), v("gt", C * b, C * b + C, ind=iof))
         qz("tq", "tsc", C * (t + 1), C, v("tt", 0, 640))
 
     o = C * R

@@ -2,10 +2,13 @@ from concourse.bass import DstId, RemoteDMATransfer
 from concourse.mybir import dt, AluOpType, AxisListType, ActivationFunctionType
 
 C, R, S, N = 160, 3, 40, 4
+NV = 6
 XW = 288
 TW = 192
-DW = 176
-WHOLE = 1.5 * 2 ** 23
+DW = 312
+WHOLE = 1.5 * 2 ** 20
+MID = 10.0
+OFF = 2.0 ** 15
 BIG = 1e29
 FAR = 2.0 ** 80
 F32, BF, I32, U16, MX, U8 = "float32", "bfloat16", "int32", "uint16", "float8_e4m3fn_x4", "uint8"
@@ -22,18 +25,18 @@ SCRATCH = {
     "upq": _sb(256, MX), "ups": _sb(256, U8), "wq": _sb(512, MX), "wsc": _sb(512, U8),
     "tq": _sb(4 * C, MX), "tsc": _sb(4 * C, U8),
     "fq": _sb(R * XW, MX), "fs": _sb(R * XW, U8), "hq": _sb(R * XW, MX), "hs": _sb(R * XW, U8),
-    "oq": _sb(R * 128, MX), "osp": _sb(R * 128, U8), "ft": _sb(640, BF), "ht": _sb(640, BF), "gt": _sb(640, BF), "tt": _sb(640, BF), "tp": _sb(640, BF),
+    "oq": _sb(R * XW, MX), "osp": _sb(R * XW, U8), "lq": _sb(R * XW, MX), "ls": _sb(R * XW, U8), "ft": _sb(640, BF), "ht": _sb(1024, BF), "gt": _sb(640, BF), "tt": _sb(640, BF), "tp": _sb(640, BF),
     "eq": _sb(512, MX), "es": _sb(512, U8), "ea": _sb(516, BF),
     "kt": _sb(512, BF), "kq": _sb(128, MX), "ks": _sb(128, U8), "ha": _sb(128, BF),
     "ct": _sb(1920, BF), "cq": _sb(480, MX), "cs": _sb(480, U8), "sg": _sb(5 * C, BF),
     "ki": _sb(20, I32), "kf": _sb(48, F32), "uoi": _sb(16, I32), "uof": _sb(16, U16), "xf": _sb(C, F32), "xb": _sb(C, BF),
     "jm": _sb(C, BF), "hj": _sb(128, BF), "pk": _sb(C, BF), "up": _sb(C, BF), "rs": _sb(C, BF),
-    "one": _sb(C, BF), "kc": _sb(2 * C, BF), "xr": _sb(C, BF), "m8": _sb(40, F32), "zi": _sb(64, F32), "zm": _sb(96, F32),
-    "awx": _sb(12, F32), "wof": _sb(6, U16),
-    "pm": _sb(C, F32), "pw": _sb(C, F32), "tie": _sb(C, BF), "so": _sb(10 * C, BF), "ato": _sb(10, U16),
+    "one": _sb(C, BF), "kc": _sb(2 * C, BF), "xr": _sb(C, BF), "m8": _sb(40, F32), "zi": _sb(192, F32), "zm": _sb(66, F32),
+    "awx": _sb(12, F32), "wof": _sb(12, U16), "lto": _sb(16, U16), "kp": _sb(2 * C, BF),
+    "pm": _sb(C, F32), "pw": _sb(C, F32), "tie": _sb(C, BF), "so": _sb(NV * C, BF), "ac": _sb(48, F32), "ato": _sb(10, U16),
     "atn": _sb(C, BF), "l0": _sb(C, BF), "l1": _sb(C, BF), "wn": _sb(2 * C, BF), "pl": _sb(2 * C, BF),
     "lab": _sb(C, BF), "pp": _sb(4, F32), "w": _sb(C, F32), "e": _sb(C, F32), "se": _sb(C + 3, F32), "fin": _sb(C + 3, F32),
-    "dl": _sb(R * DW, F32), "sm": _sb(8, F32), "za": _sb(32, F32), "zat": _sb(32, F32), "zb": _sb(128, F32), "zbt": _sb(144, F32),
+    "dl": _sb(R * DW, F32), "sm": _sb(8, F32), "za": _sb(32, F32), "zat": _sb(32, F32), "zb": _sb(64, F32), "zbt": _sb(144, F32),
     "tab": _sb(16, F32), "rx": _sb(72, F32), "rin": _sb(72, F32), "of": _sb(8, U16),
     "ky": _sb(C, BF), "fl": _sb(C, BF), "b": _sb(C, BF), "y1": _sb(C, BF), "nb": _sb(C, BF), "x1": _sb(C, BF), "yb": _sb(C, BF),
     "lf": _sb(6 * TW + 16, BF),
@@ -44,9 +47,9 @@ SCRATCH = {
     "ph": _sb(C + 2, BF),
     "olf": _sb(C, F32), "yo": _sb(C, F32),
 }
-SEMAPHORES = (["sv", "sa", "sp", "sg", "sent"] + ["ar%d" % k for k in range(3 * R)] + ["d%d" % k for k in range(12)])
+SEMAPHORES = (["sv", "sa", "sp", "sg", "sent"] + ["ar%d" % k for k in range(3 * R)] + ["al%d" % k for k in range(R)] + ["ah%d" % k for k in range(R)] + ["d%d" % k for k in range(12)])
 
-ORDER = ["max sum unit zb6 zbt turn best", "tab fl sum b zb5 y1 zbt cb best turn"]
+ORDER = ["bn mask yx rot sum yb zbt unit zb5 max best turn", "mask fl sum b zbt y1 zb6 cb best turn"]
 A = AluOpType
 AF = ActivationFunctionType
 
@@ -70,6 +73,8 @@ def _meet(a, b):
         return a[1] // 512 == b[1] // 512
     if a[5] <= b[4] or b[5] <= a[4] or a[2] <= b[1] or b[2] <= a[1]:
         return False
+    if a[2] - a[1] == 1 or b[2] - b[1] == 1:
+        return (a[1] - b[1]) % max(a[3], b[3]) == 0 or max(a[3], b[3]) == 1
     return not (a[3] == b[3] and a[3] > 1 and a[1] % a[3] != b[1] % a[3])
 
 
@@ -85,11 +90,10 @@ def deal(topo, cores, r):
         same = [o for o in free if len(free[o]) == width]
         left = [e for e in free[same[0]] if e not in taken]
         k = 1
-        while 2 * k * len(same) <= len(left) and (not taken or 2 * k <= len(out[min(out)])):
+        while 2 * k * len(same) <= len(left):
             k *= 2
-        part = len(left) // len(same)
         for n_, o in enumerate(same):
-            out[o] = left[n_ * part:(n_ + 1) * part:part // k]
+            out[o] = left[n_::len(same)][:k]
             taken += out[o]
     return out
 
@@ -178,19 +182,28 @@ def rank_program(g, core, T, topo):
     coming = sum(len(deal(topo, T.cores, r)[d]) for r in peers)
     sent = [0]
 
-    def send(sem, pairs):
-        def fn(e):
-            tr_ = []
-            for r in peers:
-                rid, pid, _se = topo.addr(T.cores[r])
-                tr_.append(RemoteDMATransfer(dst_ids=[DstId(rid=rid, pnc=pid)], dma_engine_mask=sum(1 << k for k in eng_of[r]),
-                                             remote_sem=T.sem[sem], src=ap(pairs[r][0]), dst=ap(pairs[r][1])))
-            return e.remote_dma_fused(tr_, local_sem=T.sem.sent)
-        op("g", fn, [], [pairs[r][0] for r in peers], remote=True)
-        sent[0] += sum(len(eng_of[r]) for r in peers)
+    far = [r for r in peers if topo.chip(T.cores[r]) != topo.chip(core)]
+    near = [r for r in peers if r not in far]
 
-    def arrive(sem, calls, outs):
-        ops.append(dict(eng=None, wr=outs, rd=[], arr=(sem, calls * coming)))
+    early, late = sorted(far, key=lambda r: topo.die(T.cores[r]) != topo.die(core))
+    wide = {r: sorted(k for o in (far if r in far else near) for k in eng_of[o]) for r in peers}
+
+    def send_codes(sem, r, here, there):
+        for k, f in ((0, bytes_), (1, lambda x: x)):
+            send(sem, r, f(v(here[k], here[2], here[2] + S)), f(v(there[k], there[2], there[2] + S)), wide[r])
+
+    def send(sem, r, here, there, engines):
+        to = list(zip(r, there)) if isinstance(r, list) else [(r, there)]
+
+        def fn(e):
+            ids = [DstId(rid=topo.addr(T.cores[o])[0], pnc=topo.addr(T.cores[o])[1]) for o, _ in to]
+            return e.remote_dma_fused([RemoteDMATransfer(dst_ids=ids, dma_engine_mask=sum(1 << k for k in engines), remote_sem=T.sem[sem],
+                                                         srcs=[ap(here)], dsts=[ap(x) for _, x in to])], local_sem=T.sem.sent)
+        op("g", fn, [], [here], remote=True)
+        sent[0] += len(engines)
+
+    def arrive(sem, n, outs):
+        ops.append(dict(eng=None, wr=outs, rd=[], arr=(sem, n)))
 
     def bytes_(x):
         return x[:7] + (dt.uint8,)
@@ -201,36 +214,34 @@ def rank_program(g, core, T, topo):
     rot, first = plan(d)
 
     def lay(r):
-        return (128, 8, 0, 120) if plan(r)[1] else (0, 128, 128, 8)
+        return (16, 88) if plan(r)[1] else (128, 8)
 
     def turn_(r, o):
         return [x for x in range(N) if x != r].index(o)
 
-    def slot(r, o):
-        return S * turn_(r, o) + (0 if plan(r)[1] else S)
-
     def place(r, o):
         return (S * o - plan(r)[0]) % C
+
+    assert sorted(place(d, o) for o in (early, near[0])) == [S, 2 * S]
 
     def row(k, ind=None):
         return v("lf", TW * k + 16, TW * k + 16 + C, ind=ind)
 
     dma("s", T.ut[:], T.u[:], [v("ut", 0, 512)], [])
-    dma("a", T.xt[:], T.x[:], [v("xt", 0, 640)], [])
+    dma("s", T.xt[:], T.x[:], [v("xt", 0, 640)], [])
     dma("s", T.wq[:].bitcast(dt.uint8), T.wc[:], [v("wq", 0, 512)], [v("xt", 0, 640)])
     dma("s", T.wsc[:], T.ws[:], [v("wsc", 0, 512)], [])
-    dma("s", T.vt[:], T.v[:], [v("vt", 0, 512)], [])
     iota(col("ki", 9), [[0, 1]], 0, 1)
     iota(v("uoi", 0, 8), [[16, 8]])
     iota(v("jm", 0, C), [[0, 10], [1, 16]])
-    iota(v("m8", 0, 8), [[0, 4], [1, 2]])
+    iota(v("m8", 0, 8), [[1, 2], [0, 4]])
     iota(v("m8", 8, 16), [[0, 2], [1, 2], [0, 2]])
     for q in range(4):
         for x in range(2):
-            iota(v("hj", 32 * q + x, 32 * q + 32, 2), [[0, 4], [1, 2], [-4 if q & 2 else 4, 2]], 2 * (q ^ x))
+            iota(v("hj", 32 * q + x, 32 * q + 32, 2), [[1, 2], [0, 4], [-4 if q & 2 else 4, 2]], 2 * (q ^ x))
     iota(v("xf", 0, C), [[1, C]])
-    iota(v("zi", 0, 32), [[0, 8], [1, 2], [0, 2]])
-    iota(v("zi", 32, 64), [[0, 4], [1, 4], [0, 2]])
+    for t, pat in enumerate(([[0, 8], [1, 2], [0, 4]], [[0, 16], [1, 2], [0, 2]], [[0, 16], [1, 4]])):
+        iota(v("zi", 64 * t, 64 * t + 64), pat)
     iota(v("awx", 0, 12), [[16, 12]])
     iota(v("ea", 0, 516), [[0, 516]], 1)
     op("g", lambda e: e.affine_select(ap(v("ea", 0, 516)), ap(v("ea", 0, 516)), [[1, 516]], A.is_equal, 0.0, -3, -4),
@@ -238,11 +249,14 @@ def rank_program(g, core, T, topo):
     unit = lambda b: qz("eq", "es", 128 * b, 128, v("ea", 3 - b, 515 - b))
     R_, G_, B0, B1, B2, B3, GA, N2, K1 = range(9)
     (NB3, NGA, SIG, KB, C0, W16, T1S, T1B, TI0, H1, V0, PA1, PA2, CA1, CA2, CB, COL1, COL2, O20, O21, KK, PB, PS0, PS1, PS2, NB2, NN2, Z0, NB0,
-     WB, NG) = range(9, 40)
+     WB, NG, LA, LB, G16, GC, WO) = range(9, 45)
     kf = lambda k: col("kf", k)
     p_ = col("ki", 9)
     ms(v("uoi", 8, 16), 8)
     ms(v("ct", 1280 + 3, 1920, 4), 0.0)
+    ms(col("ac", 3 * (10 - NV) - 1), 0.0)
+    for k in range(3):
+        ms(v("ac", 16 + k, 28, 3), float(k > 0))
     ts(col("ki", R_), p_, 15, A.bitwise_and)
     ts(col("ki", G_), p_, 4, A.arith_shift_right)
     for k, (sh, m) in enumerate(((0, 1), (1, 1), (2, 1), (3, 1), (4, 1), (1, 3), (2, 3))):
@@ -260,19 +274,21 @@ def rank_program(g, core, T, topo):
     act(v("kc", 0, C), v("jm", 0, C), bias=kf(B3), scale=0.0)
     act(kf(W16), kf(B3), bias=float(C), scale=-float(C))
     act(kf(NN2), kf(B3), bias=-1.0)
+    act(kf(PA1), kf(B3), bias=-2.0)
     for k in range(7):
         act(v("lf", max(0, TW * k - 16), TW * k + 16), v("one", 0, 32 if k else 16), scale=0.0)
+    act(v("m8", 24, 32), v("m8", 8, 16), bias=kf(NB3), scale=kf(PA1))
+    act(kf(WO), kf(GA), bias=40.0, scale=-32.0)
+
     act(v("ha", 0, 128), v("hj", 0, 128), AF.Abs, bias=kf(NG))
-    ts(kf(PA1), kf(B3), -2.0, A.add)
-    ts(v("m8", 16, 24), v("m8", 0, 8), kf(GA), A.is_equal, 256.0, A.mult)
-    ts(v("m8", 24, 32), v("m8", 8, 16), kf(PA1), A.mult, kf(NB3), A.add)
-    ts(kf(KK), kf(R_), 9.0, A.min)
-    ts(kf(PB), kf(R_), 10.0, A.is_ge, kf(B0), A.max)
 
     qz("uq", "us", 0, 128, v("ut", 0, 512))
-    qz("tq", "tsc", 0, C, v("xt", 0, 640))
+    ts(v("m8", 16, 24), v("m8", 0, 8), kf(GA), A.is_equal, 256.0, A.mult)
+    ts(kf(KK), kf(R_), 9.0, A.min)
+    ts(kf(PB), kf(R_), 10.0, A.is_ge, kf(B0), A.max)
     cp(words(v("upq", 0, 128)), words(v("uq", 0, 128), v("uof", 0, 8)))
     act(v("ups", 0, 128), v("us", 0, 128, ind=v("uof", 0, 8)))
+    qz("tq", "tsc", 0, C, v("xt", 0, 640))
     mm(bank(0), "upq", "ups", 0, "tq", "tsc", 0)
     mm(bank(3), "upq", "ups", 0, "tq", "tsc", 0)
     cp(words(v("upq", 128, 256)), words(v("uq", 0, 128), v("uof", 8, 16)))
@@ -289,56 +305,66 @@ def rank_program(g, core, T, topo):
     act(v("l0", 0, C), bank(4), AF.Sign)
     scan(v("pw", 0, C), v("up", 0, C), v("pm", 0, C), 0.0, A.add, A.min)
     qz("kq", "ks", 0, 128, v("kt", 0, 512))
-    NV = 6
+    na = 3 * (10 - NV)
     cmp_ = lambda c, a=0, b=C: v("ct", 640 * (c // 4) + c % 4 + 4 * a, 640 * (c // 4) + c % 4 + 4 * b - 3, 4)
     count_ = lambda c: scan(v("so", C * c, C * c + C), v("one", 0, C), cmp_(c), col("tie", 16 * c + 15), A.mult, A.add)
+    act(v("l1", 0, C), v("l0", 0, C), AF.Relu, acc=col("pp", 1))
     for c in range(NV, 10):
         act(v("sg", C * (c - NV), C * (c - NV + 1)), bank(3), AF.Sign, bias=col("pw", 16 * c + 15), scale=-1.0)
-        if c == NV:
-            act(v("l1", 0, C), v("l0", 0, C), AF.Relu, acc=col("pp", 1))
-        if c == NV + 1:
-            act(col("pp", 3), col("pp", 1), bias=kf(B3), scale=kf(NN2))
-        if c == 9:
-            act(v("wn", 0, C), v("l1", 0, C), bias=col("pp", 3), scale=kf(W16))
     for c in range(NV, 10):
         k, so = 16 * c + 16, C * (c - NV)
-        act(cmp_(c, 0, k), v("sg", so, so + k), AF.Relu, scale=-1.0)
+        act(cmp_(c, 0, k), v("sg", so, so + k), AF.Relu, scale=-1.0, acc=col("ac", 3 * (c - NV) + 1))
         if k < C:
-            act(cmp_(c, k, C), v("sg", so + k, so + C), AF.Sign, bias=1.0, scale=-1.0)
+            act(cmp_(c, k, C), v("sg", so + k, so + C), AF.Sign, bias=1.0, scale=-1.0, acc=col("ac", 3 * (c - NV) + 2))
+        if c == 8:
+            act(col("pp", 3), col("pp", 1), bias=kf(B3), scale=kf(NN2))
+    act(v("wn", 0, C), v("l1", 0, C), bias=col("pp", 3), scale=kf(W16))
     tt(cmp_(10), bank(0), v("pw", 0, C), A.is_equal)
     for c in range(NV):
         k = 16 * c + 16
         ts(cmp_(c, 0, k), bank(0, k), col("pw", k - 1), A.is_gt)
         ts(cmp_(c, k, C), v("ps", k, C), col("pw", k - 1), A.is_ge)
-        if c == 0:
+        if c == 1:
             scan(v("tie", 0, C), v("rs", 0, C), cmp_(10), 0.0, A.mult, A.add)
-    for c in range(10):
+    cp(v("ac", 0, na, 3), v("tie", 16 * NV + 15, C, 16))
+    for c in range(NV):
         count_(c)
-        if c == NV - 1:
-            scan(v("wn", C, 2 * C), v("kc", 0, C), v("wn", 0, C), -1.0, A.mult, A.add)
     qz("cq", "cs", 0, C, v("ct", 0, 640))
+    scan(v("ac", 32, 32 + na), v("ac", 16, 16 + na), v("ac", 0, na), 0.0, A.mult, A.add)
     ts(col("wof", 0), kf(PS1), 16.0, A.mult, 24.0, A.add)
-    ts(v("ato", 0, 10), v("so", C - 1, 10 * C, C), -1.0, A.mult, float(C), A.add)
+    ts(v("ato", 0, NV), v("so", C - 1, NV * C, C), -1.0, A.mult, float(C), A.add)
+    scan(v("wn", C, 2 * C), v("kc", 0, C), v("wn", 0, C), -1.0, A.mult, A.add)
+    ts(v("ato", NV, 10), v("ac", 34, 32 + na, 3), -1.0, A.mult, float(C), A.add)
     ato = v("ato", 0, 10)
     qz("cq", "cs", C, C, v("ct", 640, 1280))
     cp(row(5, ato), v("wn", C, 2 * C))
     qz("cq", "cs", 2 * C, C, v("ct", 1280, 1920))
+    ts(col("wof", 6), kf(PS1), 16.0, A.mult, kf(WO), A.add)
     for s in range(3):
         mm(bank(2), "kq", "ks", 0, "cq", "cs", C * s, start=s == 0, stop=s == 2)
     act(v("kc", C, 2 * C), v("one", 0, C), scale=kf(NB3))
+    dma("a", T.vt[:], T.v[:], [v("vt", 0, 512)], [])
     act(kf(SIG), kf(B3), bias=-1.0, scale=2.0)
     act(kf(KB), kf(B3), bias=162.0, scale=-323.0)
-    act(kf(TI0), kf(GA), bias=-1.0, scale=0.0625)
-    act(kf(Z0), kf(B3), bias=-8.0, scale=8.0)
-    act(kf(O20), kf(GA), bias=11.5, scale=16.0)
+    act(kf(TI0), kf(GA), bias=-MID / 256, scale=0.0625)
+    act(v("zm", 0, 66, 65), v("one", 0, 2), scale=OFF)
+    act(v("zm", 1, 65), v("zi", 0, 64), bias=OFF, scale=-OFF)
+    act(kf(LB), kf(B2), AF.Abs, bias=kf(NGA))
+    act(kf(GC), kf(GA), bias=-(24 + MID) / 256, scale=12.0 / 256)
+    act(kf(G16), kf(GA), scale=16.0)
     act(v("dl", 0, C), v("one", 0, C), scale=1.0 / 256)
     act(col("dl", C), col("one", 0), scale=1.0 / 256)
     act(col("dl", C + 1), col("one", 0), scale=0.0)
     act(col("se", C), col("one", 0), scale=0.0)
     act(v("se", C + 1, C + 3), v("one", 0, 2), scale=-BIG)
-    act(col("dl", C + 3), kf(G_), bias=kf(TI0), scale=0.125)
-    act(v("zm", 0, 32), v("one", 0, 32), scale=kf(Z0))
-    act(v("tp", 0, C), v("xt", 0, 640, 4))
+    act(col("dl", C + 6), kf(G_), bias=kf(TI0), scale=0.125)
+    act(v("dl", C + 22, DW - 4, 4), v("one", 0, 32), scale=0.0)
+    act(kf(LA), kf(LB), bias=1.0, scale=-1.0)
+    act(kf(C0), kf(KB), scale=kf(LB))
+    act(kf(COL1), kf(SIG), scale=kf(LB))
+    act(col("rin", 65), col("one", 0), scale=WHOLE)
+    act(col("rin", 66), col("one", 0), scale=-WHOLE)
+    act(v("zbt", 128, 144), v("one", 0, 16), scale=BIG)
     act(v("pl", 0, C), row(5), bias=kf(NB3), scale=kf(B3))
 
     def spread(put, on_vector):
@@ -351,7 +377,13 @@ def rank_program(g, core, T, topo):
         tr(v(tb, 0, TW), v("lf", TW * k, TW * k + TW))
         tr(v(tb, TW, 2 * TW), v("lf", TW * k + 16, TW * k + 16 + TW))
 
-    qf, qh, f0 = lay(d)[0], lay(d)[2], 32 if first else 0
+    def keys(own):
+        act(v("kp", 0, C), v("atn", 0, C, ind=own), scale=kf(LA))
+
+    def keys_add():
+        tt(v("ky", 0, C), v("kp", C, 2 * C, ind=v("lto", 0, 10)), v("kp", 0, C), A.add)
+
+    f0 = 32 if first else 0
     wtrue, wrot, wcol = col("wof", 0), col("wof", 2 if rot else 0), col("wof", 4)
     ltr, lro, iof, nof = v("ltr" if rot else "lro", 0, 10), v("lro", 0, 10), v("iof", 0, 10), v("nof", 0, 10)
     SZ, VO, S2, NS, LH, TP, VB, DD, HX = range(4, 13)
@@ -369,49 +401,53 @@ def rank_program(g, core, T, topo):
             step = lambda m: v("ge", go + 2 * m, go + 10 * E, E)
             tt(v("dl", DW * t, DW * t + C + 1), v("ph", 0, C + 1), v("ph", 1, C + 2), A.subtract)
             ts(v("mk", 0, C), v("a2", 0, C), sc(SZ), A.is_lt)
-            ms(v("rin", 67, 72), 32.0 / E)
+            ms(v("rin", 68, 72), -1.0 / E)
             tt(v("lab", 0, C), bank(4), v("thr", 0, C), A.is_gt)
-            ts(nof, step(1), 4.0, A.mult) if t == 1 else tt(v("nd", 0, 10), step(1), step(2), A.add)
-            red(col("pp", 0), v("lab", 0, C), A.add, True)
+            ts(nof, step(1), 4.0, A.mult, kf(G16), A.add) if t == 1 else tt(v("nd", 0, 10), step(1), step(2), A.add)
+            scan(v("l1", 0, C), v("one", 0, C), v("lab", 0, C), 0.0, A.mult, A.subtract)
             if t == 2:
                 tt(v("nd", 16, 26), v("nd", 0, 10), step(3), A.add)
-            ts(v("w", 0, 96), v("lab", 0, C, ind=v(ltr[0], 0, 6)), sc(SZ), A.mult, col("pp", 0), A.add)
-            act(v("w", 96, C), v("lab", 0, C, ind=v(ltr[0], 6, 10)), bias=col("pp", 0), scale=sc(SZ))
+            ts(v("w", 0, 96), v("lab", 0, C, ind=v(ltr[0], 0, 6)), col("nd", 30), A.mult, col("l1", C - 1), A.add)
+            act(v("w", 96, C), v("lab", 0, C, ind=v(ltr[0], 6, 10)), bias=col("l1", C - 1), scale=sc(SZ))
             if t == 2:
-                ts(nof, v("nd", 16, 26), 2.0, A.mult)
+                ts(nof, v("nd", 16, 26), 2.0, A.mult, kf(G16), A.add)
             scan(v("e", 0, C), v("w", 0, C), v("mk", 0, C), 0.0, A.add, A.mult)
         else:
-            scan(v("e", 0, C), v("one", 0, C), row(5), 0.0, A.mult, A.add)
+            scan(v("e", 0, C), v("kc", C, 2 * C), row(5), 0.0, A.mult, A.add)
             turn("tb2", 5)
         do = DW * t
         gain = col("dl", do + C + 2)
         red(gain, v("e", 0, C), A.max, True)
-        send("ar%d" % (3 * t), {r: (gain, col("dl", do + C + 4 + [x for x in range(N) if x != r].index(d))) for r in peers})
+        for to in (far, near):
+            send("ar%d" % (3 * t), to, gain, [col("dl", do + C + 10 + 4 * turn_(r, d)) for r in to], wide[to[0]])
         act(v("se", 0, C), v("e", 0, C), AF.Abs)
         if t == 0:
             cp(v("ltr", 0, 16), v("tb2", 0, 2 * TW, ind=wtrue))
-            unit(0)
+            cp(v("lto", 0, 16), v("tb2", 0, 2 * TW, ind=col("wof", 6)))
             act(v("atn", 0, C), bank(2), bias=kf(KB), scale=kf(SIG))
+            act(v("kp", C, 2 * C), bank(2), bias=kf(C0), scale=kf(COL1))
         scan(v("fin", 0, C + 3), v("dl", do, do + C + 3), v("se", 0, C + 3), 0.0 if t else -1.0 / 256, A.add, A.max)
         if t == 0:
             scan(v("pl", C, 2 * C), v("kc", C, 2 * C), v("pl", 0, C), -1.0, A.mult, A.add)
-            act(v("ky", 0, C), v("atn", 0, C, ind=v("ltr", 0, 10)))
+            ts(col("rin", 67), kf(PS1), -0.0625, A.mult, kf(GC), A.add)
+            ts(kf(PB), kf(PS0), 1.0 - TW // 16, A.mult, kf(PS2), A.add)
+            keys(v("ltr", 0, 10))
 
         def put_cut(vec, x, to, fro, t=t):
             o, m, s = v("za", x, 32, 4, *to), v("m8", 32, 40, 1, *fro), col("fin", C + 2, *fro)
             if t == 0:
                 ts(o, m, s, A.mult) if vec else act(o, m, scale=s)
             elif vec:
-                ts(o, m, s, A.mult, col("sc", S2, *fro), A.add)
+                ts(o, m, s, A.mult, col("sc", VB, *fro), A.add)
             else:
-                act(o, m, bias=col("sc", S2, *fro), scale=s)
-        spread(put_cut, 6 if t else 9)
+                act(o, m, bias=col("sc", VB, *fro), scale=s)
+        spread(put_cut, 6)
         if t == 0:
-            unit(1)
+            keys_add()
         tr(v("zat", 0, 32), v("za", 0, 32))
         if t == 0:
-            unit(2)
-            for b in range(1, 4):
+            unit(0)
+            for b in range(4):
                 act(v("tp", C * b, C * b + C), v("xt", b, 640, 4))
             act(v("xb", 0, C), v("xf", 0, C))
             act(kf(NB0), kf(B0), bias=float(rot), scale=-float(rot))
@@ -423,51 +459,57 @@ def rank_program(g, core, T, topo):
             if rot:
                 act(v("xr", 0, C - rot), v("xf", 0, C - rot), bias=kf(NB0))
                 act(v("xr", C - rot, C), v("xf", C - rot, C), bias=kf(WB))
-            ts(v("b", 0, C), v("ky", 0, C), col("zat", 0), A.subtract, col("zat", 16), A.is_gt)
-            ts(col("tab", 8), col("zat", 0), col("zat", 16), A.add, float(C), A.add)
-            ts(v("nb", 0, C), v("ky", 0, C), col("zat", 0), A.subtract, col("zat", 16), A.is_le)
-            ms(v("rin", 0, 64), 0.0)
-            ms(col("rin", 64), WHOLE)
-            scan(v("y1", 0, C), v("one", 0, C), v("b", 0, C), col("tab", 8), A.mult, A.add)
-            scan(v("x1", 0, C), v("one", 0, C), v("nb", 0, C), -1.0, A.mult, A.add)
-            ms(col("rin", 65), -WHOLE)
-            ts(kf(PB), kf(PS0), 1.0 - TW // 16, A.mult, kf(PS2), A.add)
-            ms(v("zbt", 128, 144), 0.0)
-            scan(v("yb", 0, C), v("y1", 0, C), v("b", 0, C), 0.0, A.max, A.mult)
-            ts(col("rin", 66), kf(PS1), 2.0, A.mult, 3.4375, A.add)
-            if rot:
-                ts(col("wof", 2), kf(PB), 16.0, A.mult, 24.0, A.add)
-            act(kf(O21), col("rin", 66), bias=kf(O20), scale=-8.0)
+            act(kf(O21), col("rin", 67), bias=8.0 + MID, scale=256.0)
         more = t < R - 1
         lo, hi = sc(2 * t), sc(2 * t + 1)
-        arrive("ar%d" % (3 * t), 1, [v("dl", do + C + 4, do + C + 7)])
+        arrive("ar%d" % (3 * t), sum(len(wide[r]) for r in peers), [v("dl", do + C + 10, do + C + 19)])
 
         def put_sum(vec, x, to, fro, t=t):
-            o, m, s = v("zb", 32 * x, 32 * x + 32, 1, *to), v("zm", 32 * t, 32 * t + 32, 1, *fro), col("sm", 2, *fro)
-            ts(o, m, s, A.mult, 0.4375 - x / 8.0, A.add) if vec else act(o, m, bias=0.4375 - x / 8.0, scale=s)
+            o, i = v("zbt", 32 * x, 32 * x + 32, 1, *to), v("zbt", 0, 32, 1, *fro)
+            if x:
+                ts(o, i, x / 256.0, A.add) if vec else act(o, i, bias=x / 256.0)
         steps = {
-            "tab": lambda: tt(v("tab", 0, 16), v("zat", 0, 16), v("zat", 16, 32), A.add),
-            "fl": lambda: act(v("fl", 0, C), v("tab", 8, 16, ind=nof)),
-            "b": lambda: tt(v("b", 0, C), v("tab", 0, 8, ind=nof), v("ky", 0, C), A.is_lt),
+            "fl": lambda: act(v("fl", 0, C), v("zat", 8, 32, ind=nof)),
+            "b": lambda: tt(v("b", 0, C), v("zat", 0, 32, ind=nof), v("ky", 0, C), A.is_lt),
+            "bn": lambda: (ts(v("b", 0, C), v("ky", 0, C), col("zat", 0), A.subtract, col("zat", 16), A.is_gt),
+                           ts(col("tab", 8), col("zat", 0), col("zat", 16), A.add, float(C), A.add),
+                           ts(v("nb", 0, C), v("ky", 0, C), col("zat", 0), A.subtract, col("zat", 16), A.is_le)),
+            "yx": lambda: (scan(v("y1", 0, C), v("one", 0, C), v("b", 0, C), col("tab", 8), A.mult, A.add),
+                           scan(v("x1", 0, C), v("one", 0, C), v("nb", 0, C), -1.0, A.mult, A.add)),
+            "yb": lambda: scan(v("yb", 0, C), v("y1", 0, C), v("b", 0, C), 0.0, A.max, A.mult),
+            "rot": lambda: ts(col("wof", 2), kf(PB), 16.0, A.mult, 24.0, A.add),
             "y1": lambda: scan(v("y1", 0, C), v("fl", 0, C), v("b", 0, C), -1.0, A.max, A.add),
             "cb": lambda: scan(row(3), v("y1", 0, C), v("b", 0, C), 0.0, A.max, A.mult),
             "max": lambda: tt(row(3), v("x1", 0, C), v("yb", 0, C), A.max),
             "turn": lambda: turn("tb1", 3),
             "unit": lambda: unit(3),
-            "sum": lambda: red(col("sm", 2), v("dl", do + C + 2, do + C + 7), A.add),
+            "sum": lambda: scan(v("zb", 27, 64), v("one", 0, 37), v("dl", do + C + 2, do + DW - 4, 4), 0.0, A.mult, A.add),
+            "mask": lambda: tt(v("rin", 0, 65), v("zm", 1, 66), v("zm", 0, 65), A.subtract),
             "zb5": lambda: spread(put_sum, 5), "zb6": lambda: spread(put_sum, 6), "zb4": lambda: spread(put_sum, 4), "zb7": lambda: spread(put_sum, 7),
-            "zbt": lambda: tr(v("zbt", 0, 128), v("zb", 0, 128)),
-            "best": lambda: (red(col("sm", 3), v("zbt", 0, 128, 2), A.max),
-                             scan(v("rx", 0, 66 + nk), v("zbt", 0, 132 + 2 * nk, 2), v("rin", 0, 66 + nk), 0.0, A.max, A.add)),
+            "zbt": lambda: tr(v("zbt", 0, 32), v("zb", 32, 64)),
+            "best": lambda: scan(v("rx", 0, 67 + nk), v("rin", 0, 67 + nk), v("zbt", 0, 134 + 2 * nk, 2), 2.0, A.add, A.min),
         }
         for name in ORDER[min(t, 1)].split():
             steps[name]()
-        if more:
-            for m in range(nn):
-                act(v("cu", 32 * m, 32 * m + 32), v("one", 0, 32), bias=1.0, scale=col("tab", 8 + 4 * m))
-        ts(v("of", 0, nk), v("rx", 66, 66 + nk), col("sm", 3), A.subtract, 8.0, A.mult)
+        if t == 0:
+            act(v("cu", 0, 32), v("one", 0, 32), bias=1.0, scale=col("tab", 8))
+            act(v("ph", 0, C + 2, C + 1), v("one", 0, 2), scale=0.0)
+            act(v("awx", 0, 12), v("awx", 0, 12), bias=kf(R_))
+            act(kf(CB), kf(B0), bias=kf(GC), scale=-8.0 / 256)
+            act(kf(CA2), kf(B1), bias=8.0 + MID, scale=32.0)
+            act(v("dl", DW + C + 6, R * DW, DW), v("one", 0, 2), scale=col("dl", C + 6))
+            for k in (1, 2):
+                act(v("dl", DW * k + C + 22, DW * k + DW - 4, 4), v("one", 0, 32), scale=0.0)
+                act(v("ge", 128 * k - 128, 128 * k), v("one", 0, 128))
+            act(v("ht", 512 + 4 * S, 1024), v("xt", 0, 512 - 4 * S), scale=0.0)
+            act(v("ht", 0 if first else 480, 32 if first else 512), v("one", 0, 32), scale=0.0)
+        if t == 1:
+            act(v("cu", 0, 64), v("zat", 8, 32, ind=v("wof", 8, 12)), bias=1.0)
+        ts(v("of", 0, nk), v("rx", 67, 67 + nk), col("rx", 64), A.subtract, -256.0, A.mult)
         if more:
             tr(v("cut", 0, 32 * nn), v("cu", 0, 32 * nn))
+        if t == 0:
+            unit(2)
         picks = v("tb1", 0, 2 * TW, ind=v("of", 0, nk))
         bounds = []
         if more:
@@ -509,67 +551,66 @@ def rank_program(g, core, T, topo):
                 tt(v("gt", C * b + at, C * b + at + n), v("ft", 4 * at + b, 4 * (at + n), 4), v("ps", 512 * (k + b) + a, 512 * (k + b) + a + n), A.add)
 
         gather_f(f0 // 16, f0 // 16 + 8, 2)
-        qz("fq", "fs", x0 + qf, 128, v("ft", 4 * f0, 4 * f0 + 512))
-        for nm, f in (("fq", bytes_), ("fs", lambda x: x)):
-            send("ar%d" % (3 * t + 1), {r: (f(v(nm, x0 + qf + place(d, r) - f0, x0 + qf + place(d, r) - f0 + S)),
-                                            f(v(nm, x0 + lay(r)[1] + S * turn_(r, d), x0 + lay(r)[1] + S * turn_(r, d) + S))) for r in peers})
+        qz("fq", "fs", x0 + 48, 128, v("ft", 4 * f0, 4 * f0 + 512))
+        mine = lambda r: ("fq", "fs", x0 + 48 + place(d, r) - f0)
+        send_codes("ar%d" % (3 * t + 1), early, mine(early), ("oq", "osp", x0 + lay(early)[0] + S))
+        send_codes("ar%d" % (3 * t + 1), near[0], mine(near[0]), ("oq", "osp", x0 + lay(near[0])[0]))
+        send_codes("al%d" % t, late, mine(late), ("fq", "fs", x0 + 8))
         gather_f(*((0, 2) if first else (8, 10)), 1)
         if more and rot:
             cp(v("ltr", 0, 16), v("tb2", 0, 2 * TW, ind=wtrue))
         if more:
+            cp(v("lto", 0, 16), v("tb2", 0, 2 * TW, ind=col("wof", 6)))
             ts(sc(VB), lo, -1.0, A.add, kf(B3), A.mult)
             act(v("t1", 0, C), row(t), bias=kf(T1B), scale=kf(T1S))
             act(v("a2", 0, C), v("xf", 0, C), AF.Abs, bias=sc(LH), scale=-2.0)
-        qz("oq", "osp", 128 * t, 128, v("ft", 128 - 4 * f0, 640 - 4 * f0))
-        for b in range(4):
-            mm(bank(b, 128), "wq", "wsc", 128 * b, "oq", "osp", 128 * t, 128)
+        qz("oq", "osp", x0 + (96 if first else 0), 128, v("ft", 128 - 4 * f0, 640 - 4 * f0))
         cp(row(4, lro), v("xr" if rot else "xb", 0, C))
-        if more:
-            act(v("ky", 0, C), v("atn", 0, C, ind=ltr))
-        scaled(3 * S if first else 0, 0, 0 if first else 128 - S, S, 1)
+        if t == 0:
+            ts(col("wof", 4), kf(PS1), 16.0, A.mult, 25.0, A.add)
+            ts(v("wof", 8, 12), v("m8", 8, 12), 4.0, A.mult, kf(G16), A.add)
         if more:
             act(sc(NS), sc(SZ), scale=-FAR)
+            act(col("nd", 30), sc(SZ))
         else:
             act(v("olf", 0, C), row(t))
             dma("s", T.ol[:], T.olf[8:128:16, :], [], [v("olf", 0, C)])
-        lo_ = x0 + lay(d)[1]
-        arrive("ar%d" % (3 * t + 1), 2, [v("fq", lo_, lo_ + 3 * S), v("fs", lo_, lo_ + 3 * S)])
+        lo_, qh, h0 = x0 + lay(d)[0], x0 + (0 if first else 128), 8 if first else S
+        arrive("ar%d" % (3 * t + 1), 2 * (len(wide[early]) + len(wide[near[0]])), [v("oq", lo_, lo_ + 2 * S), v("osp", lo_, lo_ + 2 * S)])
+        arrive("al%d" % t, 2 * len(wide[late]), [v("fq", x0 + 8, x0 + 48), v("fs", x0 + 8, x0 + 48)])
         for b in range(4):
-            mm(bank(4 + b, 128), "wq", "wsc", 128 * b, "fq", "fs", x0 + (8 if first else 120), 128)
-        scaled(0 if first else S, 4, 0 if first else 8, 3 * S, 2)
-        qz("hq", "hs", x0 + qh, C, v("ht", 0, 640))
-        for nm, f in (("hq", bytes_), ("hs", lambda x: x)):
-            send("ar%d" % (3 * t + 2), {r: (f(v(nm, x0 + qh + slot(d, r), x0 + qh + slot(d, r) + S)),
-                                            f(v(nm, x0 + lay(r)[3] + place(r, d), x0 + lay(r)[3] + place(r, d) + S))) for r in peers})
+            mm(bank(b, 128), "wq", "wsc", 128 * b, "oq", "osp", x0 + (16 if first else 80), 128)
         for b in range(4):
-            mm(bank(4 + b, 128), "eq", "es", 128 * b, "hq", "hs", x0 + (32 if first else 128), 128)
+            mm(bank(4 + b, 128), "wq", "wsc", 128 * b, "fq", "fs", x0 + 8, 128)
+        scaled(8 if first else 0, 0, 0 if first else 8, 3 * S, 2)
+        scaled(128, 4, 0, S, 1)
+        home = lambda r: ("hq", "hs", x0 + lay(r)[1] + place(r, d))
+        qz("hq", "hs", qh, 128, v("ht", 0, 512))
+        send_codes("ar%d" % (3 * t + 2), near[0], ("hq", "hs", qh + h0), home(near[0]))
+        send_codes("ar%d" % (3 * t + 2), early, ("hq", "hs", qh + h0 + S), home(early))
+        qz("lq", "ls", x0 + 48, 128, v("ht", 512, 1024))
+        send_codes("ah%d" % t, late, ("lq", "ls", x0 + 48), ("lq", "ls", x0 + 8))
         turn("tb3", 4)
+        if t == 0:
+            unit(1)
         if not more:
             qz("vq", "vs", 0, 128, v("vt", 0, 512))
         else:
+            keys(ltr)
             act(v("a3", 0, C), row(4), AF.Abs, bias=sc(LH), scale=-2.0)
             ts(v("at0", 0, C), v("xb", 0, C), lo, A.is_equal)
             scan(v("t2", 0, C), v("kc", 0, C), v("t1", 0, C), 161.0 / 256, A.mult, A.add)
-        if t == 0:
-            ts(col("wof", 4), kf(PS1), 16.0, A.mult, 25.0, A.add)
-            ms(v("ph", 0, C + 2, C + 1), 0.0)
-            ms(v("ge", 0, 256), 1.0)
-            ts(v("awx", 0, 12), v("awx", 0, 12), kf(R_), A.add)
-            act(v("dl", DW + C + 3, R * DW, DW), v("one", 0, 2), scale=col("dl", C + 3))
-            ts(v("zm", 32, 64), v("zi", 0, 32), kf(B2), A.is_equal, -8.0, A.mult)
-            ts(v("zm", 64, 96), v("zi", 32, 64), kf(N2), A.is_equal, -8.0, A.mult)
-            act(kf(CB), kf(B0), bias=2.0 * (TW // 16 - 1) + 2.4375)
-            act(kf(CA2), kf(B1), bias=kf(O20), scale=32.0)
         cp(v("iof", 0, 16), v("tb3", 0, 2 * TW, ind=wcol))
         if more:
             E2, g2 = 4 * nn, 48 * t
             n2 = 12 if t == 0 else 10
             act(kf(PA2), kf(B2 + t), AF.Abs, bias=kf(NGA))
             act(v("thr", 0, C), v("a3", 0, C), AF.Relu, bias=sc(NS), scale=FAR)
-            act(kf(CA1), kf(B3 if t else K1), bias=kf(CB), scale=2.0)
-            act(sc(S2), sc(VB), scale=0.5)
+            act(kf(CA1), kf(B3 if t else K1), bias=kf(CB), scale=-0.0625)
+            act(kf(PA1), kf(PA2), bias=(24.0 - TW) / 256, scale=(TW - 16.0) / 256)
+            ts(v("zm", 1, 65), v("zi", 64 * t + 64, 64 * t + 128), kf(N2 if t else B1), A.is_equal, OFF, A.mult)
             act(col("dl", do + DW + C + 1), sc(VB), bias=kf(V0), scale=1.0 / 256)
-            act(col("rin", 66), kf(PA2), bias=kf(CA1), scale=-2.0 * (TW // 16 - 1))
+            act(col("rin", 67), kf(PA1), bias=kf(CA1))
             scan(v("ph", 1, C + 1), v("at0", 0, C), v("t2", 0, C), 0.0, A.add, A.min)
             starts = [col("th", 0)] if t == 0 else [col("th", 16), col("th", 0), col("th", 18)]
             for m, st in enumerate(starts):
@@ -577,13 +618,17 @@ def rank_program(g, core, T, topo):
             act(v("ge", g2 + 1, g2 + n2 * E2, 2), v("ge", g2, g2 + n2 * E2, 2))
             act(v("ge", 128 + g2, 128 + g2 + n2 * E2, 2), v("ge", g2, g2 + n2 * E2, 2), bias=1.0, scale=-1.0)
             if t == 0:
-                act(kf(O21), col("rin", 66), bias=kf(CA2), scale=-8.0)
-        added(0 if first else 3 * S, 4, 128 - S if first else 0, S)
-        lo_ = x0 + (C if first else 8)
-        arrive("ar%d" % (3 * t + 2), 2, [v("hq", lo_, lo_ + 3 * S), v("hs", lo_, lo_ + 3 * S)])
+                act(kf(O21), col("rin", 67), bias=kf(CA2), scale=256.0)
+            keys_add()
+        lo_ = x0 + lay(d)[1] + S
+        arrive("ar%d" % (3 * t + 2), 2 * (len(wide[early]) + len(wide[near[0]])), [v("hq", lo_, lo_ + 2 * S), v("hs", lo_, lo_ + 2 * S)])
+        arrive("ah%d" % t, 2 * len(wide[late]), [v("lq", x0 + 8, x0 + 48), v("ls", x0 + 8, x0 + 48)])
         for b in range(4):
-            mm(bank(b, 128), "eq", "es", 128 * b, "hq", "hs", x0 + (C - 8 if first else 8), 128)
-        added(S if first else 0, 0, 8 if first else 0, 3 * S)
+            mm(bank(b, 128), "eq", "es", 128 * b, "hq", "hs", x0 + (80 if first else 48), 128)
+        for b in range(4):
+            mm(bank(4 + b, 128), "eq", "es", 128 * b, "lq", "ls", x0 + 8, 128)
+        added(0 if first else S, 0, 8 if first else 0, 3 * S)
+        added(place(d, late), 4, 0, S)
         for b in range(4):
             (cp if b % 2 else act)(v("tt", b, 640, 4), v("gt", C * b, C * b + C, ind=iof))
         qz("tq", "tsc", C * (t + 1), C, v("tt", 0, 640))
@@ -592,7 +637,7 @@ def rank_program(g, core, T, topo):
     mm(bank(5), "vq", "vs", 0, "tq", "tsc", o)
     dma("s", T.oc[:], T.tq[:, o:o + C].bitcast(dt.uint8), [], [v("tq", o, o + C)])
     for k in range(4):
-        dma("a" if k else "s", T.osc[4 * k:4 * k + 4, :], T.tsc[32 * k:32 * k + 4, o:o + C], [], [v("tsc", o, o + C)])
+        dma("a", T.osc[4 * k:4 * k + 4, :], T.tsc[32 * k:32 * k + 4, o:o + C], [], [v("tsc", o, o + C)])
     cp(v("yo", 0, C), bank(5))
     dma("s", T.y[:], T.yo[:], [], [v("yo", 0, C)])
 

from concourse.bass import DstId, RemoteDMATransfer
from concourse.mybir import dt, AluOpType, AxisListType, ActivationFunctionType

C, R, S, N = 160, 3, 40, 4
NV = 6
XW = 288
TW = 192
DW = 312
WHOLE = 1.5 * 2 ** 20
MID = 10.0
OFF = 2.0 ** 15
BIG = 1e29
FAR = 2.0 ** 80
F32, BF, I32, U16, MX, U8 = "float32", "bfloat16", "int32", "uint16", "float8_e4m3fn_x4", "uint8"


def _sb(n, d):
    return ("sbuf", [128, n], d)


SCRATCH = {
    "ps": ("psum", [128, 4096], F32),
    "xt": _sb(640, BF), "ut": _sb(512, BF), "vt": _sb(512, BF),
    "uq": _sb(128, MX), "us": _sb(128, U8), "vq": _sb(128, MX), "vs": _sb(128, U8),
    "upq": _sb(256, MX), "ups": _sb(256, U8), "wq": _sb(512, MX), "wsc": _sb(512, U8),
    "tq": _sb(4 * C, MX), "tsc": _sb(4 * C, U8),
    "fq": _sb(R * XW, MX), "fs": _sb(R * XW, U8), "hq": _sb(R * XW, MX), "hs": _sb(R * XW, U8),
    "oq": _sb(R * XW, MX), "osp": _sb(R * XW, U8), "lq": _sb(R * XW, MX), "ls": _sb(R * XW, U8), "ft": _sb(640, BF), "ht": _sb(1024, BF), "gt": _sb(640, BF), "tt": _sb(640, BF), "tp": _sb(640, BF),
    "eq": _sb(512, MX), "es": _sb(512, U8), "ea": _sb(516, BF),
    "kt": _sb(512, BF), "kq": _sb(128, MX), "ks": _sb(128, U8), "ha": _sb(128, BF),
    "ct": _sb(1920, BF), "cq": _sb(480, MX), "cs": _sb(480, U8), "sg": _sb(5 * C, BF),
    "ki": _sb(20, I32), "kf": _sb(48, F32), "uoi": _sb(16, I32), "uof": _sb(16, U16), "xf": _sb(C, F32), "xb": _sb(C, BF),
    "jm": _sb(C, BF), "hj": _sb(128, BF), "pk": _sb(C, BF), "up": _sb(C, BF), "rs": _sb(C, BF),
    "one": _sb(C, BF), "kc": _sb(2 * C, BF), "xr": _sb(C, BF), "m8": _sb(40, F32), "zi": _sb(192, F32), "zm": _sb(66, F32),
    "awx": _sb(12, F32), "wof": _sb(12, U16), "lto": _sb(16, U16), "kp": _sb(2 * C, BF),
    "pm": _sb(C, F32), "pw": _sb(C, F32), "tie": _sb(C, BF), "so": _sb(NV * C, BF), "ac": _sb(48, F32), "ato": _sb(10, U16),
    "atn": _sb(C, BF), "l0": _sb(C, BF), "l1": _sb(C, BF), "wn": _sb(2 * C, BF), "pl": _sb(2 * C, BF),
    "lab": _sb(C, BF), "pp": _sb(4, F32), "w": _sb(C, F32), "e": _sb(C, F32), "se": _sb(C + 3, F32), "fin": _sb(C + 3, F32),
    "dl": _sb(R * DW, F32), "sm": _sb(8, F32), "za": _sb(32, F32), "zat": _sb(32, F32), "zb": _sb(64, F32), "zbt": _sb(144, F32),
    "tab": _sb(16, F32), "rx": _sb(72, F32), "rin": _sb(72, F32), "of": _sb(8, U16),
    "ky": _sb(C, BF), "fl": _sb(C, BF), "b": _sb(C, BF), "y1": _sb(C, BF), "nb": _sb(C, BF), "x1": _sb(C, BF), "yb": _sb(C, BF),
    "lf": _sb(6 * TW + 16, BF),
    "tb1": _sb(2 * TW, BF), "tb2": _sb(2 * TW, BF), "tb3": _sb(2 * TW, BF), "gm": _sb(80, BF), "hm": _sb(80, BF),
    "npo": _sb(16, U16), "lro": _sb(16, U16), "ltr": _sb(16, U16), "iof": _sb(16, U16),
    "cu": _sb(64, F32), "cut": _sb(64, F32), "th": _sb(32, F32), "sc": _sb(24, F32), "ge": _sb(256, BF), "nd": _sb(32, BF), "nof": _sb(10, U16),
    "a2": _sb(C, BF), "a3": _sb(C, BF), "mk": _sb(C, BF), "thr": _sb(C, F32), "t1": _sb(C, BF), "t2": _sb(C, BF), "at0": _sb(C, BF),
    "ph": _sb(C + 2, BF),
    "olf": _sb(C, F32), "yo": _sb(C, F32),
}
SEMAPHORES = (["sv", "sa", "sp", "sg", "sent"] + ["ar%d" % k for k in range(3 * R)] + ["al%d" % k for k in range(R)] + ["ah%d" % k for k in range(R)] + ["d%d" % k for k in range(12)])

ORDER = ["bn mask yx rot sum yb zbt unit zb5 max best turn", "mask fl sum b zbt y1 zb6 cb best turn"]
A = AluOpType
AF = ActivationFunctionType


def v(name, c0, c1, step=1, p0=0, p1=128, ind=None, cast=None):
    return (name, c0, c1, step, p0, p1, ind, cast)


def col(name, c, p0=0, p1=128):
    return v(name, c, c + 1, 1, p0, p1)


def bank(k, n=C):
    return v("ps", 512 * k, 512 * k + n)


def _meet(a, b):
    if a[0] != b[0]:
        return False
    if a[0] == "ps":
        return a[1] // 512 == b[1] // 512
    if a[5] <= b[4] or b[5] <= a[4] or a[2] <= b[1] or b[2] <= a[1]:
        return False
    if a[2] - a[1] == 1 or b[2] - b[1] == 1:
        return (a[1] - b[1]) % max(a[3], b[3]) == 0 or max(a[3], b[3]) == 1
    return not (a[3] == b[3] and a[3] > 1 and a[1] % a[3] != b[1] % a[3])


def plan(d):
    rot = 2 * S if (S * d) % (2 * S) != (S if 2 * d >= N else 0) else 0
    return rot, (S * d - rot) % C == 0


def deal(topo, cores, r):
    free = {o: topo.engines(cores[r], cores[o]) for o in range(N) if o != r}
    out, taken = {}, []
    for width in sorted(set(len(f) for f in free.values())):
        same = [o for o in free if len(free[o]) == width]
        left = [e for e in free[same[0]] if e not in taken]
        k = 1
        while 2 * k * len(same) <= len(left):
            k *= 2
        for n_, o in enumerate(same):
            out[o] = left[n_::len(same)][:k]
            taken += out[o]
    return out


def rank_program(g, core, T, topo):
    d = T.rank_of(core)
    if d is None:
        return
    ops = []

    def ap(x):
        if not isinstance(x, tuple):
            return x
        a = T[x[0]][x[4]:x[5], x[1]:x[2]] if x[3] == 1 else T[x[0]][x[4]:x[5], x[1]:x[2]:x[3]]
        if x[7] is not None:
            a = a.bitcast(x[7])
        if x[6] is not None:
            a = a.indirect(ap(x[6]))
        return a

    def op(eng, fn, outs, ins, **kw):
        rd = [x for x in ins if isinstance(x, tuple)]
        rd += [x[6] for x in rd + list(outs) if x[6] is not None]
        ops.append(dict(eng=eng, fn=fn, wr=list(outs), rd=rd, **kw))

    def ts(o, i, s1, op0, s2=None, op1=None):
        if op1 is None:
            op("v", lambda e: e.tensor_scalar(ap(o), ap(i), ap(s1), None, op0), [o], [i, s1])
        else:
            op("v", lambda e: e.tensor_scalar(ap(o), ap(i), ap(s1), ap(s2), op0, op1), [o], [i, s1, s2])

    def tt(o, a, b, k):
        op("v", lambda e: e.tensor_tensor(ap(o), ap(a), ap(b), k), [o], [a, b])

    def cp(o, i):
        op("v", lambda e: e.tensor_copy(ap(o), ap(i)), [o], [i])

    def ms(o, c):
        op("v", lambda e: e.memset(ap(o), c), [o], [])

    def red(o, i, k, absolute=False):
        if absolute:
            op("v", lambda e: e.tensor_reduce(ap(o), ap(i), AxisListType.X, k, negate=True, apply_absolute_value=True), [o], [i])
        else:
            op("v", lambda e: e.tensor_reduce(ap(o), ap(i), AxisListType.X, k), [o], [i])

    def scan(o, a, b, init, op0, op1):
        op("v", lambda e: e.tensor_tensor_scan(ap(o), ap(a), ap(b), ap(init), op0, op1), [o], [a, b, init])

    def tr(o, i):
        op("v", lambda e: e.transpose(ap(o), ap(i)), [o], [i])

    def qz(q, s, c, n, i):
        op("v", lambda e: e.quantize_mx(ap(v(q, c, c + n)), ap(v(s, c, c + n)), ap(i)), [v(q, c, c + n), v(s, c, c + n)], [i])

    def act(o, i, f=None, bias=None, scale=None, acc=None):
        kw = {}
        if bias is not None:
            kw["bias"] = bias
        if scale is not None:
            kw["scale"] = scale
        if acc is not None:
            kw["accum_out"] = acc
        f = f if f is not None else (AF.Copy if bias is None else AF.Identity)
        op("a", lambda e: e.activation(ap(o), ap(i), f, **{k: ap(x) for k, x in kw.items()}),
           [o] + ([acc] if acc is not None else []), [i, bias, scale])

    def mm(o, wq, ws, wc, xq, xs, xc, n=C, start=True, stop=True):
        a = [v(wq, wc, wc + 128), v(ws, wc, wc + 128), v(xq, xc, xc + n), v(xs, xc, xc + n)]
        op("p", lambda e: e.matmul_mx(ap(o), ap(a[0]), ap(a[1]), ap(a[2]), ap(a[3]), start, stop), [o], a, chain=not start)

    def iota(o, pat, base=0, cm=0):
        if SCRATCH[o[0]][2] == I32:
            op("g", lambda e: e.iota(ap(o), pat, base, cm), [o], [])
        else:
            op("g", lambda e: e.iota(ap(o), pat, base, cm, allow_small_or_imprecise_dtypes=True), [o], [])

    nd = [0]

    def dma(eng, o, i, outs, ins):
        op(eng, lambda e: e.dma_start(o, i), outs, ins, dma="d%d" % nd[0])
        nd[0] += 1

    peers = [r for r in range(N) if r != d]
    eng_of = deal(topo, T.cores, d)
    coming = sum(len(deal(topo, T.cores, r)[d]) for r in peers)
    sent = [0]

    far = [r for r in peers if topo.chip(T.cores[r]) != topo.chip(core)]
    near = [r for r in peers if r not in far]

    early, late = sorted(far, key=lambda r: topo.die(T.cores[r]) != topo.die(core))
    wide = {r: sorted(k for o in (far if r in far else near) for k in eng_of[o]) for r in peers}

    def send_codes(sem, r, here, there):
        for k, f in ((0, bytes_), (1, lambda x: x)):
            send(sem, r, f(v(here[k], here[2], here[2] + S)), f(v(there[k], there[2], there[2] + S)), wide[r])

    def send(sem, r, here, there, engines):
        to = list(zip(r, there)) if isinstance(r, list) else [(r, there)]

        def fn(e):
            ids = [DstId(rid=topo.addr(T.cores[o])[0], pnc=topo.addr(T.cores[o])[1]) for o, _ in to]
            return e.remote_dma_fused([RemoteDMATransfer(dst_ids=ids, dma_engine_mask=sum(1 << k for k in engines), remote_sem=T.sem[sem],
                                                         srcs=[ap(here)], dsts=[ap(x) for _, x in to])], local_sem=T.sem.sent)
        op("g", fn, [], [here], remote=True)
        sent[0] += len(engines)

    def arrive(sem, n, outs):
        ops.append(dict(eng=None, wr=outs, rd=[], arr=(sem, n)))

    def bytes_(x):
        return x[:7] + (dt.uint8,)

    def words(x, ind=None):
        return x[:6] + (ind, dt.uint32)

    rot, first = plan(d)

    def lay(r):
        return (16, 88) if plan(r)[1] else (128, 8)

    def turn_(r, o):
        return [x for x in range(N) if x != r].index(o)

    def place(r, o):
        return (S * o - plan(r)[0]) % C

    assert sorted(place(d, o) for o in (early, near[0])) == [S, 2 * S]

    def row(k, ind=None):
        return v("lf", TW * k + 16, TW * k + 16 + C, ind=ind)

    dma("s", T.ut[:], T.u[:], [v("ut", 0, 512)], [])
    dma("s", T.xt[:], T.x[:], [v("xt", 0, 640)], [])
    dma("s", T.wq[:].bitcast(dt.uint8), T.wc[:], [v("wq", 0, 512)], [v("xt", 0, 640)])
    dma("s", T.wsc[:], T.ws[:], [v("wsc", 0, 512)], [])
    iota(col("ki", 9), [[0, 1]], 0, 1)
    iota(v("uoi", 0, 8), [[16, 8]])
    iota(v("jm", 0, C), [[0, 10], [1, 16]])
    iota(v("m8", 0, 8), [[1, 2], [0, 4]])
    iota(v("m8", 8, 16), [[0, 2], [1, 2], [0, 2]])
    for q in range(4):
        for x in range(2):
            iota(v("hj", 32 * q + x, 32 * q + 32, 2), [[1, 2], [0, 4], [-4 if q & 2 else 4, 2]], 2 * (q ^ x))
    iota(v("xf", 0, C), [[1, C]])
    for t, pat in enumerate(([[0, 8], [1, 2], [0, 4]], [[0, 16], [1, 2], [0, 2]], [[0, 16], [1, 4]])):
        iota(v("zi", 64 * t, 64 * t + 64), pat)
    iota(v("awx", 0, 12), [[16, 12]])
    iota(v("ea", 0, 516), [[0, 516]], 1)
    op("g", lambda e: e.affine_select(ap(v("ea", 0, 516)), ap(v("ea", 0, 516)), [[1, 516]], A.is_equal, 0.0, -3, -4),
       [v("ea", 0, 516)], [v("ea", 0, 516)])
    unit = lambda b: qz("eq", "es", 128 * b, 128, v("ea", 3 - b, 515 - b))
    R_, G_, B0, B1, B2, B3, GA, N2, K1 = range(9)
    (NB3, NGA, SIG, KB, C0, W16, T1S, T1B, TI0, H1, V0, PA1, PA2, CA1, CA2, CB, COL1, COL2, O20, O21, KK, PB, PS0, PS1, PS2, NB2, NN2, Z0, NB0,
     WB, NG, LA, LB, G16, GC, WO) = range(9, 45)
    kf = lambda k: col("kf", k)
    p_ = col("ki", 9)
    ms(v("uoi", 8, 16), 8)
    ms(v("ct", 1280 + 3, 1920, 4), 0.0)
    ms(col("ac", 3 * (10 - NV) - 1), 0.0)
    for k in range(3):
        ms(v("ac", 16 + k, 28, 3), float(k > 0))
    ts(col("ki", R_), p_, 15, A.bitwise_and)
    ts(col("ki", G_), p_, 4, A.arith_shift_right)
    for k, (sh, m) in enumerate(((0, 1), (1, 1), (2, 1), (3, 1), (4, 1), (1, 3), (2, 3))):
        ts(col("ki", B0 + k), p_, sh, A.arith_shift_right, m, A.bitwise_and)
    cp(v("uof", 0, 16), v("uoi", 0, 16))
    cp(v("kf", 0, 9), v("ki", 0, 9))
    ts(v("pk", 0, C), v("jm", 0, C), kf(R_), A.not_equal, 2 * BIG, A.mult)
    ts(v("up", 0, C), v("jm", 0, C), 0.0, A.is_equal, 2 * BIG, A.mult)
    ts(v("rs", 0, C), v("jm", 0, C), 0.0, A.not_equal)
    ts(v("pk", 0, C), v("pk", 0, C), -BIG, A.add)
    act(kf(NGA), kf(GA), scale=-1.0)
    act(kf(NB3), kf(B3), bias=1.0, scale=-1.0)
    act(v("one", 0, C), v("jm", 0, C), bias=1.0, scale=0.0)
    act(kf(NG), kf(G_), scale=-1.0)
    act(v("kc", 0, C), v("jm", 0, C), bias=kf(B3), scale=0.0)
    act(kf(W16), kf(B3), bias=float(C), scale=-float(C))
    act(kf(NN2), kf(B3), bias=-1.0)
    act(kf(PA1), kf(B3), bias=-2.0)
    for k in range(7):
        act(v("lf", max(0, TW * k - 16), TW * k + 16), v("one", 0, 32 if k else 16), scale=0.0)
    act(v("m8", 24, 32), v("m8", 8, 16), bias=kf(NB3), scale=kf(PA1))
    act(kf(WO), kf(GA), bias=40.0, scale=-32.0)

    act(v("ha", 0, 128), v("hj", 0, 128), AF.Abs, bias=kf(NG))

    qz("uq", "us", 0, 128, v("ut", 0, 512))
    ts(v("m8", 16, 24), v("m8", 0, 8), kf(GA), A.is_equal, 256.0, A.mult)
    ts(kf(KK), kf(R_), 9.0, A.min)
    ts(kf(PB), kf(R_), 10.0, A.is_ge, kf(B0), A.max)
    cp(words(v("upq", 0, 128)), words(v("uq", 0, 128), v("uof", 0, 8)))
    act(v("ups", 0, 128), v("us", 0, 128, ind=v("uof", 0, 8)))
    qz("tq", "tsc", 0, C, v("xt", 0, 640))
    mm(bank(0), "upq", "ups", 0, "tq", "tsc", 0)
    mm(bank(3), "upq", "ups", 0, "tq", "tsc", 0)
    cp(words(v("upq", 128, 256)), words(v("uq", 0, 128), v("uof", 8, 16)))
    act(v("ups", 128, 256), v("us", 0, 128, ind=v("uof", 8, 16)))
    mm(bank(4), "upq", "ups", 128, "tq", "tsc", 0)
    tt(kf(PS0), kf(PB), kf(GA), A.is_equal)
    tt(v("m8", 32, 40), v("m8", 16, 24), v("m8", 24, 32), A.mult)
    ts(kf(PS2), kf(R_), 10.0 - rot // 16, A.is_ge, -10.0, A.mult)
    for t in range(4):
        act(v("kt", t, 512, 4), v("ha", 0, 128), AF.Relu, bias=1.0, scale=-1.0)
    tt(v("pm", 0, C), bank(0), v("pk", 0, C), A.max)
    ts(kf(PS1), kf(PS0), TW // 16 - 1.0, A.mult, kf(KK), A.add)
    ts(kf(PS2), kf(PS2), kf(KK), A.add, float(TW // 16 - 1 + rot // 16), A.add)
    act(v("l0", 0, C), bank(4), AF.Sign)
    scan(v("pw", 0, C), v("up", 0, C), v("pm", 0, C), 0.0, A.add, A.min)
    qz("kq", "ks", 0, 128, v("kt", 0, 512))
    na = 3 * (10 - NV)
    cmp_ = lambda c, a=0, b=C: v("ct", 640 * (c // 4) + c % 4 + 4 * a, 640 * (c // 4) + c % 4 + 4 * b - 3, 4)
    count_ = lambda c: scan(v("so", C * c, C * c + C), v("one", 0, C), cmp_(c), col("tie", 16 * c + 15), A.mult, A.add)
    act(v("l1", 0, C), v("l0", 0, C), AF.Relu, acc=col("pp", 1))
    for c in range(NV, 10):
        act(v("sg", C * (c - NV), C * (c - NV + 1)), bank(3), AF.Sign, bias=col("pw", 16 * c + 15), scale=-1.0)
    for c in range(NV, 10):
        k, so = 16 * c + 16, C * (c - NV)
        act(cmp_(c, 0, k), v("sg", so, so + k), AF.Relu, scale=-1.0, acc=col("ac", 3 * (c - NV) + 1))
        if k < C:
            act(cmp_(c, k, C), v("sg", so + k, so + C), AF.Sign, bias=1.0, scale=-1.0, acc=col("ac", 3 * (c - NV) + 2))
        if c == 8:
            act(col("pp", 3), col("pp", 1), bias=kf(B3), scale=kf(NN2))
    act(v("wn", 0, C), v("l1", 0, C), bias=col("pp", 3), scale=kf(W16))
    tt(cmp_(10), bank(0), v("pw", 0, C), A.is_equal)
    for c in range(NV):
        k = 16 * c + 16
        ts(cmp_(c, 0, k), bank(0, k), col("pw", k - 1), A.is_gt)
        ts(cmp_(c, k, C), v("ps", k, C), col("pw", k - 1), A.is_ge)
        if c == 1:
            scan(v("tie", 0, C), v("rs", 0, C), cmp_(10), 0.0, A.mult, A.add)
    cp(v("ac", 0, na, 3), v("tie", 16 * NV + 15, C, 16))
    for c in range(NV):
        count_(c)
    qz("cq", "cs", 0, C, v("ct", 0, 640))
    scan(v("ac", 32, 32 + na), v("ac", 16, 16 + na), v("ac", 0, na), 0.0, A.mult, A.add)
    ts(col("wof", 0), kf(PS1), 16.0, A.mult, 24.0, A.add)
    ts(v("ato", 0, NV), v("so", C - 1, NV * C, C), -1.0, A.mult, float(C), A.add)
    scan(v("wn", C, 2 * C), v("kc", 0, C), v("wn", 0, C), -1.0, A.mult, A.add)
    ts(v("ato", NV, 10), v("ac", 34, 32 + na, 3), -1.0, A.mult, float(C), A.add)
    ato = v("ato", 0, 10)
    qz("cq", "cs", C, C, v("ct", 640, 1280))
    cp(row(5, ato), v("wn", C, 2 * C))
    qz("cq", "cs", 2 * C, C, v("ct", 1280, 1920))
    ts(col("wof", 6), kf(PS1), 16.0, A.mult, kf(WO), A.add)
    for s in range(3):
        mm(bank(2), "kq", "ks", 0, "cq", "cs", C * s, start=s == 0, stop=s == 2)
    act(v("kc", C, 2 * C), v("one", 0, C), scale=kf(NB3))
    dma("a", T.vt[:], T.v[:], [v("vt", 0, 512)], [])
    act(kf(SIG), kf(B3), bias=-1.0, scale=2.0)
    act(kf(KB), kf(B3), bias=162.0, scale=-323.0)
    act(kf(TI0), kf(GA), bias=-MID / 256, scale=0.0625)
    act(v("zm", 0, 66, 65), v("one", 0, 2), scale=OFF)
    act(v("zm", 1, 65), v("zi", 0, 64), bias=OFF, scale=-OFF)
    act(kf(LB), kf(B2), AF.Abs, bias=kf(NGA))
    act(kf(GC), kf(GA), bias=-(24 + MID) / 256, scale=12.0 / 256)
    act(kf(G16), kf(GA), scale=16.0)
    act(v("dl", 0, C), v("one", 0, C), scale=1.0 / 256)
    act(col("dl", C), col("one", 0), scale=1.0 / 256)
    act(col("dl", C + 1), col("one", 0), scale=0.0)
    act(col("se", C), col("one", 0), scale=0.0)
    act(v("se", C + 1, C + 3), v("one", 0, 2), scale=-BIG)
    act(col("dl", C + 6), kf(G_), bias=kf(TI0), scale=0.125)
    act(v("dl", C + 22, DW - 4, 4), v("one", 0, 32), scale=0.0)
    act(kf(LA), kf(LB), bias=1.0, scale=-1.0)
    act(kf(C0), kf(KB), scale=kf(LB))
    act(kf(COL1), kf(SIG), scale=kf(LB))
    act(col("rin", 65), col("one", 0), scale=WHOLE)
    act(col("rin", 66), col("one", 0), scale=-WHOLE)
    act(v("zbt", 128, 144), v("one", 0, 16), scale=BIG)
    act(v("pl", 0, C), row(5), bias=kf(NB3), scale=kf(B3))

    def spread(put, on_vector):
        jobs = [(0, 0, 0, 128), (2, 0, 64, 64), (2, 64, 0, 64)]
        jobs += [(x, 32 * q, 32 * (q ^ x), 32) for x in (1, 3) for q in range(4)]
        for n_, (x, to, fro, k) in enumerate(jobs):
            put(n_ < on_vector, x, (to, to + k), (fro, fro + k))

    def turn(tb, k):
        tr(v(tb, 0, TW), v("lf", TW * k, TW * k + TW))
        tr(v(tb, TW, 2 * TW), v("lf", TW * k + 16, TW * k + 16 + TW))

    def keys(own):
        act(v("kp", 0, C), v("atn", 0, C, ind=own), scale=kf(LA))

    def keys_add():
        tt(v("ky", 0, C), v("kp", C, 2 * C, ind=v("lto", 0, 10)), v("kp", 0, C), A.add)

    f0 = 32 if first else 0
    wtrue, wrot, wcol = col("wof", 0), col("wof", 2 if rot else 0), col("wof", 4)
    ltr, lro, iof, nof = v("ltr" if rot else "lro", 0, 10), v("lro", 0, 10), v("iof", 0, 10), v("nof", 0, 10)
    SZ, VO, S2, NS, LH, TP, VB, DD, HX = range(4, 13)
    sc = lambda k: col("sc", k)

    for t in range(R):
        nn = 2 ** t
        E = 2 * nn if t else 1
        nk = -(-10 * E // 16)
        go = 48 * (t - 1)
        if t > 0:
            mm(bank(4), "upq", "ups", 128, "tq", "tsc", C * t)
            for b in range(4):
                act(v("tp", C * b, C * b + C), v("tt", b, 640, 4))
            step = lambda m: v("ge", go + 2 * m, go + 10 * E, E)
            tt(v("dl", DW * t, DW * t + C + 1), v("ph", 0, C + 1), v("ph", 1, C + 2), A.subtract)
            ts(v("mk", 0, C), v("a2", 0, C), sc(SZ), A.is_lt)
            ms(v("rin", 68, 72), -1.0 / E)
            tt(v("lab", 0, C), bank(4), v("thr", 0, C), A.is_gt)
            ts(nof, step(1), 4.0, A.mult, kf(G16), A.add) if t == 1 else tt(v("nd", 0, 10), step(1), step(2), A.add)
            scan(v("l1", 0, C), v("one", 0, C), v("lab", 0, C), 0.0, A.mult, A.subtract)
            if t == 2:
                tt(v("nd", 16, 26), v("nd", 0, 10), step(3), A.add)
            ts(v("w", 0, 96), v("lab", 0, C, ind=v(ltr[0], 0, 6)), col("nd", 30), A.mult, col("l1", C - 1), A.add)
            act(v("w", 96, C), v("lab", 0, C, ind=v(ltr[0], 6, 10)), bias=col("l1", C - 1), scale=sc(SZ))
            if t == 2:
                ts(nof, v("nd", 16, 26), 2.0, A.mult, kf(G16), A.add)
            scan(v("e", 0, C), v("w", 0, C), v("mk", 0, C), 0.0, A.add, A.mult)
        else:
            scan(v("e", 0, C), v("kc", C, 2 * C), row(5), 0.0, A.mult, A.add)
            turn("tb2", 5)
        do = DW * t
        gain = col("dl", do + C + 2)
        red(gain, v("e", 0, C), A.max, True)
        for to in (far, near):
            send("ar%d" % (3 * t), to, gain, [col("dl", do + C + 10 + 4 * turn_(r, d)) for r in to], wide[to[0]])
        act(v("se", 0, C), v("e", 0, C), AF.Abs)
        if t == 0:
            cp(v("ltr", 0, 16), v("tb2", 0, 2 * TW, ind=wtrue))
            cp(v("lto", 0, 16), v("tb2", 0, 2 * TW, ind=col("wof", 6)))
            act(v("atn", 0, C), bank(2), bias=kf(KB), scale=kf(SIG))
            act(v("kp", C, 2 * C), bank(2), bias=kf(C0), scale=kf(COL1))
        scan(v("fin", 0, C + 3), v("dl", do, do + C + 3), v("se", 0, C + 3), 0.0 if t else -1.0 / 256, A.add, A.max)
        if t == 0:
            scan(v("pl", C, 2 * C), v("kc", C, 2 * C), v("pl", 0, C), -1.0, A.mult, A.add)
            ts(col("rin", 67), kf(PS1), -0.0625, A.mult, kf(GC), A.add)
            ts(kf(PB), kf(PS0), 1.0 - TW // 16, A.mult, kf(PS2), A.add)
            keys(v("ltr", 0, 10))

        def put_cut(vec, x, to, fro, t=t):
            o, m, s = v("za", x, 32, 4, *to), v("m8", 32, 40, 1, *fro), col("fin", C + 2, *fro)
            if t == 0:
                ts(o, m, s, A.mult) if vec else act(o, m, scale=s)
            elif vec:
                ts(o, m, s, A.mult, col("sc", VB, *fro), A.add)
            else:
                act(o, m, bias=col("sc", VB, *fro), scale=s)
        spread(put_cut, 6)
        if t == 0:
            keys_add()
        tr(v("zat", 0, 32), v("za", 0, 32))
        if t == 0:
            unit(0)
            for b in range(4):
                act(v("tp", C * b, C * b + C), v("xt", b, 640, 4))
            act(v("xb", 0, C), v("xf", 0, C))
            act(kf(NB0), kf(B0), bias=float(rot), scale=-float(rot))
            act(kf(WB), kf(B0), bias=-float(rot), scale=float(rot))
            act(kf(T1S), kf(B3), bias=-1.0 / 256, scale=1.0 / 256)
            act(kf(T1B), kf(B3), bias=160.0 / 256, scale=-161.0 / 256)
            act(kf(V0), kf(B3), scale=-160.0 / 256)
            act(kf(H1), kf(B1), scale=float(C))
            if rot:
                act(v("xr", 0, C - rot), v("xf", 0, C - rot), bias=kf(NB0))
                act(v("xr", C - rot, C), v("xf", C - rot, C), bias=kf(WB))
            act(kf(O21), col("rin", 67), bias=8.0 + MID, scale=256.0)
        more = t < R - 1
        lo, hi = sc(2 * t), sc(2 * t + 1)
        arrive("ar%d" % (3 * t), sum(len(wide[r]) for r in peers), [v("dl", do + C + 10, do + C + 19)])

        def put_sum(vec, x, to, fro, t=t):
            o, i = v("zbt", 32 * x, 32 * x + 32, 1, *to), v("zbt", 0, 32, 1, *fro)
            if x:
                ts(o, i, x / 256.0, A.add) if vec else act(o, i, bias=x / 256.0)
        steps = {
            "fl": lambda: act(v("fl", 0, C), v("zat", 8, 32, ind=nof)),
            "b": lambda: tt(v("b", 0, C), v("zat", 0, 32, ind=nof), v("ky", 0, C), A.is_lt),
            "bn": lambda: (ts(v("b", 0, C), v("ky", 0, C), col("zat", 0), A.subtract, col("zat", 16), A.is_gt),
                           ts(col("tab", 8), col("zat", 0), col("zat", 16), A.add, float(C), A.add),
                           ts(v("nb", 0, C), v("ky", 0, C), col("zat", 0), A.subtract, col("zat", 16), A.is_le)),
            "yx": lambda: (scan(v("y1", 0, C), v("one", 0, C), v("b", 0, C), col("tab", 8), A.mult, A.add),
                           scan(v("x1", 0, C), v("one", 0, C), v("nb", 0, C), -1.0, A.mult, A.add)),
            "yb": lambda: scan(v("yb", 0, C), v("y1", 0, C), v("b", 0, C), 0.0, A.max, A.mult),
            "rot": lambda: ts(col("wof", 2), kf(PB), 16.0, A.mult, 24.0, A.add),
            "y1": lambda: scan(v("y1", 0, C), v("fl", 0, C), v("b", 0, C), -1.0, A.max, A.add),
            "cb": lambda: scan(row(3), v("y1", 0, C), v("b", 0, C), 0.0, A.max, A.mult),
            "max": lambda: tt(row(3), v("x1", 0, C), v("yb", 0, C), A.max),
            "turn": lambda: turn("tb1", 3),
            "unit": lambda: unit(3),
            "sum": lambda: scan(v("zb", 27, 64), v("one", 0, 37), v("dl", do + C + 2, do + DW - 4, 4), 0.0, A.mult, A.add),
            "mask": lambda: tt(v("rin", 0, 65), v("zm", 1, 66), v("zm", 0, 65), A.subtract),
            "zb5": lambda: spread(put_sum, 5), "zb6": lambda: spread(put_sum, 6), "zb4": lambda: spread(put_sum, 4), "zb7": lambda: spread(put_sum, 7),
            "zbt": lambda: tr(v("zbt", 0, 32), v("zb", 32, 64)),
            "best": lambda: scan(v("rx", 0, 67 + nk), v("rin", 0, 67 + nk), v("zbt", 0, 134 + 2 * nk, 2), 2.0, A.add, A.min),
        }
        for name in ORDER[min(t, 1)].split():
            steps[name]()
        if t == 0:
            act(v("cu", 0, 32), v("one", 0, 32), bias=1.0, scale=col("tab", 8))
            act(v("ph", 0, C + 2, C + 1), v("one", 0, 2), scale=0.0)
            act(v("awx", 0, 12), v("awx", 0, 12), bias=kf(R_))
            act(kf(CB), kf(B0), bias=kf(GC), scale=-8.0 / 256)
            act(kf(CA2), kf(B1), bias=8.0 + MID, scale=32.0)
            act(v("dl", DW + C + 6, R * DW, DW), v("one", 0, 2), scale=col("dl", C + 6))
            for k in (1, 2):
                act(v("dl", DW * k + C + 22, DW * k + DW - 4, 4), v("one", 0, 32), scale=0.0)
                act(v("ge", 128 * k - 128, 128 * k), v("one", 0, 128))
            act(v("ht", 512 + 4 * S, 1024), v("xt", 0, 512 - 4 * S), scale=0.0)
            act(v("ht", 0 if first else 480, 32 if first else 512), v("one", 0, 32), scale=0.0)
        if t == 1:
            act(v("cu", 0, 64), v("zat", 8, 32, ind=v("wof", 8, 12)), bias=1.0)
        ts(v("of", 0, nk), v("rx", 67, 67 + nk), col("rx", 64), A.subtract, -256.0, A.mult)
        if more:
            tr(v("cut", 0, 32 * nn), v("cu", 0, 32 * nn))
        if t == 0:
            unit(2)
        picks = v("tb1", 0, 2 * TW, ind=v("of", 0, nk))
        bounds = []
        if more:
            bounds += [lambda: ts(col("of", 6), col("of", 0), kf(O21), A.add),
                       lambda: cp(v("th", 16 * t, 16 * t + 16), v("cut", 0, 32 * nn, ind=col("of", 6)))]
        if t == 0:
            bounds += [lambda: (ts(lo, kf(B2), col("th", 0), A.mult), ts(hi, kf(B2), float(C), A.mult, col("th", 0), A.max))]
        if t == 1:
            bounds += [lambda: ts(sc(DD), col("th", 18), col("th", 16), A.subtract, kf(B2), A.mult),
                       lambda: ts(sc(TP), sc(DD), col("th", 16), A.add),
                       lambda: (ts(lo, kf(B1), sc(TP), A.mult, sc(0), A.max), ts(hi, kf(H1), sc(TP), A.max, sc(1), A.min))]
        if more:
            bounds += [lambda: (ts(sc(LH), lo, hi, A.add, -1.0, A.add), tt(sc(SZ), hi, lo, A.subtract))]
        chain = [lambda: cp(v("npo", 0, 16), picks)]
        if t:
            chain = [lambda: tt(v("gm", 0, 16 * nk), picks, v("ge", go, go + 16 * nk), A.mult),
                     lambda: scan(v("hm", 0, 16 * nk), v("ge", 128 + go, 128 + go + 16 * nk), v("gm", 0, 16 * nk), 0.0, A.mult, A.add),
                     lambda: cp(v("npo", 0, 10), v("hm", E - 1, 10 * E, E))]
        chain += [lambda: cp(row(t, v("npo", 0, 10)), row(t - 1) if t else v("pl", C, 2 * C)),
                  lambda: turn("tb2", t),
                  lambda: cp(v("lro", 0, 16), v("tb2", 0, 2 * TW, ind=wrot))]
        for k, step_ in enumerate(chain):
            step_()
            if k < len(bounds):
                bounds[k]()
        x0 = XW * t

        def gather_f(c0, c1, every):
            for b in range(4):
                (cp if (b + 1) % every else act)(v("ft", 64 * c0 + b, 64 * c1, 4), v("tp", C * b, C * b + C, ind=v("lro", c0, c1)))

        def scaled(at, k, a, n, every):
            for b in range(4):
                o, i = v("ht", 4 * at + b, 4 * (at + n), 4), v("ps", 512 * (k + b) + a, 512 * (k + b) + a + n)
                ts(o, i, 0.015625, A.mult) if b % every else act(o, i, scale=0.015625)

        def added(at, k, a, n):
            for b in range(4):
                tt(v("gt", C * b + at, C * b + at + n), v("ft", 4 * at + b, 4 * (at + n), 4), v("ps", 512 * (k + b) + a, 512 * (k + b) + a + n), A.add)

        gather_f(f0 // 16, f0 // 16 + 8, 2)
        qz("fq", "fs", x0 + 48, 128, v("ft", 4 * f0, 4 * f0 + 512))
        mine = lambda r: ("fq", "fs", x0 + 48 + place(d, r) - f0)
        send_codes("ar%d" % (3 * t + 1), early, mine(early), ("oq", "osp", x0 + lay(early)[0] + S))
        send_codes("ar%d" % (3 * t + 1), near[0], mine(near[0]), ("oq", "osp", x0 + lay(near[0])[0]))
        send_codes("al%d" % t, late, mine(late), ("fq", "fs", x0 + 8))
        gather_f(*((0, 2) if first else (8, 10)), 1)
        if more and rot:
            cp(v("ltr", 0, 16), v("tb2", 0, 2 * TW, ind=wtrue))
        if more:
            cp(v("lto", 0, 16), v("tb2", 0, 2 * TW, ind=col("wof", 6)))
            ts(sc(VB), lo, -1.0, A.add, kf(B3), A.mult)
            act(v("t1", 0, C), row(t), bias=kf(T1B), scale=kf(T1S))
            act(v("a2", 0, C), v("xf", 0, C), AF.Abs, bias=sc(LH), scale=-2.0)
        qz("oq", "osp", x0 + (96 if first else 0), 128, v("ft", 128 - 4 * f0, 640 - 4 * f0))
        cp(row(4, lro), v("xr" if rot else "xb", 0, C))
        if t == 0:
            ts(col("wof", 4), kf(PS1), 16.0, A.mult, 25.0, A.add)
            ts(v("wof", 8, 12), v("m8", 8, 12), 4.0, A.mult, kf(G16), A.add)
        if more:
            act(sc(NS), sc(SZ), scale=-FAR)
            act(col("nd", 30), sc(SZ))
        else:
            act(v("olf", 0, C), row(t))
            dma("s", T.ol[:], T.olf[8:128:16, :], [], [v("olf", 0, C)])
        lo_, qh, h0 = x0 + lay(d)[0], x0 + (0 if first else 128), 8 if first else S
        arrive("ar%d" % (3 * t + 1), 2 * (len(wide[early]) + len(wide[near[0]])), [v("oq", lo_, lo_ + 2 * S), v("osp", lo_, lo_ + 2 * S)])
        arrive("al%d" % t, 2 * len(wide[late]), [v("fq", x0 + 8, x0 + 48), v("fs", x0 + 8, x0 + 48)])
        for b in range(4):
            mm(bank(b, 128), "wq", "wsc", 128 * b, "oq", "osp", x0 + (16 if first else 80), 128)
        for b in range(4):
            mm(bank(4 + b, 128), "wq", "wsc", 128 * b, "fq", "fs", x0 + 8, 128)
        scaled(8 if first else 0, 0, 0 if first else 8, 3 * S, 2)
        scaled(128, 4, 0, S, 1)
        home = lambda r: ("hq", "hs", x0 + lay(r)[1] + place(r, d))
        qz("hq", "hs", qh, 128, v("ht", 0, 512))
        send_codes("ar%d" % (3 * t + 2), near[0], ("hq", "hs", qh + h0), home(near[0]))
        send_codes("ar%d" % (3 * t + 2), early, ("hq", "hs", qh + h0 + S), home(early))
        qz("lq", "ls", x0 + 48, 128, v("ht", 512, 1024))
        send_codes("ah%d" % t, late, ("lq", "ls", x0 + 48), ("lq", "ls", x0 + 8))
        turn("tb3", 4)
        if t == 0:
            unit(1)
        if not more:
            qz("vq", "vs", 0, 128, v("vt", 0, 512))
        else:
            keys(ltr)
            act(v("a3", 0, C), row(4), AF.Abs, bias=sc(LH), scale=-2.0)
            ts(v("at0", 0, C), v("xb", 0, C), lo, A.is_equal)
            scan(v("t2", 0, C), v("kc", 0, C), v("t1", 0, C), 161.0 / 256, A.mult, A.add)
        cp(v("iof", 0, 16), v("tb3", 0, 2 * TW, ind=wcol))
        if more:
            E2, g2 = 4 * nn, 48 * t
            n2 = 12 if t == 0 else 10
            act(kf(PA2), kf(B2 + t), AF.Abs, bias=kf(NGA))
            act(v("thr", 0, C), v("a3", 0, C), AF.Relu, bias=sc(NS), scale=FAR)
            act(kf(CA1), kf(B3 if t else K1), bias=kf(CB), scale=-0.0625)
            act(kf(PA1), kf(PA2), bias=(24.0 - TW) / 256, scale=(TW - 16.0) / 256)
            ts(v("zm", 1, 65), v("zi", 64 * t + 64, 64 * t + 128), kf(N2 if t else B1), A.is_equal, OFF, A.mult)
            act(col("dl", do + DW + C + 1), sc(VB), bias=kf(V0), scale=1.0 / 256)
            act(col("rin", 67), kf(PA1), bias=kf(CA1))
            scan(v("ph", 1, C + 1), v("at0", 0, C), v("t2", 0, C), 0.0, A.add, A.min)
            starts = [col("th", 0)] if t == 0 else [col("th", 16), col("th", 0), col("th", 18)]
            for m, st in enumerate(starts):
                ts(v("ge", g2 + 2 * m + 2, g2 + n2 * E2, E2), v("awx", 0, n2), st, A.is_ge)
            act(v("ge", g2 + 1, g2 + n2 * E2, 2), v("ge", g2, g2 + n2 * E2, 2))
            act(v("ge", 128 + g2, 128 + g2 + n2 * E2, 2), v("ge", g2, g2 + n2 * E2, 2), bias=1.0, scale=-1.0)
            if t == 0:
                act(kf(O21), col("rin", 67), bias=kf(CA2), scale=256.0)
            keys_add()
        lo_ = x0 + lay(d)[1] + S
        arrive("ar%d" % (3 * t + 2), 2 * (len(wide[early]) + len(wide[near[0]])), [v("hq", lo_, lo_ + 2 * S), v("hs", lo_, lo_ + 2 * S)])
        arrive("ah%d" % t, 2 * len(wide[late]), [v("lq", x0 + 8, x0 + 48), v("ls", x0 + 8, x0 + 48)])
        for b in range(4):
            mm(bank(b, 128), "eq", "es", 128 * b, "hq", "hs", x0 + (80 if first else 48), 128)
        for b in range(4):
            mm(bank(4 + b, 128), "eq", "es", 128 * b, "lq", "ls", x0 + 8, 128)
        added(0 if first else S, 0, 8 if first else 0, 3 * S)
        added(place(d, late), 4, 0, S)
        for b in range(4):
            (cp if b % 2 else act)(v("tt", b, 640, 4), v("gt", C * b, C * b + C, ind=iof))
        qz("tq", "tsc", C * (t + 1), C, v("tt", 0, 640))

    o = C * R
    mm(bank(5), "vq", "vs", 0, "tq", "tsc", o)
    dma("s", T.oc[:], T.tq[:, o:o + C].bitcast(dt.uint8), [], [v("tq", o, o + C)])
    for k in range(4):
        dma("a", T.osc[4 * k:4 * k + 4, :], T.tsc[32 * k:32 * k + 4, o:o + C], [], [v("tsc", o, o + C)])
    cp(v("yo", 0, C), bank(5))
    dma("s", T.y[:], T.yo[:], [], [v("yo", 0, C)])

    queue = {"v": g.vector, "a": g.scalar, "p": g.tensor, "s": g.sync, "g": g}
    counter = {"v": "sv", "a": "sa", "p": "sp", "g": "sg"}
    known = {q: {} for q in queue}
    for i, o_ in enumerate(ops):
        o_["src"] = o_["arr"][0] if "arr" in o_ else o_.get("dma", o_["eng"])
        if o_["eng"] is None:
            o_["after"] = {}
            continue
        need = {}
        for j in range(i):
            e_ = ops[j]
            if e_.get("remote") or (o_.get("chain") and e_["eng"] == "p"):
                continue
            if (any(_meet(a, b_) for a in o_["rd"] + o_["wr"] for b_ in e_["wr"]) or any(_meet(a, b_) for a in o_["wr"] for b_ in e_["rd"])
                    or (e_["eng"] != o_["eng"] and any(a[0] == "ps" and _meet(a, b_) for a in o_["rd"] for b_ in e_["rd"]))):
                need[e_["src"]] = j
        kn = known[o_["eng"]]
        o_["waits"] = []
        for src, j in sorted(need.items(), key=lambda x: -x[1]):
            if kn.get(src, -1) < j:
                o_["waits"].append(j)
                ops[j]["told"] = True
                kn[src] = j
                for s2, j2 in ops[j]["after"].items():
                    kn[s2] = max(kn.get(s2, -1), j2)
        o_["after"] = dict(kn)
    count = {q: 0 for q in counter}
    for o_ in ops:
        if o_["eng"] is None:
            o_["sig"] = o_["arr"]
            continue
        q = queue[o_["eng"]]
        for j in o_["waits"]:
            q.wait_ge(T.sem[ops[j]["sig"][0]], ops[j]["sig"][1])
        ins = o_["fn"](q)
        if "dma" in o_:
            ins.then_inc(T.sem[o_["dma"]], 16)
            o_["sig"] = (o_["dma"], 16)
        elif o_.get("told"):
            count[o_["eng"]] += 1
            ins.then_inc(T.sem[counter[o_["eng"]]], 1)
            o_["sig"] = (counter[o_["eng"]], count[o_["eng"]])
    g.wait_ge(T.sem.sent, sent[0])
    for o_ in ops:
        if "dma" in o_ and not o_.get("told"):
            queue[o_["eng"]].wait_ge(T.sem[o_["dma"]], 16)
